import numpy as np
import ml_dtypes


def mxq(x, axis, fmt="e4m3"):
    dtype, down = {"e4m3": (ml_dtypes.float8_e4m3fn, 7), "e5m2": (ml_dtypes.float8_e5m2, 14)}[fmt]
    v = np.moveaxis(np.asarray(x, np.float32).astype(ml_dtypes.bfloat16).astype(np.float64), axis, -1)
    blocks = v.reshape(v.shape[:-1] + (-1, 32))
    amax = np.abs(blocks).max(-1, keepdims=True)
    byte = np.maximum(np.where(amax > 0, np.frexp(amax)[1] - 1 + 127, 0) - down, 1)
    scale = np.exp2(byte - 127.0)
    codes = (blocks / scale).astype(np.float32).astype(dtype).astype(np.float64)
    return np.moveaxis((codes * scale).reshape(v.shape), -1, axis)


WIDE = False


def mx_kscale(k):
    if not WIDE:
        return np.ones(k)
    levels = np.array([10, -10, 5, -5, 0])
    if k % 512:
        return np.exp2(np.random.permutation(np.resize(levels, k // 32))).repeat(32)
    a = np.empty((k // 512, 16))
    for p in range(k // 512):
        a[p, :8] = np.random.permutation(np.resize(levels, 8))
        for g in range(8):
            far = levels[np.abs(levels - a[p, g]) >= 10]
            a[p, g + 8] = far[np.random.randint(len(far))]
    return np.exp2(a.ravel()).repeat(32)


def f64(x):
    return np.asarray(x).astype(np.float64)


def striped(idx):
    return np.tile(np.asarray(idx).reshape(-1, 16).T, (8, 1)).astype(np.uint16)


def unstriped(offs):
    return offs[:16].T.reshape(-1).astype(np.int64)


E2M1 = np.array([0.0, 0.5, 1.0, 1.5, 2.0, 3.0, 4.0, 6.0, -0.0, -0.5, -1.0, -1.5, -2.0, -3.0, -4.0, -6.0])


def pack_weight(w, fmt):
    k, n = w.shape
    w = f64(np.asarray(w, np.float32).astype(ml_dtypes.bfloat16)).reshape(k // 32, 32, n)
    amax = np.abs(w).max(1)
    if fmt == "e4m3":
        byte = np.frexp(amax)[1] - 1 + 127 - 7
    else:
        mant, ex = np.frexp(amax / 6.0)
        byte = np.where(mant > 0.5, ex, ex - 1) + 127
    byte = np.clip(np.where(amax > 0, byte, 1), 1, 254)
    scaled = (w * np.exp2(127.0 - byte)[:, None, :]).reshape(k, n).astype(np.float32)
    by_word = np.ascontiguousarray(scaled.reshape(k // 512, 128, 4, n).transpose(0, 1, 3, 2))
    if fmt == "e4m3":
        words = by_word.astype(ml_dtypes.float8_e4m3fn).view(np.uint8)
    else:
        c = by_word.astype(ml_dtypes.float4_e2m1fn).view(np.uint8) & 0xF
        words = (c[..., 0::2] | (c[..., 1::2] << 4)).reshape(k // 512, 128, 2 * n)
    return np.ascontiguousarray(words), np.ascontiguousarray(byte.astype(np.uint8).reshape(k // 512, 16, n))


def unpack_weight(words, scales, fmt):
    g, _, n = scales.shape
    words = np.ascontiguousarray(words).reshape(g, 128, n, -1)
    if fmt == "e4m3":
        vals = words.view(ml_dtypes.float8_e4m3fn).astype(np.float64)
    else:
        nib = np.empty((g, 128, n, 4), np.uint8)
        nib[..., 0::2] = words & 0xF
        nib[..., 1::2] = words >> 4
        vals = E2M1[nib]
    vals = vals * np.repeat(np.exp2(scales.astype(np.float64) - 127.0), 8, axis=1)[..., None]
    return vals.transpose(0, 1, 3, 2).reshape(g * 512, n)


def gelu(v):
    return 0.5 * v * (1.0 + np.tanh(0.7978845608028654 * (v + 0.044715 * v ** 3)))


B, N, T, D, NQ = 1, 512, 2048, 512, 512
DV = 512


def sgn(shape):
    return np.random.uniform(0.5, 2.0, shape) * np.where(np.random.standard_normal(shape) < 0, -1.0, 1.0)


def setup_inputs():
    n = np.random.standard_normal
    idx = np.random.permutation(T)[:B * N]
    s = mx_kscale(D)[:, None]
    u = mx_kscale(N)
    ut = np.ones(T)
    ut[idx] = u
    kp = pack_weight(n((D, T)) / s, "e4m3")
    return {
        "qT": (n((B, D, NQ)) * s * (1.00 / np.sqrt(D))).astype(np.float32),
        "k_words": kp[0],
        "k_scales": kp[1],
        "vT": (n((DV, T)) / ut).astype(np.float32),
        "nb": np.tile(0.5 * n(2048), (128, 1)).astype(np.float32),
        "rs": (n((B, NQ, DV))).astype(np.float32),
        "us": (sgn((B, N, 1)) * u[:, None]).astype(np.float32),
        "offs": striped(idx),
    }


def reference(qT, k_words, k_scales, vT, nb, rs, us, offs):
    idx = unstriped(offs)
    pick = lambda x, which: x[:, which].reshape(x.shape[0], B, -1).transpose(1, 0, 2)
    k = unpack_weight(k_words, k_scales, "e4m3")
    kg = pick(k, idx)
    qq = mxq(f64(qT), 1, "e4m3")
    a = kg.transpose(0, 2, 1) @ qq
    y = gelu(a + pick(f64(nb), idx)[:, :1, :].transpose(0, 2, 1)) * f64(us)
    wq = mxq(y, 1, "e4m3")
    o = wq.transpose(0, 2, 1) @ mxq(pick(f64(vT), idx).transpose(0, 2, 1), 1, "e4m3")
    r_ = o + f64(rs)
    return r_

@@ -1,0 +1,187 @@
+from contextlib import ExitStack
+
+import concourse.mybir as mybir
+from concourse.masks import make_identity
+
+N, T, D, NQ, DV = 512, 2048, 512, 512, 512
+FLOPS = 2 * N * NQ * (D + DV)
+BYTES = 4 * (D * NQ + DV * T + T + 2 * NQ * DV + N) + D * T + 16 * T + 128 * 32 * 2
+
+F32 = mybir.dt.float32
+BF16 = mybir.dt.bfloat16
+I32 = mybir.dt.int32
+U32 = mybir.dt.uint32
+U16 = mybir.dt.uint16
+U8 = mybir.dt.uint8
+FP8X4 = mybir.dt.float8_e4m3fn_x4
+ACT = mybir.ActivationFunctionType
+ALU = mybir.AluOpType
+
+P = 128
+PACK = 4
+NB_ROW = 0
+HALF = NQ // 2
+
+
+def packed(tile, h):
+    return tile[:, h * HALF:(h + 1) * HALF, :].rearrange("p (c i) t -> p c t i", i=4)
+
+
+def planes(tile, h):
+    return tile[:, :, h * HALF:(h + 1) * HALF].rearrange("p t (c i) -> p c t i", i=4)
+
+
+def tile_attend_mlpb_gelu_topk_kernel(tc, qT, k_words, k_scales, vT, nb, rs, us, offs, out):
+    nc = tc.nc
+    with ExitStack() as ctx:
+        keep = ctx.enter_context(tc.tile_pool(name="keep", bufs=1))
+        acc_pool = ctx.enter_context(tc.psum_pool(name="acc", bufs=4))
+        turn_pool = ctx.enter_context(tc.psum_pool(name="turn", bufs=3))
+
+        offsets = keep.tile([P, N // 16], U16, name="offsets")
+        nc.sync.dma_start(offsets[:], offs)
+
+        ks_pool = keep.tile([P, T], U8, name="ks_pool", align_bytes=64)
+        nb_pool = keep.tile([P, T], F32, name="nb_pool")
+        nb_row = keep.tile([1, T], F32, name="nb_row")
+        nc.scalar.dma_start(nb_row[:], nb[0:1, :])
+        nc.gpsimd.memset(ks_pool[:].bitcast(I32), 0)
+        nc.vector.memset(nb_pool[:], 0.0)
+
+        q_raw = keep.tile([P, PACK, NQ], F32, name="q_raw")
+        nc.sync.dma_start(q_raw[:], qT[0].rearrange("(p j) w -> p j w", j=PACK))
+        kw_pool = keep.tile([P, T], I32, name="kw_pool")
+        nc.sync.dma_start(kw_pool[:], k_words[0].rearrange("p n t -> p (n t)").bitcast(I32))
+        v_pool = [keep.tile([P, T], F32, name="v_pool%d" % b) for b in range(4)]
+        for b in range(4):
+            nc.sync.dma_start(v_pool[b][:], vT[b * P:(b + 1) * P, :])
+        rs_rows = rs[0].rearrange("(b p) e -> p b e", p=P)
+        out_rows = out[0].rearrange("(b p) e -> p b e", p=P)
+        rs_sb = [keep.tile([P, 4, 2 * P], F32, name="rs_sb%d" % h) for h in range(2)]
+        for h in range(2):
+            nc.sync.dma_start(rs_sb[h][:], rs_rows[:, :, h * 2 * P:(h + 1) * 2 * P])
+
+        us_sb = keep.tile([P, 1, PACK, 1], F32, name="us_sb")
+        nc.scalar.dma_start(us_sb[:, 0, :, 0], us[0].rearrange("(p t) o -> p (t o)", t=PACK))
+        scale_rows = k_scales[0].rearrange("(g r) n -> r g n", r=4)
+        for r in range(4):
+            nc.scalar.dma_start(ks_pool[r:P:32, :].bitcast(I32), scale_rows[r].bitcast(I32))
+
+        ident = keep.tile([P, P], F32, name="ident")
+        make_identity(nc, ident[:])
+        warm = keep.tile([P, 1], F32, name="warm")
+        nc.scalar.activation(warm[:], ident[:, 0:1], ACT.Gelu_apprx_tanh)
+
+        nc.scalar.activation(nb_pool[0:1, T // 2:], nb_row[:, T // 2:], ACT.Copy)
+        nc.vector.tensor_copy(nb_pool[0:1, :T // 2], nb_row[:, :T // 2])
+        nb_list = keep.tile([P, N], F32, name="nb_list")
+        nc.vector.tensor_copy(nb_list[:], nb_pool[:].indirect(offsets[:]))
+        nb_turn = turn_pool.tile([P, PACK, P], F32, name="turn")
+        for t in range(PACK):
+            nc.tensor.transpose(nb_turn[:, t, :], nb_list[:, t:N:PACK], ident[:])
+        bias = keep.tile([P, PACK], F32, name="bias")
+        nc.scalar.copy(bias[:], nb_turn[:, :, NB_ROW])
+
+        ks_list = keep.tile([P, N], U8, name="ks_list", align_bytes=64)
+        nc.vector.tensor_copy(ks_list[:], ks_pool[:].indirect(offsets[:]))
+        ks_g = keep.tile([P, PACK, P], U8, name="ks_g", align_bytes=64)
+        nc.vector.tensor_copy(ks_g[:], ks_list[:].rearrange("p (m t) -> p t m", t=PACK))
+
+        q_bf = keep.tile([P, NQ, PACK], BF16, name="q_bf", align_bytes=64)
+        q_codes = keep.tile([P, NQ], U32, name="q_codes", align_bytes=64)
+        q_scales = keep.tile([P, NQ], U8, name="q_scales", align_bytes=64)
+        nc.vector.tensor_copy(packed(q_bf, 0), planes(q_raw, 0))
+        nc.scalar.copy(packed(q_bf, 1), planes(q_raw, 1))
+        for h in range(2):
+            cols = slice(h * HALF, (h + 1) * HALF)
+            nc.vector.quantize_mx(out=q_codes[:, cols].bitcast(FP8X4), scales=q_scales[:, cols],
+                                  in_=q_bf[:, cols, :].rearrange("p w j -> p (w j)"))
+
+        kw_g = keep.tile([P, PACK, P], U32, name="kw_g", align_bytes=64)
+        nc.vector.tensor_copy(kw_g[:].rearrange("p t m -> p m t"), kw_pool[:].bitcast(U32).indirect(offsets[:]))
+
+        g = keep.tile([P, PACK, NQ], F32, name="g")
+        first = []
+        for t in range(PACK):
+            a = acc_pool.tile([P, NQ], F32, name="acc")
+            nc.tensor.matmul_mx(out=a[:], lhsT=kw_g[:, t, :].bitcast(FP8X4), lhsT_scale=ks_g[:, t, :],
+                                rhs=q_codes[:].bitcast(FP8X4), rhs_scale=q_scales[:], start=True, stop=True)
+            first.append(a)
+        for h in range(2):
+            cols = slice(h * HALF, (h + 1) * HALF)
+            for t in range(PACK):
+                nc.scalar.activation(g[:, t, cols], first[t][:, cols], ACT.Gelu_apprx_tanh, bias=bias[:, t:t + 1])
+
+        v_codes = keep.tile([P, DV], U32, name="v_codes", align_bytes=64)
+        v_scales = keep.tile([P, DV], U8, name="v_scales", align_bytes=64)
+
+        def gather_v(b):
+            v_g = keep.tile([P, 2, P, 2], BF16, name="v_g%d" % b)
+            nc.vector.tensor_copy(v_g[:].rearrange("p u m e -> p m u e"), v_pool[b][:].indirect(offsets[:]))
+            words = v_g[:].rearrange("p u m e -> p (u m e)").bitcast(F32)
+            turn = turn_pool.tile([P, PACK, P], F32, name="turn")
+            for u in range(2):
+                nc.tensor.transpose(turn[:, u, :], words[:, u * P:(u + 1) * P], ident[:])
+            v_bf = keep.tile([P, P * PACK], BF16, name="v_bf%d" % b, align_bytes=64)
+            nc.scalar.copy(v_bf[:].bitcast(F32).rearrange("p (r u) -> p r u", u=2),
+                           turn[:, 0:2, :].rearrange("p u r -> p r u"))
+            return v_bf
+
+        def quantize_v(b, v_bf):
+            cols = slice(b * P, (b + 1) * P)
+            nc.vector.quantize_mx(out=v_codes[:, cols].bitcast(FP8X4), scales=v_scales[:, cols], in_=v_bf[:])
+
+        y_bf = keep.tile([P, NQ, PACK], BF16, name="y_bf", align_bytes=64)
+        y_codes = keep.tile([P, NQ], U32, name="y_codes", align_bytes=64)
+        y_scales = keep.tile([P, NQ], U8, name="y_scales", align_bytes=64)
+        y_planes = keep.tile([P, PACK, NQ], BF16, name="y_planes")
+
+        def scale_y(h):
+            if h == 0:
+                nc.vector.tensor_tensor(packed(y_bf, 0), planes(g, 0), us_sb[:].to_broadcast([P, HALF // 4, PACK, 4]), ALU.mult)
+            else:
+                for t in range(PACK):
+                    nc.scalar.activation(y_planes[:, t, HALF:], g[:, t, HALF:], ACT.Copy, scale=us_sb[:, 0, t, :])
+                nc.vector.tensor_copy(packed(y_bf, 1), planes(y_planes, 1))
+
+        def quantize_y(h):
+            cols = slice(h * HALF, (h + 1) * HALF)
+            nc.vector.quantize_mx(out=y_codes[:, cols].bitcast(FP8X4), scales=y_scales[:, cols],
+                                  in_=y_bf[:, cols, :].rearrange("p w j -> p (w j)"))
+
+        res = [keep.tile([P, 4, 2 * P], F32, name="res%d" % h) for h in range(2)]
+
+        def second(b):
+            cols = slice(b * P, (b + 1) * P)
+            o = acc_pool.tile([P, 4, P], F32, name="acc")
+            for c in range(4):
+                rows = slice(c * P, (c + 1) * P)
+                nc.tensor.matmul_mx(out=o[:, c, :], lhsT=y_codes[:, rows].bitcast(FP8X4), lhsT_scale=y_scales[:, rows],
+                                    rhs=v_codes[:, cols].bitcast(FP8X4), rhs_scale=v_scales[:, cols], start=True, stop=True)
+            return o
+
+        def finish(b, o):
+            part = slice((b % 2) * P, (b % 2 + 1) * P)
+            nc.vector.tensor_tensor(res[b // 2][:, :, part], o[:], rs_sb[b // 2][:, :, part], ALU.add)
+
+        v0 = gather_v(0)
+        scale_y(0)
+        quantize_v(0, v0)
+        v1 = gather_v(1)
+        quantize_y(0)
+        v2 = gather_v(2)
+        quantize_v(1, v1)
+        scale_y(1)
+        quantize_y(1)
+        quantize_v(2, v2)
+        outs = [second(b) for b in range(3)]
+        v3 = gather_v(3)
+        finish(0, outs[0])
+        finish(1, outs[1])
+        nc.sync.dma_start(out_rows[:, :, 0:2 * P], res[0][:])
+        quantize_v(3, v3)
+        o3 = second(3)
+        finish(2, outs[2])
+        nc.sync.dma_start(out_rows[:, :, 2 * P:3 * P], res[1][:, :, 0:P])
+        finish(3, o3)
+        nc.sync.dma_start(out_rows[:, :, 3 * P:4 * P], res[1][:, :, P:2 * P])

@@ -19,7 +19,7 @@ ALU = mybir.AluOpType
 
 P = 128
 PACK = 4
-NB_ROW = 0
+NB_ROW = 8
 HALF = NQ // 2
 
 
@@ -35,72 +35,90 @@ def tile_attend_mlpb_gelu_topk_kernel(tc, qT, k_words, k_scales, vT, nb, rs, us,
     nc = tc.nc
     with ExitStack() as ctx:
         keep = ctx.enter_context(tc.tile_pool(name="keep", bufs=1))
+        early = ctx.enter_context(tc.tile_pool(name="early", bufs=1))
         acc_pool = ctx.enter_context(tc.psum_pool(name="acc", bufs=4))
         turn_pool = ctx.enter_context(tc.psum_pool(name="turn", bufs=3))
 
         offsets = keep.tile([P, N // 16], U16, name="offsets")
         nc.sync.dma_start(offsets[:], offs)
 
-        ks_pool = keep.tile([P, T], U8, name="ks_pool", align_bytes=64)
-        nb_pool = keep.tile([P, T], F32, name="nb_pool")
-        nb_row = keep.tile([1, T], F32, name="nb_row")
-        nc.scalar.dma_start(nb_row[:], nb[0:1, :])
-        nc.gpsimd.memset(ks_pool[:].bitcast(I32), 0)
-        nc.vector.memset(nb_pool[:], 0.0)
+        def big(shape, dtype, name, slot):
+            return keep.tile(shape, dtype, name=name, tag=slot, align_bytes=64)
 
-        q_raw = keep.tile([P, PACK, NQ], F32, name="q_raw")
+        def over_nb(shape, dtype, name, offset):
+            return early.tile(shape, dtype, name=name, offset=offset, align_bytes=64)
+
+        q_raw = big([P, PACK, NQ], F32, "q_raw", "slot_c")
         nc.sync.dma_start(q_raw[:], qT[0].rearrange("(p j) w -> p j w", j=PACK))
-        kw_pool = keep.tile([P, T], I32, name="kw_pool")
+        kw_pool = big([P, T], I32, "kw_pool", "slot_d")
         nc.sync.dma_start(kw_pool[:], k_words[0].rearrange("p n t -> p (n t)").bitcast(I32))
-        v_pool = [keep.tile([P, T], F32, name="v_pool%d" % b) for b in range(4)]
-        for b in range(4):
-            nc.sync.dma_start(v_pool[b][:], vT[b * P:(b + 1) * P, :])
-        rs_rows = rs[0].rearrange("(b p) e -> p b e", p=P)
-        out_rows = out[0].rearrange("(b p) e -> p b e", p=P)
-        rs_sb = [keep.tile([P, 4, 2 * P], F32, name="rs_sb%d" % h) for h in range(2)]
-        for h in range(2):
-            nc.sync.dma_start(rs_sb[h][:], rs_rows[:, :, h * 2 * P:(h + 1) * 2 * P])
 
-        us_sb = keep.tile([P, 1, PACK, 1], F32, name="us_sb")
-        nc.scalar.dma_start(us_sb[:, 0, :, 0], us[0].rearrange("(p t) o -> p (t o)", t=PACK))
+        ks_pool = big([P, T], U8, "ks_pool", "ks_pool")
+        nc.gpsimd.memset(ks_pool[:].bitcast(I32), 0)
         scale_rows = k_scales[0].rearrange("(g r) n -> r g n", r=4)
         for r in range(4):
             nc.scalar.dma_start(ks_pool[r:P:32, :].bitcast(I32), scale_rows[r].bitcast(I32))
-
         ident = keep.tile([P, P], F32, name="ident")
         make_identity(nc, ident[:])
+        us_sb = keep.tile([P, 1, PACK, 1], F32, name="us_sb")
+        nc.gpsimd.dma_start(us_sb[:, 0, :, 0], us[0].rearrange("(p t) o -> p (t o)", t=PACK))
+        nb_pool = over_nb([P, T], F32, "nb_pool", 0)
+        nc.vector.memset(nb_pool[:], 0.0)
+        nc.scalar.dma_start(nb_pool[NB_ROW:NB_ROW + 1, :], nb[0:1, :])
         warm = keep.tile([P, 1], F32, name="warm")
         nc.scalar.activation(warm[:], ident[:, 0:1], ACT.Gelu_apprx_tanh)
 
-        nc.scalar.activation(nb_pool[0:1, T // 2:], nb_row[:, T // 2:], ACT.Copy)
-        nc.vector.tensor_copy(nb_pool[0:1, :T // 2], nb_row[:, :T // 2])
-        nb_list = keep.tile([P, N], F32, name="nb_list")
+        v_pool = []
+
+        def load_v(b, slot):
+            if slot is None:
+                v_pool.append(over_nb([P, T], F32, "v_pool%d" % b, 7168))
+            else:
+                v_pool.append(big([P, T], F32, "v_pool%d" % b, slot))
+            nc.sync.dma_start(v_pool[b][:], vT[b * P:(b + 1) * P, :])
+
+        rs_rows = rs[0].rearrange("(b p) e -> p b e", p=P)
+        out_rows = out[0].rearrange("(b p) e -> p b e", p=P)
+        rs_sb = []
+
+        def load_rs(h, slot):
+            if slot is None:
+                rs_sb.append(over_nb([P, 4, 2 * P], F32, "rs_sb%d" % h, 7168))
+            else:
+                rs_sb.append(big([P, 4, 2 * P], F32, "rs_sb%d" % h, slot))
+            nc.sync.dma_start(rs_sb[h][:], rs_rows[:, :, h * 2 * P:(h + 1) * 2 * P])
+
+        load_v(0, "slot_a")
+        ks_list = keep.tile([P, N], U8, name="ks_list", align_bytes=64)
+        nc.vector.tensor_copy(ks_list[:], ks_pool[:].indirect(offsets[:]))
+        ks_g = keep.tile([P, PACK, P], U8, name="ks_g", align_bytes=64)
+        nc.vector.tensor_copy(ks_g[:], ks_list[:].rearrange("p (m t) -> p t m", t=PACK))
+
+        nb_list = big([P, N], F32, "nb_list", "nb_list")
         nc.vector.tensor_copy(nb_list[:], nb_pool[:].indirect(offsets[:]))
+        load_v(1, None)
+        q_bf = [big([P, HALF, PACK], BF16, "q_bf0", "q_bf0"), big([P, HALF, PACK], BF16, "q_bf1", "q_bf1")]
+        q_codes = over_nb([P, NQ], U32, "q_codes", 2048)
+        q_scales = keep.tile([P, NQ], U8, name="q_scales", align_bytes=64)
+        nc.scalar.copy(packed(q_bf[0], 0), planes(q_raw, 0))
+        nc.scalar.copy(packed(q_bf[1], 0), planes(q_raw, 1))
+        load_v(2, "slot_c")
         nb_turn = turn_pool.tile([P, PACK, P], F32, name="turn")
         for t in range(PACK):
             nc.tensor.transpose(nb_turn[:, t, :], nb_list[:, t:N:PACK], ident[:])
         bias = keep.tile([P, PACK], F32, name="bias")
         nc.scalar.copy(bias[:], nb_turn[:, :, NB_ROW])
 
-        ks_list = keep.tile([P, N], U8, name="ks_list", align_bytes=64)
-        nc.vector.tensor_copy(ks_list[:], ks_pool[:].indirect(offsets[:]))
-        ks_g = keep.tile([P, PACK, P], U8, name="ks_g", align_bytes=64)
-        nc.vector.tensor_copy(ks_g[:], ks_list[:].rearrange("p (m t) -> p t m", t=PACK))
-
-        q_bf = keep.tile([P, NQ, PACK], BF16, name="q_bf", align_bytes=64)
-        q_codes = keep.tile([P, NQ], U32, name="q_codes", align_bytes=64)
-        q_scales = keep.tile([P, NQ], U8, name="q_scales", align_bytes=64)
-        nc.vector.tensor_copy(packed(q_bf, 0), planes(q_raw, 0))
-        nc.scalar.copy(packed(q_bf, 1), planes(q_raw, 1))
         for h in range(2):
             cols = slice(h * HALF, (h + 1) * HALF)
             nc.vector.quantize_mx(out=q_codes[:, cols].bitcast(FP8X4), scales=q_scales[:, cols],
-                                  in_=q_bf[:, cols, :].rearrange("p w j -> p (w j)"))
+                                  in_=q_bf[h][:].rearrange("p w j -> p (w j)"))
 
-        kw_g = keep.tile([P, PACK, P], U32, name="kw_g", align_bytes=64)
+        kw_g = over_nb([P, PACK, P], U32, "kw_g", 4096)
         nc.vector.tensor_copy(kw_g[:].rearrange("p t m -> p m t"), kw_pool[:].bitcast(U32).indirect(offsets[:]))
+        load_v(3, "slot_d")
 
-        g = keep.tile([P, PACK, NQ], F32, name="g")
+        g = big([P, PACK, NQ], F32, "g", "slot_g")
         first = []
         for t in range(PACK):
             a = acc_pool.tile([P, NQ], F32, name="acc")
@@ -116,13 +134,16 @@ def tile_attend_mlpb_gelu_topk_kernel(tc, qT, k_words, k_scales, vT, nb, rs, us,
         v_scales = keep.tile([P, DV], U8, name="v_scales", align_bytes=64)
 
         def gather_v(b):
-            v_g = keep.tile([P, 2, P, 2], BF16, name="v_g%d" % b)
+            if b == 0:
+                v_g = over_nb([P, 2, P, 2], BF16, "v_g0", 6144)
+            else:
+                v_g = big([P, 2, P, 2], BF16, "v_g%d" % b, "v_g%d" % b)
             nc.vector.tensor_copy(v_g[:].rearrange("p u m e -> p m u e"), v_pool[b][:].indirect(offsets[:]))
             words = v_g[:].rearrange("p u m e -> p (u m e)").bitcast(F32)
             turn = turn_pool.tile([P, PACK, P], F32, name="turn")
             for u in range(2):
                 nc.tensor.transpose(turn[:, u, :], words[:, u * P:(u + 1) * P], ident[:])
-            v_bf = keep.tile([P, P * PACK], BF16, name="v_bf%d" % b, align_bytes=64)
+            v_bf = big([P, P * PACK], BF16, "v_bf%d" % b, "v_bf%d" % b)
             nc.scalar.copy(v_bf[:].bitcast(F32).rearrange("p (r u) -> p r u", u=2),
                            turn[:, 0:2, :].rearrange("p u r -> p r u"))
             return v_bf
@@ -149,8 +170,6 @@ def tile_attend_mlpb_gelu_topk_kernel(tc, qT, k_words, k_scales, vT, nb, rs, us,
             nc.vector.quantize_mx(out=y_codes[:, cols].bitcast(FP8X4), scales=y_scales[:, cols],
                                   in_=y_bf[:, cols, :].rearrange("p w j -> p (w j)"))
 
-        res = [keep.tile([P, 4, 2 * P], F32, name="res%d" % h) for h in range(2)]
-
         def second(b):
             cols = slice(b * P, (b + 1) * P)
             o = acc_pool.tile([P, 4, P], F32, name="acc")
@@ -160,28 +179,35 @@ def tile_attend_mlpb_gelu_topk_kernel(tc, qT, k_words, k_scales, vT, nb, rs, us,
                                     rhs=v_codes[:, cols].bitcast(FP8X4), rhs_scale=v_scales[:, cols], start=True, stop=True)
             return o
 
-        def finish(b, o):
+        def finish(b, o, res):
             part = slice((b % 2) * P, (b % 2 + 1) * P)
-            nc.vector.tensor_tensor(res[b // 2][:, :, part], o[:], rs_sb[b // 2][:, :, part], ALU.add)
+            nc.vector.tensor_tensor(res, o[:], rs_sb[b // 2][:, :, part], ALU.add)
 
         v0 = gather_v(0)
+        load_rs(0, "slot_a")
         scale_y(0)
-        quantize_v(0, v0)
         v1 = gather_v(1)
+        load_rs(1, None)
         quantize_y(0)
-        v2 = gather_v(2)
-        quantize_v(1, v1)
+        quantize_v(0, v0)
         scale_y(1)
+        v2 = gather_v(2)
         quantize_y(1)
-        quantize_v(2, v2)
-        outs = [second(b) for b in range(3)]
+        quantize_v(1, v1)
+        o0 = second(0)
+        o1 = second(1)
         v3 = gather_v(3)
-        finish(0, outs[0])
-        finish(1, outs[1])
-        nc.sync.dma_start(out_rows[:, :, 0:2 * P], res[0][:])
+        quantize_v(2, v2)
+        o2 = second(2)
+        res01 = big([P, 4, 2 * P], F32, "res01", "slot_d")
+        finish(0, o0, res01[:, :, 0:P])
+        finish(1, o1, res01[:, :, P:2 * P])
+        nc.sync.dma_start(out_rows[:, :, 0:2 * P], res01[:])
         quantize_v(3, v3)
         o3 = second(3)
-        finish(2, outs[2])
-        nc.sync.dma_start(out_rows[:, :, 2 * P:3 * P], res[1][:, :, 0:P])
-        finish(3, o3)
-        nc.sync.dma_start(out_rows[:, :, 3 * P:4 * P], res[1][:, :, P:2 * P])
+        res2 = big([P, 4, P], F32, "res2", "v_bf3")
+        finish(2, o2, res2[:])
+        nc.sync.dma_start(out_rows[:, :, 2 * P:3 * P], res2[:])
+        res3 = big([P, 4, P], F32, "res3", "res3")
+        finish(3, o3, res3[:])
+        nc.sync.dma_start(out_rows[:, :, 3 * P:4 * P], res3[:])

@@ -19,178 +19,193 @@ ALU = mybir.AluOpType
 
 P = 128
 PACK = 4
-NB_ROW = 8
 HALF = NQ // 2
+NB_SPLIT = 1344
+
+PLAN = {
+    "q_bf0": 0, "q_bf1": 2048, "v_g0": 3072, "kw_pool": 4096,
+    "v_pool3": 4608, "res01": 4608, "v_codes2": 8704, "v_scales2": 9216,
+    "warm_in": 12224, "us_sb": 12800,
+    "v_pool0": 12864, "rs_sb0": 12864, "y_bf0": 16960,
+    "v_pool1": 21056, "rs_sb1": 21056, "y_bf1": 25152, "v_g3": 25152,
+    "y_codes0": 27200, "v_codes0": 28224, "y_scales0": 28736, "v_scales0": 28992,
+    "ks_pool": 28224, "v_pool2": 29248, "q_raw": 30272,
+    "y_codes1": 29248, "v_codes1": 30272, "y_scales1": 30784, "v_scales1": 31040,
+    "nb_pool": 38464, "ks_list": 38464, "q_codes0": 40512, "q_scales1": 4096,"q_codes1": 41536, "kw_g": 42560,
+    "g0": 46656, "v_g1": 46656,
+    "y_planes": 50752, "v_g2": 50752,
+    "v_bf3": 52800, "res2": 52800,
+}
+BANK = 2048
 
 
-def packed(tile, h):
-    return tile[:, h * HALF:(h + 1) * HALF, :].rearrange("p (c i) t -> p c t i", i=4)
+def packed(tile):
+    return tile.rearrange("p (c i) t -> p c t i", i=4)
 
 
-def planes(tile, h):
-    return tile[:, :, h * HALF:(h + 1) * HALF].rearrange("p t (c i) -> p c t i", i=4)
+def planes(tile):
+    return tile.rearrange("p t (c i) -> p c t i", i=4)
 
 
 def tile_attend_mlpb_gelu_topk_kernel(tc, qT, k_words, k_scales, vT, nb, rs, us, offs, out):
     nc = tc.nc
     with ExitStack() as ctx:
         keep = ctx.enter_context(tc.tile_pool(name="keep", bufs=1))
-        early = ctx.enter_context(tc.tile_pool(name="early", bufs=1))
-        acc_pool = ctx.enter_context(tc.psum_pool(name="acc", bufs=4))
-        turn_pool = ctx.enter_context(tc.psum_pool(name="turn", bufs=3))
+        shared = ctx.enter_context(tc.tile_pool(name="shared", bufs=1))
+        psum = ctx.enter_context(tc.psum_pool(name="psum", bufs=1))
+
+        def sbuf(name, shape, dtype):
+            if name in PLAN:
+                return shared.tile(shape, dtype, name=name, offset=PLAN[name], align_bytes=64)
+            return keep.tile(shape, dtype, name=name, align_bytes=64)
+
+        def bank(name, number, shape):
+            return psum.tile(shape, F32, name=name, offset=number * BANK)
+
+        def quantize(codes, scales, cols, values):
+            nc.vector.quantize_mx(out=codes[:, cols].bitcast(FP8X4), scales=scales[:, cols], in_=values)
+
+        def quantize_new(name, width, values):
+            codes = sbuf(name % "codes", [P, width], U32)
+            scales = sbuf(name % "scales", [P, width], U8)
+            quantize(codes, scales, slice(0, width), values)
+            return codes, scales
+
+        halves = [slice(h * HALF, (h + 1) * HALF) for h in range(2)]
+        blocks = [slice(b * P, (b + 1) * P) for b in range(4)]
 
         offsets = keep.tile([P, N // 16], U16, name="offsets")
         nc.sync.dma_start(offsets[:], offs)
-
-        def big(shape, dtype, name, slot):
-            return keep.tile(shape, dtype, name=name, tag=slot, align_bytes=64)
-
-        def over_nb(shape, dtype, name, offset):
-            return early.tile(shape, dtype, name=name, offset=offset, align_bytes=64)
-
-        q_raw = big([P, PACK, NQ], F32, "q_raw", "slot_c")
+        nb_row = sbuf("nb_row", [1, T], F32)
+        nc.scalar.dma_start(nb_row[:], nb[0:1, :])
+        q_raw = sbuf("q_raw", [P, PACK, NQ], F32)
         nc.sync.dma_start(q_raw[:], qT[0].rearrange("(p j) w -> p j w", j=PACK))
-        kw_pool = big([P, T], I32, "kw_pool", "slot_d")
-        nc.sync.dma_start(kw_pool[:], k_words[0].rearrange("p n t -> p (n t)").bitcast(I32))
 
-        ks_pool = big([P, T], U8, "ks_pool", "ks_pool")
+        warm_in = sbuf("warm_in", [P, 176], F32)
+        nc.gpsimd.memset(warm_in[:], 0.0)
+        warm = sbuf("warm", [P, 176], F32)
+        nc.scalar.activation(warm[:], warm_in[:], ACT.Gelu_apprx_tanh)
+        ks_pool = sbuf("ks_pool", [P, T], U8)
         nc.gpsimd.memset(ks_pool[:].bitcast(I32), 0)
-        scale_rows = k_scales[0].rearrange("(g r) n -> r g n", r=4)
-        for r in range(4):
-            nc.scalar.dma_start(ks_pool[r:P:32, :].bitcast(I32), scale_rows[r].bitcast(I32))
-        ident = keep.tile([P, P], F32, name="ident")
+        for quad in range(4):
+            nc.sync.dma_start(ks_pool[32 * quad:32 * quad + 4, :].bitcast(I32),
+                              k_scales[0, 4 * quad:4 * quad + 4, :].bitcast(I32))
+        ident = sbuf("ident", [P, P], F32)
         make_identity(nc, ident[:])
-        us_sb = keep.tile([P, 1, PACK, 1], F32, name="us_sb")
-        nc.gpsimd.dma_start(us_sb[:, 0, :, 0], us[0].rearrange("(p t) o -> p (t o)", t=PACK))
-        nb_pool = over_nb([P, T], F32, "nb_pool", 0)
-        nc.vector.memset(nb_pool[:], 0.0)
-        nc.scalar.dma_start(nb_pool[NB_ROW:NB_ROW + 1, :], nb[0:1, :])
-        warm = keep.tile([P, 1], F32, name="warm")
-        nc.scalar.activation(warm[:], ident[:, 0:1], ACT.Gelu_apprx_tanh)
+        kw_pool = sbuf("kw_pool", [P, T], I32)
+        nc.sync.dma_start(kw_pool[:], k_words[0].rearrange("p n t -> p (n t)").bitcast(I32))
+        us_sb = sbuf("us_sb", [P, 1, PACK, 1], F32)
+        nc.sync.dma_start(us_sb[:, 0, :, 0], us[0].rearrange("(p t) o -> p (t o)", t=PACK))
 
         v_pool = []
 
-        def load_v(b, slot):
-            if slot is None:
-                v_pool.append(over_nb([P, T], F32, "v_pool%d" % b, 7168))
-            else:
-                v_pool.append(big([P, T], F32, "v_pool%d" % b, slot))
-            nc.sync.dma_start(v_pool[b][:], vT[b * P:(b + 1) * P, :])
+        def load_v(b):
+            v_pool.append(sbuf("v_pool%d" % b, [P, T], F32))
+            nc.sync.dma_start(v_pool[b][:], vT[blocks[b], :])
 
-        rs_rows = rs[0].rearrange("(b p) e -> p b e", p=P)
-        out_rows = out[0].rearrange("(b p) e -> p b e", p=P)
+        rs_rows = rs[0].rearrange("(c p) e -> p c e", p=P)
+        out_rows = out[0].rearrange("(c p) e -> p c e", p=P)
         rs_sb = []
 
-        def load_rs(h, slot):
-            if slot is None:
-                rs_sb.append(over_nb([P, 4, 2 * P], F32, "rs_sb%d" % h, 7168))
-            else:
-                rs_sb.append(big([P, 4, 2 * P], F32, "rs_sb%d" % h, slot))
-            nc.sync.dma_start(rs_sb[h][:], rs_rows[:, :, h * 2 * P:(h + 1) * 2 * P])
+        def load_rs(h):
+            rs_sb.append(sbuf("rs_sb%d" % h, [P, 4, HALF], F32))
+            nc.sync.dma_start(rs_sb[h][:], rs_rows[:, :, halves[h]])
 
-        load_v(0, "slot_a")
-        ks_list = keep.tile([P, N], U8, name="ks_list", align_bytes=64)
-        nc.vector.tensor_copy(ks_list[:], ks_pool[:].indirect(offsets[:]))
-        ks_g = keep.tile([P, PACK, P], U8, name="ks_g", align_bytes=64)
-        nc.vector.tensor_copy(ks_g[:], ks_list[:].rearrange("p (m t) -> p t m", t=PACK))
+        load_v(0)
 
-        nb_list = big([P, N], F32, "nb_list", "nb_list")
+        nb_pool = sbuf("nb_pool", [P, T], F32)
+        nc.vector.memset(nb_pool[:], 0.0)
+        nc.vector.tensor_copy(nb_pool[0:1, :NB_SPLIT], nb_row[:, :NB_SPLIT])
+        nc.scalar.activation(nb_pool[0:1, NB_SPLIT:], nb_row[:, NB_SPLIT:], ACT.Copy)
+        nb_list = sbuf("nb_list", [P, N], F32)
         nc.vector.tensor_copy(nb_list[:], nb_pool[:].indirect(offsets[:]))
-        load_v(1, None)
-        q_bf = [big([P, HALF, PACK], BF16, "q_bf0", "q_bf0"), big([P, HALF, PACK], BF16, "q_bf1", "q_bf1")]
-        q_codes = over_nb([P, NQ], U32, "q_codes", 2048)
-        q_scales = keep.tile([P, NQ], U8, name="q_scales", align_bytes=64)
-        nc.scalar.copy(packed(q_bf[0], 0), planes(q_raw, 0))
-        nc.scalar.copy(packed(q_bf[1], 0), planes(q_raw, 1))
-        load_v(2, "slot_c")
-        nb_turn = turn_pool.tile([P, PACK, P], F32, name="turn")
+
+        ks_list = sbuf("ks_list", [P, N], U8)
+        nc.vector.tensor_copy(ks_list[:], ks_pool[:].indirect(offsets[:]))
+        ks_g = sbuf("ks_g", [P, PACK, P], U8)
+        nc.vector.tensor_copy(ks_g[:], ks_list[:].rearrange("p (m t) -> p t m", t=PACK))
+        load_v(1)
+
+        q_bf = [sbuf("q_bf%d" % h, [P, HALF, PACK], BF16) for h in range(2)]
+        for h in range(2):
+            nc.scalar.copy(packed(q_bf[h][:]), planes(q_raw[:, :, halves[h]]))
+        load_v(2)
+
+        nb_turn = bank("nb_turn", 4, [P, PACK, P])
         for t in range(PACK):
             nc.tensor.transpose(nb_turn[:, t, :], nb_list[:, t:N:PACK], ident[:])
-        bias = keep.tile([P, PACK], F32, name="bias")
-        nc.scalar.copy(bias[:], nb_turn[:, :, NB_ROW])
+        bias = sbuf("bias", [P, PACK], F32)
+        nc.scalar.copy(bias[:], nb_turn[:, :, 0])
 
-        for h in range(2):
-            cols = slice(h * HALF, (h + 1) * HALF)
-            nc.vector.quantize_mx(out=q_codes[:, cols].bitcast(FP8X4), scales=q_scales[:, cols],
-                                  in_=q_bf[h][:].rearrange("p w j -> p (w j)"))
+        def quantize_q(h):
+            return quantize_new("q_%s" + str(h), HALF, q_bf[h][:].rearrange("p w j -> p (w j)"))
 
-        kw_g = over_nb([P, PACK, P], U32, "kw_g", 4096)
-        nc.vector.tensor_copy(kw_g[:].rearrange("p t m -> p m t"), kw_pool[:].bitcast(U32).indirect(offsets[:]))
-        load_v(3, "slot_d")
+        g = []
 
-        g = big([P, PACK, NQ], F32, "g", "slot_g")
-        first = []
-        for t in range(PACK):
-            a = acc_pool.tile([P, NQ], F32, name="acc")
-            nc.tensor.matmul_mx(out=a[:], lhsT=kw_g[:, t, :].bitcast(FP8X4), lhsT_scale=ks_g[:, t, :],
-                                rhs=q_codes[:].bitcast(FP8X4), rhs_scale=q_scales[:], start=True, stop=True)
-            first.append(a)
-        for h in range(2):
-            cols = slice(h * HALF, (h + 1) * HALF)
+        def first(h, q_codes, q_scales):
+            banks = [bank("a%d%d" % (h, pair), 2 * h + pair, [P, 2, HALF]) for pair in range(2)]
             for t in range(PACK):
-                nc.scalar.activation(g[:, t, cols], first[t][:, cols], ACT.Gelu_apprx_tanh, bias=bias[:, t:t + 1])
+                nc.tensor.matmul_mx(out=banks[t // 2][:, t % 2, :], lhsT=kw_g[:, t, :].bitcast(FP8X4),
+                                    lhsT_scale=ks_g[:, t, :], rhs=q_codes[:].bitcast(FP8X4),
+                                    rhs_scale=q_scales[:], start=True, stop=True)
+            g.append(sbuf("g%d" % h, [P, PACK, HALF], F32))
+            for t in range(PACK):
+                nc.scalar.activation(g[h][:, t, :], banks[t // 2][:, t % 2, :], ACT.Gelu_apprx_tanh, bias=bias[:, t:t + 1])
 
-        v_codes = keep.tile([P, DV], U32, name="v_codes", align_bytes=64)
-        v_scales = keep.tile([P, DV], U8, name="v_scales", align_bytes=64)
+        q0 = quantize_q(0)
+        kw_g = sbuf("kw_g", [P, PACK, P], U32)
+        nc.vector.tensor_copy(kw_g[:].rearrange("p t m -> p m t"), kw_pool[:].bitcast(U32).indirect(offsets[:]))
+        load_v(3)
+        first(0, *q0)
+        first(1, *quantize_q(1))
+
+        v_q, y_q = {}, {}
 
         def gather_v(b):
-            if b == 0:
-                v_g = over_nb([P, 2, P, 2], BF16, "v_g0", 6144)
-            else:
-                v_g = big([P, 2, P, 2], BF16, "v_g%d" % b, "v_g%d" % b)
+            v_g = sbuf("v_g%d" % b, [P, 2, P, 2], BF16)
             nc.vector.tensor_copy(v_g[:].rearrange("p u m e -> p m u e"), v_pool[b][:].indirect(offsets[:]))
             words = v_g[:].rearrange("p u m e -> p (u m e)").bitcast(F32)
-            turn = turn_pool.tile([P, PACK, P], F32, name="turn")
+            turn = bank("v_turn%d" % b, b, [P, 2, P])
             for u in range(2):
-                nc.tensor.transpose(turn[:, u, :], words[:, u * P:(u + 1) * P], ident[:])
-            v_bf = big([P, P * PACK], BF16, "v_bf%d" % b, "v_bf%d" % b)
+                nc.tensor.transpose(turn[:, u, :], words[:, blocks[u]], ident[:])
+            v_bf = sbuf("v_bf%d" % b, [P, P * PACK], BF16)
             nc.scalar.copy(v_bf[:].bitcast(F32).rearrange("p (r u) -> p r u", u=2),
-                           turn[:, 0:2, :].rearrange("p u r -> p r u"))
+                           turn[:].rearrange("p u r -> p r u"))
             return v_bf
 
         def quantize_v(b, v_bf):
-            cols = slice(b * P, (b + 1) * P)
-            nc.vector.quantize_mx(out=v_codes[:, cols].bitcast(FP8X4), scales=v_scales[:, cols], in_=v_bf[:])
+            v_q[b] = quantize_new("v_%s" + str(b), P, v_bf[:])
 
-        y_bf = keep.tile([P, NQ, PACK], BF16, name="y_bf", align_bytes=64)
-        y_codes = keep.tile([P, NQ], U32, name="y_codes", align_bytes=64)
-        y_scales = keep.tile([P, NQ], U8, name="y_scales", align_bytes=64)
-        y_planes = keep.tile([P, PACK, NQ], BF16, name="y_planes")
-
-        def scale_y(h):
-            if h == 0:
-                nc.vector.tensor_tensor(packed(y_bf, 0), planes(g, 0), us_sb[:].to_broadcast([P, HALF // 4, PACK, 4]), ALU.mult)
-            else:
-                for t in range(PACK):
-                    nc.scalar.activation(y_planes[:, t, HALF:], g[:, t, HALF:], ACT.Copy, scale=us_sb[:, 0, t, :])
-                nc.vector.tensor_copy(packed(y_bf, 1), planes(y_planes, 1))
+        y_bf = []
 
         def quantize_y(h):
-            cols = slice(h * HALF, (h + 1) * HALF)
-            nc.vector.quantize_mx(out=y_codes[:, cols].bitcast(FP8X4), scales=y_scales[:, cols],
-                                  in_=y_bf[:, cols, :].rearrange("p w j -> p (w j)"))
+            y_q[h] = quantize_new("y_%s" + str(h), HALF, y_bf[h][:].rearrange("p w j -> p (w j)"))
 
         def second(b):
-            cols = slice(b * P, (b + 1) * P)
-            o = acc_pool.tile([P, 4, P], F32, name="acc")
+            o = bank("o%d" % b, 4 + b, [P, 4, P])
             for c in range(4):
-                rows = slice(c * P, (c + 1) * P)
-                nc.tensor.matmul_mx(out=o[:, c, :], lhsT=y_codes[:, rows].bitcast(FP8X4), lhsT_scale=y_scales[:, rows],
-                                    rhs=v_codes[:, cols].bitcast(FP8X4), rhs_scale=v_scales[:, cols], start=True, stop=True)
+                y_codes, y_scales = y_q[c // 2]
+                nc.tensor.matmul_mx(out=o[:, c, :], lhsT=y_codes[:, blocks[c % 2]].bitcast(FP8X4),
+                                    lhsT_scale=y_scales[:, blocks[c % 2]], rhs=v_q[b][0][:].bitcast(FP8X4),
+                                    rhs_scale=v_q[b][1][:], start=True, stop=True)
             return o
 
         def finish(b, o, res):
-            part = slice((b % 2) * P, (b % 2 + 1) * P)
-            nc.vector.tensor_tensor(res, o[:], rs_sb[b // 2][:, :, part], ALU.add)
+            nc.vector.tensor_tensor(res, o[:], rs_sb[b // 2][:, :, blocks[b % 2]], ALU.add)
 
         v0 = gather_v(0)
-        load_rs(0, "slot_a")
-        scale_y(0)
+        load_rs(0)
+        y_bf.append(sbuf("y_bf0", [P, HALF, PACK], BF16))
+        nc.vector.tensor_tensor(packed(y_bf[0][:]), planes(g[0][:]), us_sb[:].to_broadcast([P, HALF // 4, PACK, 4]), ALU.mult)
+        y_planes = sbuf("y_planes", [P, PACK, HALF], BF16)
+        for t in range(PACK):
+            nc.scalar.activation(y_planes[:, t, :], g[1][:, t, :], ACT.Copy, scale=us_sb[:, 0, t, :])
         v1 = gather_v(1)
-        load_rs(1, None)
+        load_rs(1)
         quantize_y(0)
         quantize_v(0, v0)
-        scale_y(1)
+        y_bf.append(sbuf("y_bf1", [P, HALF, PACK], BF16))
+        nc.vector.tensor_copy(packed(y_bf[1][:]), planes(y_planes[:]))
         v2 = gather_v(2)
         quantize_y(1)
         quantize_v(1, v1)
@@ -199,15 +214,15 @@ def tile_attend_mlpb_gelu_topk_kernel(tc, qT, k_words, k_scales, vT, nb, rs, us,
         v3 = gather_v(3)
         quantize_v(2, v2)
         o2 = second(2)
-        res01 = big([P, 4, 2 * P], F32, "res01", "slot_d")
-        finish(0, o0, res01[:, :, 0:P])
-        finish(1, o1, res01[:, :, P:2 * P])
-        nc.sync.dma_start(out_rows[:, :, 0:2 * P], res01[:])
+        res01 = sbuf("res01", [P, 4, HALF], F32)
+        finish(0, o0, res01[:, :, blocks[0]])
+        finish(1, o1, res01[:, :, blocks[1]])
+        nc.sync.dma_start(out_rows[:, :, halves[0]], res01[:])
         quantize_v(3, v3)
         o3 = second(3)
-        res2 = big([P, 4, P], F32, "res2", "v_bf3")
+        res2 = sbuf("res2", [P, 4, P], F32)
         finish(2, o2, res2[:])
-        nc.sync.dma_start(out_rows[:, :, 2 * P:3 * P], res2[:])
-        res3 = big([P, 4, P], F32, "res3", "res3")
+        nc.sync.dma_start(out_rows[:, :, blocks[2]], res2[:])
+        res3 = sbuf("res3", [P, 4, P], F32)
         finish(3, o3, res3[:])
-        nc.sync.dma_start(out_rows[:, :, 3 * P:4 * P], res3[:])
+        nc.sync.dma_start(out_rows[:, :, blocks[3]], res3[:])

@@ -21,20 +21,19 @@ P = 128
 PACK = 4
 HALF = NQ // 2
 NB_SPLIT = 1344
+K = 1024
 
 PLAN = {
-    "q_bf0": 0, "q_bf1": 2048, "v_g0": 3072, "kw_pool": 4096,
-    "v_pool3": 4608, "res01": 4608, "v_codes2": 8704, "v_scales2": 9216,
-    "warm_in": 12224, "us_sb": 12800,
-    "v_pool0": 12864, "rs_sb0": 12864, "y_bf0": 16960,
-    "v_pool1": 21056, "rs_sb1": 21056, "y_bf1": 25152, "v_g3": 25152,
-    "y_codes0": 27200, "v_codes0": 28224, "y_scales0": 28736, "v_scales0": 28992,
-    "ks_pool": 28224, "v_pool2": 29248, "q_raw": 30272,
-    "y_codes1": 29248, "v_codes1": 30272, "y_scales1": 30784, "v_scales1": 31040,
-    "nb_pool": 38464, "ks_list": 38464, "q_codes0": 40512, "q_scales1": 4096,"q_codes1": 41536, "kw_g": 42560,
-    "g0": 46656, "v_g1": 46656,
-    "y_planes": 50752, "v_g2": 50752,
-    "v_bf3": 52800, "res2": 52800,
+    "v_pool1": 0, "nb_pool": 4 * K, "v_pool2": 8 * K, "q_raw": 12 * K, "v_pool3": 16 * K, "kw_pool": 23 * K,
+    "y_codes1": 8 * K, "y_scales1": 9 * K, "v_codes01": 10 * K, "v_scales01": 11 * K,
+    "v_g0": 30 * K, "q_scales1": 29 * K,
+    "warm_in": 31 * K - 64, "us_sb": 31 * K,
+    "v_pool0": 31 * K + 64, "y_bf0": 32 * K, "rs_sb0": 34 * K, "rs_sb1": 36 * K, "rs_sb2": 38 * K,
+    "v_codes3": 34 * K,
+    "bias0": 42 * K, "v_g1": 42 * K,
+    "g1": 44 * K, "v_bf01": 44 * K,
+    "v_bf3": 52 * K, "res2": 52 * K,
+    "ks_pool": 54 * K, "q_codes0": 54 * K,
 }
 BANK = 2048
 
@@ -62,13 +61,10 @@ def tile_attend_mlpb_gelu_topk_kernel(tc, qT, k_words, k_scales, vT, nb, rs, us,
         def bank(name, number, shape):
             return psum.tile(shape, F32, name=name, offset=number * BANK)
 
-        def quantize(codes, scales, cols, values):
-            nc.vector.quantize_mx(out=codes[:, cols].bitcast(FP8X4), scales=scales[:, cols], in_=values)
-
         def quantize_new(name, width, values):
             codes = sbuf(name % "codes", [P, width], U32)
             scales = sbuf(name % "scales", [P, width], U8)
-            quantize(codes, scales, slice(0, width), values)
+            nc.vector.quantize_mx(out=codes[:].bitcast(FP8X4), scales=scales[:], in_=values)
             return codes, scales
 
         halves = [slice(h * HALF, (h + 1) * HALF) for h in range(2)]
@@ -81,21 +77,20 @@ def tile_attend_mlpb_gelu_topk_kernel(tc, qT, k_words, k_scales, vT, nb, rs, us,
         q_raw = sbuf("q_raw", [P, PACK, NQ], F32)
         nc.sync.dma_start(q_raw[:], qT[0].rearrange("(p j) w -> p j w", j=PACK))
 
-        warm_in = sbuf("warm_in", [P, 176], F32)
-        nc.gpsimd.memset(warm_in[:], 0.0)
-        warm = sbuf("warm", [P, 176], F32)
-        nc.scalar.activation(warm[:], warm_in[:], ACT.Gelu_apprx_tanh)
         ks_pool = sbuf("ks_pool", [P, T], U8)
         nc.gpsimd.memset(ks_pool[:].bitcast(I32), 0)
         for quad in range(4):
             nc.sync.dma_start(ks_pool[32 * quad:32 * quad + 4, :].bitcast(I32),
                               k_scales[0, 4 * quad:4 * quad + 4, :].bitcast(I32))
+        warm_in = sbuf("warm_in", [P, 48], F32)
+        nc.gpsimd.memset(warm_in[:], 0.0)
+        warm = sbuf("warm", [P, 48], F32)
+        nc.scalar.activation(warm[:], warm_in[:], ACT.Gelu_apprx_tanh)
         ident = sbuf("ident", [P, P], F32)
         make_identity(nc, ident[:])
+
         kw_pool = sbuf("kw_pool", [P, T], I32)
         nc.sync.dma_start(kw_pool[:], k_words[0].rearrange("p n t -> p (n t)").bitcast(I32))
-        us_sb = sbuf("us_sb", [P, 1, PACK, 1], F32)
-        nc.sync.dma_start(us_sb[:, 0, :, 0], us[0].rearrange("(p t) o -> p (t o)", t=PACK))
 
         v_pool = []
 
@@ -103,126 +98,134 @@ def tile_attend_mlpb_gelu_topk_kernel(tc, qT, k_words, k_scales, vT, nb, rs, us,
             v_pool.append(sbuf("v_pool%d" % b, [P, T], F32))
             nc.sync.dma_start(v_pool[b][:], vT[blocks[b], :])
 
-        rs_rows = rs[0].rearrange("(c p) e -> p c e", p=P)
-        out_rows = out[0].rearrange("(c p) e -> p c e", p=P)
-        rs_sb = []
-
-        def load_rs(h):
-            rs_sb.append(sbuf("rs_sb%d" % h, [P, 4, HALF], F32))
-            nc.sync.dma_start(rs_sb[h][:], rs_rows[:, :, halves[h]])
-
         load_v(0)
+        us_sb = sbuf("us_sb", [P, 1, PACK, 1], F32)
+        nc.sync.dma_start(us_sb[:, 0, :, 0], us[0].rearrange("(p t) o -> p (t o)", t=PACK))
 
         nb_pool = sbuf("nb_pool", [P, T], F32)
         nc.vector.memset(nb_pool[:], 0.0)
         nc.vector.tensor_copy(nb_pool[0:1, :NB_SPLIT], nb_row[:, :NB_SPLIT])
         nc.scalar.activation(nb_pool[0:1, NB_SPLIT:], nb_row[:, NB_SPLIT:], ACT.Copy)
+
+        rs_rows = rs[0].rearrange("(c p) e -> p c e", p=P)
+        out_rows = out[0].rearrange("(c p) e -> p c e", p=P)
+        rs_sb = []
+
+        def load_rs(rows, cols):
+            part = rs_rows[:, rows, cols]
+            rs_sb.append(sbuf("rs_sb%d" % len(rs_sb), list(part.shape), F32))
+            nc.sync.dma_start(rs_sb[-1][:], part)
+
         nb_list = sbuf("nb_list", [P, N], F32)
         nc.vector.tensor_copy(nb_list[:], nb_pool[:].indirect(offsets[:]))
-
+        load_v(1)
         ks_list = sbuf("ks_list", [P, N], U8)
         nc.vector.tensor_copy(ks_list[:], ks_pool[:].indirect(offsets[:]))
-        ks_g = sbuf("ks_g", [P, PACK, P], U8)
-        nc.vector.tensor_copy(ks_g[:], ks_list[:].rearrange("p (m t) -> p t m", t=PACK))
-        load_v(1)
 
         q_bf = [sbuf("q_bf%d" % h, [P, HALF, PACK], BF16) for h in range(2)]
         for h in range(2):
             nc.scalar.copy(packed(q_bf[h][:]), planes(q_raw[:, :, halves[h]]))
         load_v(2)
 
-        nb_turn = bank("nb_turn", 4, [P, PACK, P])
+        nb_turn = bank("nb_turn", 7, [P, PACK, P])
         for t in range(PACK):
             nc.tensor.transpose(nb_turn[:, t, :], nb_list[:, t:N:PACK], ident[:])
-        bias = sbuf("bias", [P, PACK], F32)
-        nc.scalar.copy(bias[:], nb_turn[:, :, 0])
+        bias = [sbuf("bias%d" % h, [P, PACK], F32) for h in range(2)]
+        for h in range(2):
+            nc.scalar.copy(bias[h][:], nb_turn[:, :, 0])
 
         def quantize_q(h):
             return quantize_new("q_%s" + str(h), HALF, q_bf[h][:].rearrange("p w j -> p (w j)"))
 
+        q_q0 = quantize_q(0)
+        ks_g = sbuf("ks_g", [P, PACK, P], U8)
+        nc.vector.tensor_copy(ks_g[:], ks_list[:].rearrange("p (m t) -> p t m", t=PACK))
+
+        kw_g = sbuf("kw_g", [P, PACK, P], U32)
+        nc.vector.tensor_copy(kw_g[:].rearrange("p t m -> p m t"), kw_pool[:].bitcast(U32).indirect(offsets[:]))
+        load_v(3)
+
         g = []
 
         def first(h, q_codes, q_scales):
-            banks = [bank("a%d%d" % (h, pair), 2 * h + pair, [P, 2, HALF]) for pair in range(2)]
+            banks = [bank("a%d%d" % (h, t), PACK * h + t, [P, HALF]) for t in range(PACK)]
             for t in range(PACK):
-                nc.tensor.matmul_mx(out=banks[t // 2][:, t % 2, :], lhsT=kw_g[:, t, :].bitcast(FP8X4),
+                nc.tensor.matmul_mx(out=banks[t][:], lhsT=kw_g[:, t, :].bitcast(FP8X4),
                                     lhsT_scale=ks_g[:, t, :], rhs=q_codes[:].bitcast(FP8X4),
                                     rhs_scale=q_scales[:], start=True, stop=True)
             g.append(sbuf("g%d" % h, [P, PACK, HALF], F32))
             for t in range(PACK):
-                nc.scalar.activation(g[h][:, t, :], banks[t // 2][:, t % 2, :], ACT.Gelu_apprx_tanh, bias=bias[:, t:t + 1])
+                nc.scalar.activation(g[h][:, t, :], banks[t][:], ACT.Gelu_apprx_tanh, bias=bias[h][:, t:t + 1])
 
-        q0 = quantize_q(0)
-        kw_g = sbuf("kw_g", [P, PACK, P], U32)
-        nc.vector.tensor_copy(kw_g[:].rearrange("p t m -> p m t"), kw_pool[:].bitcast(U32).indirect(offsets[:]))
-        load_v(3)
-        first(0, *q0)
+        first(0, *q_q0)
         first(1, *quantize_q(1))
 
-        v_q, y_q = {}, {}
-
         def gather_v(b):
-            v_g = sbuf("v_g%d" % b, [P, 2, P, 2], BF16)
-            nc.vector.tensor_copy(v_g[:].rearrange("p u m e -> p m u e"), v_pool[b][:].indirect(offsets[:]))
-            words = v_g[:].rearrange("p u m e -> p (u m e)").bitcast(F32)
+            v_g = sbuf("v_g%d" % b, [P, N], BF16)
+            nc.vector.tensor_copy(v_g[:], v_pool[b][:].indirect(offsets[:]))
+            words = v_g[:].bitcast(F32)
             turn = bank("v_turn%d" % b, b, [P, 2, P])
             for u in range(2):
-                nc.tensor.transpose(turn[:, u, :], words[:, blocks[u]], ident[:])
-            v_bf = sbuf("v_bf%d" % b, [P, P * PACK], BF16)
-            nc.scalar.copy(v_bf[:].bitcast(F32).rearrange("p (r u) -> p r u", u=2),
-                           turn[:].rearrange("p u r -> p r u"))
-            return v_bf
+                nc.tensor.transpose(turn[:, u, :], words[:, u:N // 2:2], ident[:])
+            return turn
 
-        def quantize_v(b, v_bf):
-            v_q[b] = quantize_new("v_%s" + str(b), P, v_bf[:])
+        def empty_turn(turn, v_bf):
+            nc.scalar.copy(v_bf.bitcast(F32).rearrange("p (r u) -> p r u", u=2), turn[:].rearrange("p u r -> p r u"))
 
+        y_q = {}
         y_bf = []
 
         def quantize_y(h):
             y_q[h] = quantize_new("y_%s" + str(h), HALF, y_bf[h][:].rearrange("p w j -> p (w j)"))
 
-        def second(b):
-            o = bank("o%d" % b, 4 + b, [P, 4, P])
-            for c in range(4):
-                y_codes, y_scales = y_q[c // 2]
-                nc.tensor.matmul_mx(out=o[:, c, :], lhsT=y_codes[:, blocks[c % 2]].bitcast(FP8X4),
-                                    lhsT_scale=y_scales[:, blocks[c % 2]], rhs=v_q[b][0][:].bitcast(FP8X4),
-                                    rhs_scale=v_q[b][1][:], start=True, stop=True)
-            return o
+        def second(o, c, v_q):
+            y_codes, y_scales = y_q[c // 2]
+            nc.tensor.matmul_mx(out=o, lhsT=y_codes[:, blocks[c % 2]].bitcast(FP8X4),
+                                lhsT_scale=y_scales[:, blocks[c % 2]], rhs=v_q[0][:].bitcast(FP8X4),
+                                rhs_scale=v_q[1][:], start=True, stop=True)
 
-        def finish(b, o, res):
-            nc.vector.tensor_tensor(res, o[:], rs_sb[b // 2][:, :, blocks[b % 2]], ALU.add)
-
-        v0 = gather_v(0)
-        load_rs(0)
+        turn0 = gather_v(0)
+        load_rs(slice(0, 2), halves[0])
+        load_rs(slice(2, 4), halves[0])
+        load_rs(slice(0, 4), halves[1])
         y_bf.append(sbuf("y_bf0", [P, HALF, PACK], BF16))
         nc.vector.tensor_tensor(packed(y_bf[0][:]), planes(g[0][:]), us_sb[:].to_broadcast([P, HALF // 4, PACK, 4]), ALU.mult)
         y_planes = sbuf("y_planes", [P, PACK, HALF], BF16)
         for t in range(PACK):
             nc.scalar.activation(y_planes[:, t, :], g[1][:, t, :], ACT.Copy, scale=us_sb[:, 0, t, :])
-        v1 = gather_v(1)
-        load_rs(1)
+        turn1 = gather_v(1)
+        v_bf01 = sbuf("v_bf01", [P, 2 * P * PACK], BF16)
+        empty_turn(turn0, v_bf01[:, :P * PACK])
         quantize_y(0)
-        quantize_v(0, v0)
         y_bf.append(sbuf("y_bf1", [P, HALF, PACK], BF16))
-        nc.vector.tensor_copy(packed(y_bf[1][:]), planes(y_planes[:]))
-        v2 = gather_v(2)
+        nc.scalar.copy(packed(y_bf[1][:]), planes(y_planes[:]))
+        empty_turn(turn1, v_bf01[:, P * PACK:])
+        turn2 = gather_v(2)
+        v_bf2 = sbuf("v_bf2", [P, P * PACK], BF16)
+        empty_turn(turn2, v_bf2[:])
+        v_q01 = quantize_new("v_%s01", 2 * P, v_bf01[:])
         quantize_y(1)
-        quantize_v(1, v1)
-        o0 = second(0)
-        o1 = second(1)
-        v3 = gather_v(3)
-        quantize_v(2, v2)
-        o2 = second(2)
+        o01 = [bank("o01_%d" % h, 4 + h, [P, 2, HALF]) for h in range(2)]
+        for c in range(4):
+            second(o01[c // 2][:, c % 2, :], c, v_q01)
+        v_q2 = quantize_new("v_%s2", P, v_bf2[:])
+        o2 = bank("o2", 6, [P, 4, P])
+        for c in range(4):
+            second(o2[:, c, :], c, v_q2)
+        turn3 = gather_v(3)
+        v_bf3 = sbuf("v_bf3", [P, P * PACK], BF16)
+        empty_turn(turn3, v_bf3[:])
         res01 = sbuf("res01", [P, 4, HALF], F32)
-        finish(0, o0, res01[:, :, blocks[0]])
-        finish(1, o1, res01[:, :, blocks[1]])
-        nc.sync.dma_start(out_rows[:, :, halves[0]], res01[:])
-        quantize_v(3, v3)
-        o3 = second(3)
+        for h in range(2):
+            nc.vector.tensor_tensor(res01[:, 2 * h:2 * h + 2, :], o01[h][:], rs_sb[h][:], ALU.add)
+            nc.sync.dma_start(out_rows[:, 2 * h:2 * h + 2, halves[0]], res01[:, 2 * h:2 * h + 2, :])
+        v_q3 = quantize_new("v_%s3", P, v_bf3[:])
+        o3 = bank("o3", 7, [P, 4, P])
+        for c in range(4):
+            second(o3[:, c, :], c, v_q3)
         res2 = sbuf("res2", [P, 4, P], F32)
-        finish(2, o2, res2[:])
+        nc.vector.tensor_tensor(res2[:], o2[:], rs_sb[2][:, :, blocks[0]], ALU.add)
         nc.sync.dma_start(out_rows[:, :, blocks[2]], res2[:])
         res3 = sbuf("res3", [P, 4, P], F32)
-        finish(3, o3, res3[:])
+        nc.vector.tensor_tensor(res3[:], o3[:], rs_sb[2][:, :, blocks[1]], ALU.add)
         nc.sync.dma_start(out_rows[:, :, blocks[3]], res3[:])

@@ -26,13 +26,13 @@ K = 1024
 PLAN = {
     "v_pool1": 0, "nb_pool": 4 * K, "v_pool2": 8 * K, "q_raw": 12 * K, "v_pool3": 16 * K, "kw_pool": 23 * K,
     "y_codes1": 8 * K, "y_scales1": 9 * K, "v_codes01": 10 * K, "v_scales01": 11 * K,
+    "y_codes0": 12 * K, "y_scales0": 13 * K, "v_codes2": 16 * K, "v_scales2": 17 * K,
     "v_g0": 30 * K, "q_scales1": 29 * K,
     "warm_in": 31 * K - 64, "us_sb": 31 * K,
     "v_pool0": 31 * K + 64, "y_bf0": 32 * K, "rs_sb0": 34 * K, "rs_sb1": 36 * K, "rs_sb2": 38 * K,
     "v_codes3": 34 * K,
-    "bias0": 42 * K, "v_g1": 42 * K,
+    "bias0": 42 * K, "v_g1": 42 * K, "y_bf1": 42 * K,
     "g1": 44 * K, "v_bf01": 44 * K,
-    "v_bf3": 52 * K, "res2": 52 * K,
     "ks_pool": 54 * K, "q_codes0": 54 * K,
 }
 BANK = 2048
@@ -196,36 +196,38 @@ def tile_attend_mlpb_gelu_topk_kernel(tc, qT, k_words, k_scales, vT, nb, rs, us,
         turn1 = gather_v(1)
         v_bf01 = sbuf("v_bf01", [P, 2 * P * PACK], BF16)
         empty_turn(turn0, v_bf01[:, :P * PACK])
-        quantize_y(0)
+        empty_turn(turn1, v_bf01[:, P * PACK:])
         y_bf.append(sbuf("y_bf1", [P, HALF, PACK], BF16))
         nc.scalar.copy(packed(y_bf[1][:]), planes(y_planes[:]))
-        empty_turn(turn1, v_bf01[:, P * PACK:])
         turn2 = gather_v(2)
         v_bf2 = sbuf("v_bf2", [P, P * PACK], BF16)
         empty_turn(turn2, v_bf2[:])
+        quantize_y(0)
         v_q01 = quantize_new("v_%s01", 2 * P, v_bf01[:])
         quantize_y(1)
         o01 = [bank("o01_%d" % h, 4 + h, [P, 2, HALF]) for h in range(2)]
         for c in range(4):
             second(o01[c // 2][:, c % 2, :], c, v_q01)
+        turn3 = gather_v(3)
+        v_bf3 = sbuf("v_bf3", [P, P * PACK], BF16)
+        empty_turn(turn3, v_bf3[:])
+
+        def finish(name, o, residual, rows, cols):
+            res = sbuf(name, list(o.shape), F32)
+            nc.vector.tensor_tensor(res[:], o, residual, ALU.add)
+            nc.sync.dma_start(out_rows[:, rows, cols], res[:])
+
+        finish("res01_0", o01[0][:], rs_sb[0][:], slice(0, 2), halves[0])
         v_q2 = quantize_new("v_%s2", P, v_bf2[:])
         o2 = bank("o2", 6, [P, 4, P])
         for c in range(4):
             second(o2[:, c, :], c, v_q2)
-        turn3 = gather_v(3)
-        v_bf3 = sbuf("v_bf3", [P, P * PACK], BF16)
-        empty_turn(turn3, v_bf3[:])
-        res01 = sbuf("res01", [P, 4, HALF], F32)
-        for h in range(2):
-            nc.vector.tensor_tensor(res01[:, 2 * h:2 * h + 2, :], o01[h][:], rs_sb[h][:], ALU.add)
-            nc.sync.dma_start(out_rows[:, 2 * h:2 * h + 2, halves[0]], res01[:, 2 * h:2 * h + 2, :])
+        finish("res01_1", o01[1][:], rs_sb[1][:], slice(2, 4), halves[0])
         v_q3 = quantize_new("v_%s3", P, v_bf3[:])
-        o3 = bank("o3", 7, [P, 4, P])
+        o3 = [bank("o3_%d" % h, 7 * h, [P, 2, P]) for h in range(2)]
         for c in range(4):
-            second(o3[:, c, :], c, v_q3)
-        res2 = sbuf("res2", [P, 4, P], F32)
-        nc.vector.tensor_tensor(res2[:], o2[:], rs_sb[2][:, :, blocks[0]], ALU.add)
-        nc.sync.dma_start(out_rows[:, :, blocks[2]], res2[:])
-        res3 = sbuf("res3", [P, 4, P], F32)
-        nc.vector.tensor_tensor(res3[:], o3[:], rs_sb[2][:, :, blocks[1]], ALU.add)
-        nc.sync.dma_start(out_rows[:, :, blocks[3]], res3[:])
+            second(o3[c // 2][:, c % 2, :], c, v_q3)
+        finish("res2", o2[:], rs_sb[2][:, :, blocks[0]], slice(0, 4), blocks[2])
+        for h in range(2):
+            rows = slice(2 * h, 2 * h + 2)
+            finish("res3_%d" % h, o3[h][:], rs_sb[2][:, rows, blocks[1]], rows, blocks[3])

@@ -26,12 +26,12 @@ K = 1024
 PLAN = {
     "v_pool1": 0, "nb_pool": 4 * K, "v_pool2": 8 * K, "q_raw": 12 * K, "v_pool3": 16 * K, "kw_pool": 23 * K,
     "y_codes1": 8 * K, "y_scales1": 9 * K, "v_codes01": 10 * K, "v_scales01": 11 * K,
-    "y_codes0": 12 * K, "y_scales0": 13 * K, "v_codes2": 16 * K, "v_scales2": 17 * K,
+    "y_codes0": 0, "y_scales0": K, "v_codes2": 16 * K, "v_scales2": 17 * K,
     "v_g0": 30 * K, "q_scales1": 29 * K,
     "warm_in": 31 * K - 64, "us_sb": 31 * K,
     "v_pool0": 31 * K + 64, "y_bf0": 32 * K, "rs_sb0": 34 * K, "rs_sb1": 36 * K, "rs_sb2": 38 * K,
     "v_codes3": 34 * K,
-    "bias0": 42 * K, "v_g1": 42 * K, "y_bf1": 42 * K,
+    "bias0": 42 * K, "v_g1": 42 * K,
     "g1": 44 * K, "v_bf01": 44 * K,
     "ks_pool": 54 * K, "q_codes0": 54 * K,
 }
@@ -77,15 +77,14 @@ def tile_attend_mlpb_gelu_topk_kernel(tc, qT, k_words, k_scales, vT, nb, rs, us,
         q_raw = sbuf("q_raw", [P, PACK, NQ], F32)
         nc.sync.dma_start(q_raw[:], qT[0].rearrange("(p j) w -> p j w", j=PACK))
 
-        ks_pool = sbuf("ks_pool", [P, T], U8)
-        nc.gpsimd.memset(ks_pool[:].bitcast(I32), 0)
-        for quad in range(4):
-            nc.sync.dma_start(ks_pool[32 * quad:32 * quad + 4, :].bitcast(I32),
-                              k_scales[0, 4 * quad:4 * quad + 4, :].bitcast(I32))
         warm_in = sbuf("warm_in", [P, 48], F32)
         nc.gpsimd.memset(warm_in[:], 0.0)
         warm = sbuf("warm", [P, 48], F32)
         nc.scalar.activation(warm[:], warm_in[:], ACT.Gelu_apprx_tanh)
+        ks_pool = sbuf("ks_pool", [P, T], U8)
+        nc.gpsimd.memset(ks_pool[:].bitcast(I32), 0)
+        for r in range(4):
+            nc.sync.dma_start(ks_pool[r:P:32, :].bitcast(I32), k_scales[0, r:16:4, :].bitcast(I32))
         ident = sbuf("ident", [P, P], F32)
         make_identity(nc, ident[:])
 
@@ -160,17 +159,16 @@ def tile_attend_mlpb_gelu_topk_kernel(tc, qT, k_words, k_scales, vT, nb, rs, us,
         first(0, *q_q0)
         first(1, *quantize_q(1))
 
-        def gather_v(b):
+        def gather_v(b, turn):
             v_g = sbuf("v_g%d" % b, [P, N], BF16)
             nc.vector.tensor_copy(v_g[:], v_pool[b][:].indirect(offsets[:]))
             words = v_g[:].bitcast(F32)
-            turn = bank("v_turn%d" % b, b, [P, 2, P])
             for u in range(2):
                 nc.tensor.transpose(turn[:, u, :], words[:, u:N // 2:2], ident[:])
-            return turn
 
         def empty_turn(turn, v_bf):
-            nc.scalar.copy(v_bf.bitcast(F32).rearrange("p (r u) -> p r u", u=2), turn[:].rearrange("p u r -> p r u"))
+            nc.scalar.copy(v_bf[:].bitcast(F32).rearrange("p (b r u) -> p b r u", r=P, u=2),
+                           turn[:].rearrange("p b u r -> p b r u"))
 
         y_q = {}
         y_bf = []
@@ -184,7 +182,8 @@ def tile_attend_mlpb_gelu_topk_kernel(tc, qT, k_words, k_scales, vT, nb, rs, us,
                                 lhsT_scale=y_scales[:, blocks[c % 2]], rhs=v_q[0][:].bitcast(FP8X4),
                                 rhs_scale=v_q[1][:], start=True, stop=True)
 
-        turn0 = gather_v(0)
+        turn01 = bank("v_turn01", 0, [P, 2, 2, P])
+        gather_v(0, turn01[:, 0])
         load_rs(slice(0, 2), halves[0])
         load_rs(slice(2, 4), halves[0])
         load_rs(slice(0, 4), halves[1])
@@ -193,24 +192,25 @@ def tile_attend_mlpb_gelu_topk_kernel(tc, qT, k_words, k_scales, vT, nb, rs, us,
         y_planes = sbuf("y_planes", [P, PACK, HALF], BF16)
         for t in range(PACK):
             nc.scalar.activation(y_planes[:, t, :], g[1][:, t, :], ACT.Copy, scale=us_sb[:, 0, t, :])
-        turn1 = gather_v(1)
+        gather_v(1, turn01[:, 1])
         v_bf01 = sbuf("v_bf01", [P, 2 * P * PACK], BF16)
-        empty_turn(turn0, v_bf01[:, :P * PACK])
-        empty_turn(turn1, v_bf01[:, P * PACK:])
+        quantize_y(0)
         y_bf.append(sbuf("y_bf1", [P, HALF, PACK], BF16))
         nc.scalar.copy(packed(y_bf[1][:]), planes(y_planes[:]))
-        turn2 = gather_v(2)
+        empty_turn(turn01, v_bf01)
+        turn2 = bank("v_turn2", 2, [P, 1, 2, P])
+        gather_v(2, turn2[:, 0])
         v_bf2 = sbuf("v_bf2", [P, P * PACK], BF16)
-        empty_turn(turn2, v_bf2[:])
-        quantize_y(0)
-        v_q01 = quantize_new("v_%s01", 2 * P, v_bf01[:])
+        empty_turn(turn2, v_bf2)
         quantize_y(1)
+        v_q01 = quantize_new("v_%s01", 2 * P, v_bf01[:])
         o01 = [bank("o01_%d" % h, 4 + h, [P, 2, HALF]) for h in range(2)]
         for c in range(4):
             second(o01[c // 2][:, c % 2, :], c, v_q01)
-        turn3 = gather_v(3)
+        turn3 = bank("v_turn3", 3, [P, 1, 2, P])
+        gather_v(3, turn3[:, 0])
         v_bf3 = sbuf("v_bf3", [P, P * PACK], BF16)
-        empty_turn(turn3, v_bf3[:])
+        empty_turn(turn3, v_bf3)
 
         def finish(name, o, residual, rows, cols):
             res = sbuf(name, list(o.shape), F32)

@@ -19,31 +19,33 @@ ALU = mybir.AluOpType
 
 P = 128
 PACK = 4
+RUN = 4
 HALF = NQ // 2
+SCALE_ROWS = 16
 NB_SPLIT = 1344
-K = 1024
+WARM_COLS = 48
+BANK = 2048
+KIB = 1024
 
 PLAN = {
-    "v_pool1": 0, "nb_pool": 4 * K, "v_pool2": 8 * K, "q_raw": 12 * K, "v_pool3": 16 * K, "kw_pool": 23 * K,
-    "y_codes1": 8 * K, "y_scales1": 9 * K, "v_codes01": 10 * K, "v_scales01": 11 * K,
-    "y_codes0": 0, "y_scales0": K, "v_codes2": 16 * K, "v_scales2": 17 * K,
-    "v_g0": 30 * K, "q_scales1": 29 * K,
-    "warm_in": 31 * K - 64, "us_sb": 31 * K,
-    "v_pool0": 31 * K + 64, "y_bf0": 32 * K, "rs_sb0": 34 * K, "rs_sb1": 36 * K, "rs_sb2": 38 * K,
-    "v_codes3": 34 * K,
-    "bias0": 42 * K, "v_g1": 42 * K,
-    "g1": 44 * K, "v_bf01": 44 * K,
-    "ks_pool": 54 * K, "q_codes0": 54 * K,
+    "v_pool1": 0, "nb_pool": 4 * KIB, "v_pool2": 8 * KIB, "q_raw": 12 * KIB, "v_pool3": 16 * KIB, "kw_pool": 23 * KIB,
+    "warm_in": 31 * KIB - 64, "us_sb": 31 * KIB, "v_pool0": 31 * KIB + 64,
+    "rs_sb0": 34 * KIB, "rs_sb1": 36 * KIB, "rs_sb2": 38 * KIB,
+    "ks_pool": 54 * KIB, "q_codes0": 54 * KIB, "q_scales1": 29 * KIB, "v_g0": 30 * KIB,
+    "y_bf1": 0,
+    "y_codes1": 8 * KIB, "y_scales1": 9 * KIB, "v_codes01": 10 * KIB, "v_scales01": 11 * KIB,
+    "y_codes23": 12 * KIB, "y_scales23": 13 * KIB,
+    "v_codes2": 16 * KIB, "v_scales2": 17 * KIB, "v_codes3": 34 * KIB,
+    "g123": 44 * KIB, "v_bf01": 44 * KIB,
 }
-BANK = 2048
 
 
 def packed(tile):
-    return tile.rearrange("p (c i) t -> p c t i", i=4)
+    return tile.rearrange("p (c i) t -> p c t i", i=RUN)
 
 
 def planes(tile):
-    return tile.rearrange("p t (c i) -> p c t i", i=4)
+    return tile.rearrange("p t (c i) -> p c t i", i=RUN)
 
 
 def tile_attend_mlpb_gelu_topk_kernel(tc, qT, k_words, k_scales, vT, nb, rs, us, offs, out):
@@ -61,14 +63,19 @@ def tile_attend_mlpb_gelu_topk_kernel(tc, qT, k_words, k_scales, vT, nb, rs, us,
         def bank(name, number, shape):
             return psum.tile(shape, F32, name=name, offset=number * BANK)
 
-        def quantize_new(name, width, values):
+        def quantize(name, width, values):
             codes = sbuf(name % "codes", [P, width], U32)
             scales = sbuf(name % "scales", [P, width], U8)
             nc.vector.quantize_mx(out=codes[:].bitcast(FP8X4), scales=scales[:], in_=values)
             return codes, scales
 
+        def product(o, stationary, moving):
+            nc.tensor.matmul_mx(out=o, lhsT=stationary[0].bitcast(FP8X4), lhsT_scale=stationary[1],
+                                rhs=moving[0].bitcast(FP8X4), rhs_scale=moving[1], start=True, stop=True)
+
         halves = [slice(h * HALF, (h + 1) * HALF) for h in range(2)]
         blocks = [slice(b * P, (b + 1) * P) for b in range(4)]
+        pairs = [slice(2 * h, 2 * h + 2) for h in range(2)]
 
         offsets = keep.tile([P, N // 16], U16, name="offsets")
         nc.sync.dma_start(offsets[:], offs)
@@ -77,14 +84,15 @@ def tile_attend_mlpb_gelu_topk_kernel(tc, qT, k_words, k_scales, vT, nb, rs, us,
         q_raw = sbuf("q_raw", [P, PACK, NQ], F32)
         nc.sync.dma_start(q_raw[:], qT[0].rearrange("(p j) w -> p j w", j=PACK))
 
-        warm_in = sbuf("warm_in", [P, 48], F32)
+        warm_in = sbuf("warm_in", [P, WARM_COLS], F32)
         nc.gpsimd.memset(warm_in[:], 0.0)
-        warm = sbuf("warm", [P, 48], F32)
+        warm = sbuf("warm", [P, WARM_COLS], F32)
         nc.scalar.activation(warm[:], warm_in[:], ACT.Gelu_apprx_tanh)
+
         ks_pool = sbuf("ks_pool", [P, T], U8)
         nc.gpsimd.memset(ks_pool[:].bitcast(I32), 0)
         for r in range(4):
-            nc.sync.dma_start(ks_pool[r:P:32, :].bitcast(I32), k_scales[0, r:16:4, :].bitcast(I32))
+            nc.sync.dma_start(ks_pool[r:P:32, :].bitcast(I32), k_scales[0, r:SCALE_ROWS:4, :].bitcast(I32))
         ident = sbuf("ident", [P, P], F32)
         make_identity(nc, ident[:])
 
@@ -110,8 +118,8 @@ def tile_attend_mlpb_gelu_topk_kernel(tc, qT, k_words, k_scales, vT, nb, rs, us,
         out_rows = out[0].rearrange("(c p) e -> p c e", p=P)
         rs_sb = []
 
-        def load_rs(rows, cols):
-            part = rs_rows[:, rows, cols]
+        def load_rs(query_blocks, features):
+            part = rs_rows[:, query_blocks, features]
             rs_sb.append(sbuf("rs_sb%d" % len(rs_sb), list(part.shape), F32))
             nc.sync.dma_start(rs_sb[-1][:], part)
 
@@ -129,35 +137,36 @@ def tile_attend_mlpb_gelu_topk_kernel(tc, qT, k_words, k_scales, vT, nb, rs, us,
         nb_turn = bank("nb_turn", 7, [P, PACK, P])
         for t in range(PACK):
             nc.tensor.transpose(nb_turn[:, t, :], nb_list[:, t:N:PACK], ident[:])
-        bias = [sbuf("bias%d" % h, [P, PACK], F32) for h in range(2)]
-        for h in range(2):
-            nc.scalar.copy(bias[h][:], nb_turn[:, :, 0])
+        bias = sbuf("bias", [P, PACK], F32)
+        nc.scalar.copy(bias[:], nb_turn[:, :, 0])
 
         def quantize_q(h):
-            return quantize_new("q_%s" + str(h), HALF, q_bf[h][:].rearrange("p w j -> p (w j)"))
+            return quantize("q_%s" + str(h), HALF, q_bf[h][:].rearrange("p w j -> p (w j)"))
 
-        q_q0 = quantize_q(0)
+        q_codes0, q_scales0 = quantize_q(0)
         ks_g = sbuf("ks_g", [P, PACK, P], U8)
         nc.vector.tensor_copy(ks_g[:], ks_list[:].rearrange("p (m t) -> p t m", t=PACK))
-
         kw_g = sbuf("kw_g", [P, PACK, P], U32)
         nc.vector.tensor_copy(kw_g[:].rearrange("p t m -> p m t"), kw_pool[:].bitcast(U32).indirect(offsets[:]))
         load_v(3)
+        keys = [(kw_g[:, t, :], ks_g[:, t, :]) for t in range(PACK)]
 
-        g = []
-
-        def first(h, q_codes, q_scales):
-            banks = [bank("a%d%d" % (h, t), PACK * h + t, [P, HALF]) for t in range(PACK)]
+        def gelu(name, banks, width):
+            g = sbuf(name, [P, PACK, width], F32)
             for t in range(PACK):
-                nc.tensor.matmul_mx(out=banks[t][:], lhsT=kw_g[:, t, :].bitcast(FP8X4),
-                                    lhsT_scale=ks_g[:, t, :], rhs=q_codes[:].bitcast(FP8X4),
-                                    rhs_scale=q_scales[:], start=True, stop=True)
-            g.append(sbuf("g%d" % h, [P, PACK, HALF], F32))
-            for t in range(PACK):
-                nc.scalar.activation(g[h][:, t, :], banks[t][:], ACT.Gelu_apprx_tanh, bias=bias[h][:, t:t + 1])
+                nc.scalar.activation(g[:, t, :], banks[t][:], ACT.Gelu_apprx_tanh, bias=bias[:, t:t + 1])
+            return g
 
-        first(0, *q_q0)
-        first(1, *quantize_q(1))
+        a0 = [bank("a0_%d" % t, t, [P, P]) for t in range(PACK)]
+        for t in range(PACK):
+            product(a0[t][:], keys[t], (q_codes0[:, blocks[0]], q_scales0[:, blocks[0]]))
+        g0 = gelu("g0", a0, P)
+        q_codes1, q_scales1 = quantize_q(1)
+        a123 = [bank("a123_%d" % t, PACK + t, [P, 3 * P]) for t in range(PACK)]
+        for t in range(PACK):
+            product(a123[t][:, :P], keys[t], (q_codes0[:, blocks[1]], q_scales0[:, blocks[1]]))
+            product(a123[t][:, P:], keys[t], (q_codes1[:], q_scales1[:]))
+        g123 = gelu("g123", a123, 3 * P)
 
         def gather_v(b, turn):
             v_g = sbuf("v_g%d" % b, [P, N], BF16)
@@ -166,68 +175,73 @@ def tile_attend_mlpb_gelu_topk_kernel(tc, qT, k_words, k_scales, vT, nb, rs, us,
             for u in range(2):
                 nc.tensor.transpose(turn[:, u, :], words[:, u:N // 2:2], ident[:])
 
-        def empty_turn(turn, v_bf):
-            nc.scalar.copy(v_bf[:].bitcast(F32).rearrange("p (b r u) -> p b r u", r=P, u=2),
-                           turn[:].rearrange("p b u r -> p b r u"))
+        def empty_turn(name, turn):
+            v_bf = sbuf(name, [P, turn.shape[1] * P * PACK], BF16)
+            nc.scalar.copy(v_bf[:].bitcast(F32).rearrange("p (b e u) -> p b e u", e=P, u=2),
+                           turn[:].rearrange("p b u e -> p b e u"))
+            return v_bf
 
-        y_q = {}
-        y_bf = []
+        def quantize_v(name, v_bf):
+            codes, scales = quantize(name, v_bf.shape[1] // PACK, v_bf[:])
+            return codes[:], scales[:]
 
-        def quantize_y(h):
-            y_q[h] = quantize_new("y_%s" + str(h), HALF, y_bf[h][:].rearrange("p w j -> p (w j)"))
+        def scale_y(name, g_block):
+            y_bf = sbuf(name, [P, P, PACK], BF16)
+            nc.vector.tensor_tensor(packed(y_bf[:]), planes(g_block),
+                                    us_sb[:].to_broadcast([P, P // RUN, PACK, RUN]), ALU.mult)
+            return y_bf
 
-        def second(o, c, v_q):
-            y_codes, y_scales = y_q[c // 2]
-            nc.tensor.matmul_mx(out=o, lhsT=y_codes[:, blocks[c % 2]].bitcast(FP8X4),
-                                lhsT_scale=y_scales[:, blocks[c % 2]], rhs=v_q[0][:].bitcast(FP8X4),
-                                rhs_scale=v_q[1][:], start=True, stop=True)
+        y_q = []
+
+        def quantize_y(name, y_bf):
+            width = y_bf.shape[1]
+            codes, scales = quantize(name, width, y_bf[:].rearrange("p w j -> p (w j)"))
+            y_q.extend((codes[:, cols], scales[:, cols]) for cols in blocks[:width // P])
+
+        def finish(name, o, residual, query_blocks, features):
+            res = sbuf(name, list(o.shape), F32)
+            nc.vector.tensor_tensor(res[:], o, residual, ALU.add)
+            nc.sync.dma_start(out_rows[:, query_blocks, features], res[:])
 
         turn01 = bank("v_turn01", 0, [P, 2, 2, P])
         gather_v(0, turn01[:, 0])
-        load_rs(slice(0, 2), halves[0])
-        load_rs(slice(2, 4), halves[0])
+        for query_blocks in pairs:
+            load_rs(query_blocks, halves[0])
         load_rs(slice(0, 4), halves[1])
-        y_bf.append(sbuf("y_bf0", [P, HALF, PACK], BF16))
-        nc.vector.tensor_tensor(packed(y_bf[0][:]), planes(g[0][:]), us_sb[:].to_broadcast([P, HALF // 4, PACK, 4]), ALU.mult)
+        quantize_y("y_%s0", scale_y("y_bf0", g0[:]))
         y_planes = sbuf("y_planes", [P, PACK, HALF], BF16)
         for t in range(PACK):
-            nc.scalar.activation(y_planes[:, t, :], g[1][:, t, :], ACT.Copy, scale=us_sb[:, 0, t, :])
+            nc.scalar.activation(y_planes[:, t, :], g123[:, t, P:], ACT.Copy, scale=us_sb[:, 0, t, :])
         gather_v(1, turn01[:, 1])
-        v_bf01 = sbuf("v_bf01", [P, 2 * P * PACK], BF16)
-        quantize_y(0)
-        y_bf.append(sbuf("y_bf1", [P, HALF, PACK], BF16))
-        nc.scalar.copy(packed(y_bf[1][:]), planes(y_planes[:]))
-        empty_turn(turn01, v_bf01)
+        y_bf1 = scale_y("y_bf1", g123[:, :, :P])
+        y_bf23 = sbuf("y_bf23", [P, HALF, PACK], BF16)
+        nc.scalar.copy(packed(y_bf23[:]), planes(y_planes[:]))
+        v_bf01 = empty_turn("v_bf01", turn01)
         turn2 = bank("v_turn2", 2, [P, 1, 2, P])
         gather_v(2, turn2[:, 0])
-        v_bf2 = sbuf("v_bf2", [P, P * PACK], BF16)
-        empty_turn(turn2, v_bf2)
-        quantize_y(1)
-        v_q01 = quantize_new("v_%s01", 2 * P, v_bf01[:])
+        v_bf2 = empty_turn("v_bf2", turn2)
+        quantize_y("y_%s1", y_bf1)
+        quantize_y("y_%s23", y_bf23)
+
+        v_q01 = quantize_v("v_%s01", v_bf01)
         o01 = [bank("o01_%d" % h, 4 + h, [P, 2, HALF]) for h in range(2)]
         for c in range(4):
-            second(o01[c // 2][:, c % 2, :], c, v_q01)
+            product(o01[c // 2][:, c % 2, :], y_q[c], v_q01)
         turn3 = bank("v_turn3", 3, [P, 1, 2, P])
         gather_v(3, turn3[:, 0])
-        v_bf3 = sbuf("v_bf3", [P, P * PACK], BF16)
-        empty_turn(turn3, v_bf3)
+        v_bf3 = empty_turn("v_bf3", turn3)
 
-        def finish(name, o, residual, rows, cols):
-            res = sbuf(name, list(o.shape), F32)
-            nc.vector.tensor_tensor(res[:], o, residual, ALU.add)
-            nc.sync.dma_start(out_rows[:, rows, cols], res[:])
-
-        finish("res01_0", o01[0][:], rs_sb[0][:], slice(0, 2), halves[0])
-        v_q2 = quantize_new("v_%s2", P, v_bf2[:])
+        finish("res01_0", o01[0][:], rs_sb[0][:], pairs[0], halves[0])
+        v_q2 = quantize_v("v_%s2", v_bf2)
         o2 = bank("o2", 6, [P, 4, P])
         for c in range(4):
-            second(o2[:, c, :], c, v_q2)
-        finish("res01_1", o01[1][:], rs_sb[1][:], slice(2, 4), halves[0])
-        v_q3 = quantize_new("v_%s3", P, v_bf3[:])
-        o3 = [bank("o3_%d" % h, 7 * h, [P, 2, P]) for h in range(2)]
+            product(o2[:, c, :], y_q[c], v_q2)
+        finish("res01_1", o01[1][:], rs_sb[1][:], pairs[1], halves[0])
+
+        v_q3 = quantize_v("v_%s3", v_bf3)
+        o3 = [bank("o3_%d" % h, number, [P, 2, P]) for h, number in enumerate((0, 7))]
         for c in range(4):
-            second(o3[c // 2][:, c % 2, :], c, v_q3)
+            product(o3[c // 2][:, c % 2, :], y_q[c], v_q3)
         finish("res2", o2[:], rs_sb[2][:, :, blocks[0]], slice(0, 4), blocks[2])
         for h in range(2):
-            rows = slice(2 * h, 2 * h + 2)
-            finish("res3_%d" % h, o3[h][:], rs_sb[2][:, rows, blocks[1]], rows, blocks[3])
+            finish("res3_%d" % h, o3[h][:], rs_sb[2][:, pairs[h], blocks[1]], pairs[h], blocks[3])

@@ -22,7 +22,6 @@ PACK = 4
 RUN = 4
 HALF = NQ // 2
 SCALE_ROWS = 16
-NB_SPLIT = 1344
 WARM_COLS = 48
 BANK = 2048
 KIB = 1024
@@ -32,11 +31,10 @@ PLAN = {
     "warm_in": 31 * KIB - 64, "us_sb": 31 * KIB, "v_pool0": 31 * KIB + 64,
     "rs_sb0": 34 * KIB, "rs_sb1": 36 * KIB, "rs_sb2": 38 * KIB,
     "ks_pool": 54 * KIB, "q_codes0": 54 * KIB, "q_scales1": 29 * KIB, "v_g0": 30 * KIB,
-    "y_bf1": 0,
-    "y_codes1": 8 * KIB, "y_scales1": 9 * KIB, "v_codes01": 10 * KIB, "v_scales01": 11 * KIB,
+    "v_codes1": 10 * KIB, "v_scales1": 11 * KIB,
     "y_codes23": 12 * KIB, "y_scales23": 13 * KIB,
     "v_codes2": 16 * KIB, "v_scales2": 17 * KIB, "v_codes3": 34 * KIB,
-    "g123": 44 * KIB, "v_bf01": 44 * KIB,
+    "y_planes": 29 * KIB,
 }
 
 
@@ -79,8 +77,9 @@ def tile_attend_mlpb_gelu_topk_kernel(tc, qT, k_words, k_scales, vT, nb, rs, us,
 
         offsets = keep.tile([P, N // 16], U16, name="offsets")
         nc.sync.dma_start(offsets[:], offs)
-        nb_row = sbuf("nb_row", [1, T], F32)
-        nc.scalar.dma_start(nb_row[:], nb[0:1, :])
+        nb_pool = sbuf("nb_pool", [P, T], F32)
+        nc.scalar.dma_start(nb_pool[P - 1:P, :], nb[0:1, :])
+        nc.vector.memset(nb_pool[:P - 1, :], 0.0)
         q_raw = sbuf("q_raw", [P, PACK, NQ], F32)
         nc.sync.dma_start(q_raw[:], qT[0].rearrange("(p j) w -> p j w", j=PACK))
 
@@ -109,11 +108,6 @@ def tile_attend_mlpb_gelu_topk_kernel(tc, qT, k_words, k_scales, vT, nb, rs, us,
         us_sb = sbuf("us_sb", [P, 1, PACK, 1], F32)
         nc.sync.dma_start(us_sb[:, 0, :, 0], us[0].rearrange("(p t) o -> p (t o)", t=PACK))
 
-        nb_pool = sbuf("nb_pool", [P, T], F32)
-        nc.vector.memset(nb_pool[:], 0.0)
-        nc.vector.tensor_copy(nb_pool[0:1, :NB_SPLIT], nb_row[:, :NB_SPLIT])
-        nc.scalar.activation(nb_pool[0:1, NB_SPLIT:], nb_row[:, NB_SPLIT:], ACT.Copy)
-
         rs_rows = rs[0].rearrange("(c p) e -> p c e", p=P)
         out_rows = out[0].rearrange("(c p) e -> p c e", p=P)
         rs_sb = []
@@ -138,7 +132,7 @@ def tile_attend_mlpb_gelu_topk_kernel(tc, qT, k_words, k_scales, vT, nb, rs, us,
         for t in range(PACK):
             nc.tensor.transpose(nb_turn[:, t, :], nb_list[:, t:N:PACK], ident[:])
         bias = sbuf("bias", [P, PACK], F32)
-        nc.scalar.copy(bias[:], nb_turn[:, :, 0])
+        nc.scalar.copy(bias[:], nb_turn[:, :, P - 1])
 
         def quantize_q(h):
             return quantize("q_%s" + str(h), HALF, q_bf[h][:].rearrange("p w j -> p (w j)"))
@@ -151,38 +145,34 @@ def tile_attend_mlpb_gelu_topk_kernel(tc, qT, k_words, k_scales, vT, nb, rs, us,
         load_v(3)
         keys = [(kw_g[:, t, :], ks_g[:, t, :]) for t in range(PACK)]
 
-        def gelu(name, banks, width):
-            g = sbuf(name, [P, PACK, width], F32)
+        def first_product(name, first_bank, queries):
+            width = queries[0].shape[1]
+            a = [bank("a%s_%d" % (name, t), first_bank + t, [P, width]) for t in range(PACK)]
             for t in range(PACK):
-                nc.scalar.activation(g[:, t, :], banks[t][:], ACT.Gelu_apprx_tanh, bias=bias[:, t:t + 1])
+                product(a[t][:], keys[t], queries)
+            g = sbuf("g" + name, [P, PACK, width], F32)
+            for t in range(PACK):
+                nc.scalar.activation(g[:, t, :], a[t][:], ACT.Gelu_apprx_tanh, bias=bias[:, t:t + 1])
             return g
 
-        a0 = [bank("a0_%d" % t, t, [P, P]) for t in range(PACK)]
-        for t in range(PACK):
-            product(a0[t][:], keys[t], (q_codes0[:, blocks[0]], q_scales0[:, blocks[0]]))
-        g0 = gelu("g0", a0, P)
+        g0 = first_product("0", 0, (q_codes0[:, blocks[0]], q_scales0[:, blocks[0]]))
+        g1 = first_product("1", PACK, (q_codes0[:, blocks[1]], q_scales0[:, blocks[1]]))
         q_codes1, q_scales1 = quantize_q(1)
-        a123 = [bank("a123_%d" % t, PACK + t, [P, 3 * P]) for t in range(PACK)]
-        for t in range(PACK):
-            product(a123[t][:, :P], keys[t], (q_codes0[:, blocks[1]], q_scales0[:, blocks[1]]))
-            product(a123[t][:, P:], keys[t], (q_codes1[:], q_scales1[:]))
-        g123 = gelu("g123", a123, 3 * P)
+        g23 = first_product("23", 0, (q_codes1[:], q_scales1[:]))
 
-        def gather_v(b, turn):
+        def gather_v(b):
             v_g = sbuf("v_g%d" % b, [P, N], BF16)
             nc.vector.tensor_copy(v_g[:], v_pool[b][:].indirect(offsets[:]))
             words = v_g[:].bitcast(F32)
+            turn = bank("v_turn%d" % b, b, [P, 2, P])
             for u in range(2):
                 nc.tensor.transpose(turn[:, u, :], words[:, u:N // 2:2], ident[:])
-
-        def empty_turn(name, turn):
-            v_bf = sbuf(name, [P, turn.shape[1] * P * PACK], BF16)
-            nc.scalar.copy(v_bf[:].bitcast(F32).rearrange("p (b e u) -> p b e u", e=P, u=2),
-                           turn[:].rearrange("p b u e -> p b e u"))
+            v_bf = sbuf("v_bf%d" % b, [P, P * PACK], BF16)
+            nc.scalar.copy(v_bf[:].bitcast(F32).rearrange("p (e u) -> p e u", u=2), turn[:].rearrange("p u e -> p e u"))
             return v_bf
 
-        def quantize_v(name, v_bf):
-            codes, scales = quantize(name, v_bf.shape[1] // PACK, v_bf[:])
+        def quantize_v(b, v_bf):
+            codes, scales = quantize("v_%s" + str(b), P, v_bf[:])
             return codes[:], scales[:]
 
         def scale_y(name, g_block):
@@ -203,42 +193,38 @@ def tile_attend_mlpb_gelu_topk_kernel(tc, qT, k_words, k_scales, vT, nb, rs, us,
             nc.vector.tensor_tensor(res[:], o, residual, ALU.add)
             nc.sync.dma_start(out_rows[:, query_blocks, features], res[:])
 
-        turn01 = bank("v_turn01", 0, [P, 2, 2, P])
-        gather_v(0, turn01[:, 0])
+        v_bf0 = gather_v(0)
         for query_blocks in pairs:
             load_rs(query_blocks, halves[0])
         load_rs(slice(0, 4), halves[1])
-        quantize_y("y_%s0", scale_y("y_bf0", g0[:]))
+        y_bf01 = [scale_y("y_bf%d" % c, g[:]) for c, g in enumerate((g0, g1))]
+        for c in range(2):
+            quantize_y("y_%s" + str(c), y_bf01[c])
+        v_q = [quantize_v(0, v_bf0)]
         y_planes = sbuf("y_planes", [P, PACK, HALF], BF16)
         for t in range(PACK):
-            nc.scalar.activation(y_planes[:, t, :], g123[:, t, P:], ACT.Copy, scale=us_sb[:, 0, t, :])
-        gather_v(1, turn01[:, 1])
-        y_bf1 = scale_y("y_bf1", g123[:, :, :P])
+            nc.scalar.activation(y_planes[:, t, :], g23[:, t, :], ACT.Copy, scale=us_sb[:, 0, t, :])
         y_bf23 = sbuf("y_bf23", [P, HALF, PACK], BF16)
         nc.scalar.copy(packed(y_bf23[:]), planes(y_planes[:]))
-        v_bf01 = empty_turn("v_bf01", turn01)
-        turn2 = bank("v_turn2", 2, [P, 1, 2, P])
-        gather_v(2, turn2[:, 0])
-        v_bf2 = empty_turn("v_bf2", turn2)
-        quantize_y("y_%s1", y_bf1)
+        v_bf1 = gather_v(1)
+        v_bf2 = gather_v(2)
         quantize_y("y_%s23", y_bf23)
+        v_q.append(quantize_v(1, v_bf1))
 
-        v_q01 = quantize_v("v_%s01", v_bf01)
         o01 = [bank("o01_%d" % h, 4 + h, [P, 2, HALF]) for h in range(2)]
-        for c in range(4):
-            product(o01[c // 2][:, c % 2, :], y_q[c], v_q01)
-        turn3 = bank("v_turn3", 3, [P, 1, 2, P])
-        gather_v(3, turn3[:, 0])
-        v_bf3 = empty_turn("v_bf3", turn3)
+        for b in range(2):
+            for c in range(4):
+                product(o01[c // 2][:, c % 2, blocks[b]], y_q[c], v_q[b])
+        v_bf3 = gather_v(3)
 
         finish("res01_0", o01[0][:], rs_sb[0][:], pairs[0], halves[0])
-        v_q2 = quantize_v("v_%s2", v_bf2)
+        v_q2 = quantize_v(2, v_bf2)
         o2 = bank("o2", 6, [P, 4, P])
         for c in range(4):
             product(o2[:, c, :], y_q[c], v_q2)
         finish("res01_1", o01[1][:], rs_sb[1][:], pairs[1], halves[0])
 
-        v_q3 = quantize_v("v_%s3", v_bf3)
+        v_q3 = quantize_v(3, v_bf3)
         o3 = [bank("o3_%d" % h, number, [P, 2, P]) for h, number in enumerate((0, 7))]
         for c in range(4):
             product(o3[c // 2][:, c % 2, :], y_q[c], v_q3)

@@ -22,19 +22,17 @@ PACK = 4
 RUN = 4
 HALF = NQ // 2
 SCALE_ROWS = 16
-WARM_COLS = 48
+WARM_COLS = 8
 BANK = 2048
 KIB = 1024
 
 PLAN = {
-    "v_pool1": 0, "nb_pool": 4 * KIB, "v_pool2": 8 * KIB, "q_raw": 12 * KIB, "v_pool3": 16 * KIB, "kw_pool": 23 * KIB,
-    "warm_in": 31 * KIB - 64, "us_sb": 31 * KIB, "v_pool0": 31 * KIB + 64,
-    "rs_sb0": 34 * KIB, "rs_sb1": 36 * KIB, "rs_sb2": 38 * KIB,
-    "ks_pool": 54 * KIB, "q_codes0": 54 * KIB, "q_scales1": 29 * KIB, "v_g0": 30 * KIB,
-    "v_codes1": 10 * KIB, "v_scales1": 11 * KIB,
-    "y_codes23": 12 * KIB, "y_scales23": 13 * KIB,
-    "v_codes2": 16 * KIB, "v_scales2": 17 * KIB, "v_codes3": 34 * KIB,
-    "y_planes": 29 * KIB,
+    "ks_pool": 0, "q_codes0": 0,
+    "kw_pool": 2 * KIB, "q_scales1": 2 * KIB,
+    "v_pool2": 10 * KIB, "v_codes1": 10 * KIB, "v_scales1": 11 * KIB, "y_codes1": 12 * KIB, "y_scales1": 13 * KIB,
+    "v_pool3": 18 * KIB, "v_codes2": 18 * KIB, "v_scales2": 19 * KIB,
+    "rs_sb1": 30 * KIB, "v_codes3": 30 * KIB,
+    "v_g0": 28 * KIB, "y_planes": 28 * KIB,
 }
 
 
@@ -77,26 +75,30 @@ def tile_attend_mlpb_gelu_topk_kernel(tc, qT, k_words, k_scales, vT, nb, rs, us,
 
         offsets = keep.tile([P, N // 16], U16, name="offsets")
         nc.sync.dma_start(offsets[:], offs)
+        ks_pool = sbuf("ks_pool", [P, T], U8)
+        nc.gpsimd.memset(ks_pool[:].bitcast(I32), 0)
         nb_pool = sbuf("nb_pool", [P, T], F32)
         nc.scalar.dma_start(nb_pool[P - 1:P, :], nb[0:1, :])
         nc.vector.memset(nb_pool[:P - 1, :], 0.0)
-        q_raw = sbuf("q_raw", [P, PACK, NQ], F32)
-        nc.sync.dma_start(q_raw[:], qT[0].rearrange("(p j) w -> p j w", j=PACK))
+        q_rows = qT[0].rearrange("(p j) w -> p j w", j=PACK)
+        q_raw = []
+
+        def load_q(h):
+            q_raw.append(sbuf("q_raw%d" % h, [P, PACK, HALF], F32))
+            nc.sync.dma_start(q_raw[h][:], q_rows[:, :, halves[h]])
+
+        load_q(0)
+        for r in range(4):
+            nc.sync.dma_start(ks_pool[r:P:32, :].bitcast(I32), k_scales[0, r:SCALE_ROWS:4, :].bitcast(I32))
+        kw_pool = sbuf("kw_pool", [P, T], I32)
+        nc.sync.dma_start(kw_pool[:], k_words[0].rearrange("p n t -> p (n t)").bitcast(I32))
 
         warm_in = sbuf("warm_in", [P, WARM_COLS], F32)
         nc.gpsimd.memset(warm_in[:], 0.0)
         warm = sbuf("warm", [P, WARM_COLS], F32)
         nc.scalar.activation(warm[:], warm_in[:], ACT.Gelu_apprx_tanh)
-
-        ks_pool = sbuf("ks_pool", [P, T], U8)
-        nc.gpsimd.memset(ks_pool[:].bitcast(I32), 0)
-        for r in range(4):
-            nc.sync.dma_start(ks_pool[r:P:32, :].bitcast(I32), k_scales[0, r:SCALE_ROWS:4, :].bitcast(I32))
         ident = sbuf("ident", [P, P], F32)
         make_identity(nc, ident[:])
-
-        kw_pool = sbuf("kw_pool", [P, T], I32)
-        nc.sync.dma_start(kw_pool[:], k_words[0].rearrange("p n t -> p (n t)").bitcast(I32))
 
         v_pool = []
 
@@ -104,6 +106,7 @@ def tile_attend_mlpb_gelu_topk_kernel(tc, qT, k_words, k_scales, vT, nb, rs, us,
             v_pool.append(sbuf("v_pool%d" % b, [P, T], F32))
             nc.sync.dma_start(v_pool[b][:], vT[blocks[b], :])
 
+        load_q(1)
         load_v(0)
         us_sb = sbuf("us_sb", [P, 1, PACK, 1], F32)
         nc.sync.dma_start(us_sb[:, 0, :, 0], us[0].rearrange("(p t) o -> p (t o)", t=PACK))
@@ -117,56 +120,59 @@ def tile_attend_mlpb_gelu_topk_kernel(tc, qT, k_words, k_scales, vT, nb, rs, us,
             rs_sb.append(sbuf("rs_sb%d" % len(rs_sb), list(part.shape), F32))
             nc.sync.dma_start(rs_sb[-1][:], part)
 
+        for b in range(1, 4):
+            load_v(b)
+        load_rs(slice(0, 1), halves[0])
+        load_rs(pairs[1], halves[0])
+        load_rs(slice(1, 2), halves[0])
+        load_rs(slice(0, 4), halves[1])
         nb_list = sbuf("nb_list", [P, N], F32)
         nc.vector.tensor_copy(nb_list[:], nb_pool[:].indirect(offsets[:]))
-        load_v(1)
         ks_list = sbuf("ks_list", [P, N], U8)
         nc.vector.tensor_copy(ks_list[:], ks_pool[:].indirect(offsets[:]))
 
-        q_bf = [sbuf("q_bf%d" % h, [P, HALF, PACK], BF16) for h in range(2)]
-        for h in range(2):
-            nc.scalar.copy(packed(q_bf[h][:]), planes(q_raw[:, :, halves[h]]))
-        load_v(2)
+        def cast_q(h):
+            q_bf = sbuf("q_bf%d" % h, [P, HALF, PACK], BF16)
+            nc.scalar.copy(packed(q_bf[:]), planes(q_raw[h][:]))
+            return q_bf
 
+        def quantize_q(h, q_bf):
+            codes, scales = quantize("q_%s" + str(h), HALF, q_bf[:].rearrange("p w j -> p (w j)"))
+            return codes[:], scales[:]
+
+        q_bf0 = cast_q(0)
         nb_turn = bank("nb_turn", 7, [P, PACK, P])
         for t in range(PACK):
             nc.tensor.transpose(nb_turn[:, t, :], nb_list[:, t:N:PACK], ident[:])
         bias = sbuf("bias", [P, PACK], F32)
         nc.scalar.copy(bias[:], nb_turn[:, :, P - 1])
 
-        def quantize_q(h):
-            return quantize("q_%s" + str(h), HALF, q_bf[h][:].rearrange("p w j -> p (w j)"))
-
-        q_codes0, q_scales0 = quantize_q(0)
+        q_q0 = quantize_q(0, q_bf0)
         ks_g = sbuf("ks_g", [P, PACK, P], U8)
         nc.vector.tensor_copy(ks_g[:], ks_list[:].rearrange("p (m t) -> p t m", t=PACK))
         kw_g = sbuf("kw_g", [P, PACK, P], U32)
         nc.vector.tensor_copy(kw_g[:].rearrange("p t m -> p m t"), kw_pool[:].bitcast(U32).indirect(offsets[:]))
-        load_v(3)
         keys = [(kw_g[:, t, :], ks_g[:, t, :]) for t in range(PACK)]
 
-        def first_product(name, first_bank, queries):
-            width = queries[0].shape[1]
-            a = [bank("a%s_%d" % (name, t), first_bank + t, [P, width]) for t in range(PACK)]
+        def first_product(h, queries):
+            a = [bank("a%d_%d" % (h, t), PACK * h + t, [P, HALF]) for t in range(PACK)]
             for t in range(PACK):
                 product(a[t][:], keys[t], queries)
-            g = sbuf("g" + name, [P, PACK, width], F32)
+            g = sbuf("g%d" % h, [P, PACK, HALF], F32)
             for t in range(PACK):
                 nc.scalar.activation(g[:, t, :], a[t][:], ACT.Gelu_apprx_tanh, bias=bias[:, t:t + 1])
             return g
 
-        g0 = first_product("0", 0, (q_codes0[:, blocks[0]], q_scales0[:, blocks[0]]))
-        g1 = first_product("1", PACK, (q_codes0[:, blocks[1]], q_scales0[:, blocks[1]]))
-        q_codes1, q_scales1 = quantize_q(1)
-        g23 = first_product("23", 0, (q_codes1[:], q_scales1[:]))
-
         def gather_v(b):
             v_g = sbuf("v_g%d" % b, [P, N], BF16)
-            nc.vector.tensor_copy(v_g[:], v_pool[b][:].indirect(offsets[:]))
+            nc.vector.tensor_copy(v_g[:].rearrange("p (u m s) -> p m u s", u=2, s=2), v_pool[b][:].indirect(offsets[:]))
+            return v_g
+
+        def turn_v(b, v_g):
             words = v_g[:].bitcast(F32)
             turn = bank("v_turn%d" % b, b, [P, 2, P])
             for u in range(2):
-                nc.tensor.transpose(turn[:, u, :], words[:, u:N // 2:2], ident[:])
+                nc.tensor.transpose(turn[:, u, :], words[:, blocks[u]], ident[:])
             v_bf = sbuf("v_bf%d" % b, [P, P * PACK], BF16)
             nc.scalar.copy(v_bf[:].bitcast(F32).rearrange("p (e u) -> p e u", u=2), turn[:].rearrange("p u e -> p e u"))
             return v_bf
@@ -175,10 +181,11 @@ def tile_attend_mlpb_gelu_topk_kernel(tc, qT, k_words, k_scales, vT, nb, rs, us,
             codes, scales = quantize("v_%s" + str(b), P, v_bf[:])
             return codes[:], scales[:]
 
-        def scale_y(name, g_block):
-            y_bf = sbuf(name, [P, P, PACK], BF16)
-            nc.vector.tensor_tensor(packed(y_bf[:]), planes(g_block),
-                                    us_sb[:].to_broadcast([P, P // RUN, PACK, RUN]), ALU.mult)
+        def scale_y(name, g_part):
+            width = g_part.shape[2]
+            y_bf = sbuf(name, [P, width, PACK], BF16)
+            nc.vector.tensor_tensor(packed(y_bf[:]), planes(g_part),
+                                    us_sb[:].to_broadcast([P, width // RUN, PACK, RUN]), ALU.mult)
             return y_bf
 
         y_q = []
@@ -193,41 +200,51 @@ def tile_attend_mlpb_gelu_topk_kernel(tc, qT, k_words, k_scales, vT, nb, rs, us,
             nc.vector.tensor_tensor(res[:], o, residual, ALU.add)
             nc.sync.dma_start(out_rows[:, query_blocks, features], res[:])
 
-        v_bf0 = gather_v(0)
-        for query_blocks in pairs:
-            load_rs(query_blocks, halves[0])
-        load_rs(slice(0, 4), halves[1])
-        y_bf01 = [scale_y("y_bf%d" % c, g[:]) for c, g in enumerate((g0, g1))]
-        for c in range(2):
-            quantize_y("y_%s" + str(c), y_bf01[c])
+        q_bf1 = cast_q(1)
+        g0 = first_product(0, q_q0)
+        q_q1 = quantize_q(1, q_bf1)
+        g1 = first_product(1, q_q1)
+        v_g0 = gather_v(0)
+        v_bf0 = turn_v(0, v_g0)
+        y_bf0 = scale_y("y_bf0", g0[:])
         v_q = [quantize_v(0, v_bf0)]
+        quantize_y("y_%s0", y_bf0)
         y_planes = sbuf("y_planes", [P, PACK, HALF], BF16)
         for t in range(PACK):
-            nc.scalar.activation(y_planes[:, t, :], g23[:, t, :], ACT.Copy, scale=us_sb[:, 0, t, :])
-        y_bf23 = sbuf("y_bf23", [P, HALF, PACK], BF16)
-        nc.scalar.copy(packed(y_bf23[:]), planes(y_planes[:]))
-        v_bf1 = gather_v(1)
-        v_bf2 = gather_v(2)
-        quantize_y("y_%s23", y_bf23)
+            nc.scalar.activation(y_planes[:, t, :], g1[:, t, :], ACT.Copy, scale=us_sb[:, 0, t, :])
+        y_bf1 = sbuf("y_bf1", [P, HALF, PACK], BF16)
+        nc.scalar.copy(packed(y_bf1[:]), planes(y_planes[:]))
+        v_g1 = gather_v(1)
+        v_bf1 = turn_v(1, v_g1)
+        v_g2 = gather_v(2)
+        v_bf2 = turn_v(2, v_g2)
         v_q.append(quantize_v(1, v_bf1))
+        quantize_y("y_%s1", y_bf1)
 
-        o01 = [bank("o01_%d" % h, 4 + h, [P, 2, HALF]) for h in range(2)]
-        for b in range(2):
-            for c in range(4):
-                product(o01[c // 2][:, c % 2, blocks[b]], y_q[c], v_q[b])
-        v_bf3 = gather_v(3)
+        parts = [slice(0, 1), slice(1, 2), pairs[1]]
+        o01 = [bank("o01_%d" % i, 4 + i, [P, part.stop - part.start, HALF]) for i, part in enumerate(parts)]
+        for o, part in zip(o01, parts):
+            for c in range(part.start, part.stop):
+                for b in range(2):
+                    product(o[:, c - part.start, blocks[b]], y_q[c], v_q[b])
+        o_sb = sbuf("o_sb", [P, 1, HALF], F32)
+        nc.scalar.copy(o_sb[:], o01[0][:])
+        res0 = sbuf("res0", [P, 1, HALF], F32)
+        nc.gpsimd.tensor_tensor(res0[:], o_sb[:], rs_sb[0][:], ALU.add)
+        nc.sync.dma_start(out_rows[:, 0:1, halves[0]], res0[:])
+        v_g3 = gather_v(3)
+        v_bf3 = turn_v(3, v_g3)
 
-        finish("res01_0", o01[0][:], rs_sb[0][:], pairs[0], halves[0])
         v_q2 = quantize_v(2, v_bf2)
-        o2 = bank("o2", 6, [P, 4, P])
+        o2 = bank("o2", 7, [P, 4, P])
         for c in range(4):
             product(o2[:, c, :], y_q[c], v_q2)
-        finish("res01_1", o01[1][:], rs_sb[1][:], pairs[1], halves[0])
-
+        finish("res01_1", o01[2][:], rs_sb[1][:], parts[2], halves[0])
+        finish("res01_0", o01[1][:], rs_sb[2][:], parts[1], halves[0])
         v_q3 = quantize_v(3, v_bf3)
-        o3 = [bank("o3_%d" % h, number, [P, 2, P]) for h, number in enumerate((0, 7))]
+        o3 = [bank("o3_%d" % h, h, [P, 2, P]) for h in range(2)]
         for c in range(4):
             product(o3[c // 2][:, c % 2, :], y_q[c], v_q3)
-        finish("res2", o2[:], rs_sb[2][:, :, blocks[0]], slice(0, 4), blocks[2])
+        finish("res2", o2[:], rs_sb[3][:, :, blocks[0]], slice(0, 4), blocks[2])
         for h in range(2):
-            finish("res3_%d" % h, o3[h][:], rs_sb[2][:, pairs[h], blocks[1]], pairs[h], blocks[3])
+            finish("res3_%d" % h, o3[h][:], rs_sb[3][:, pairs[h], blocks[1]], pairs[h], blocks[3])

@@ -122,9 +122,9 @@ def tile_attend_mlpb_gelu_topk_kernel(tc, qT, k_words, k_scales, vT, nb, rs, us,
 
         for b in range(1, 4):
             load_v(b)
-        load_rs(slice(0, 1), halves[0])
+        load_rs(pairs[0], blocks[0])
         load_rs(pairs[1], halves[0])
-        load_rs(slice(1, 2), halves[0])
+        load_rs(pairs[0], blocks[1])
         load_rs(slice(0, 4), halves[1])
         nb_list = sbuf("nb_list", [P, N], F32)
         nc.vector.tensor_copy(nb_list[:], nb_pool[:].indirect(offsets[:]))
@@ -216,22 +216,29 @@ def tile_attend_mlpb_gelu_topk_kernel(tc, qT, k_words, k_scales, vT, nb, rs, us,
         nc.scalar.copy(packed(y_bf1[:]), planes(y_planes[:]))
         v_g1 = gather_v(1)
         v_bf1 = turn_v(1, v_g1)
+        o00 = bank("o00", 4, [P, 2, P])
+        for c in range(2):
+            product(o00[:, c, :], y_q[c], v_q[0])
+        o_sb = sbuf("o_sb", [P, 2, P], F32)
+        nc.scalar.copy(o_sb[:], o00[:])
+        res0 = sbuf("res0", [P, 2, P], F32)
+        nc.gpsimd.tensor_tensor(res0[:], o_sb[:], rs_sb[0][:], ALU.add)
+        nc.sync.dma_start(out_rows[:, pairs[0], blocks[0]], res0[:])
+        idle = bank("idle", 1, [P, N])
+        for i in range(2):
+            product(idle[:], (q_q0[0][:, blocks[i]], q_q0[1][:, blocks[i]]),
+                    (kw_g[:].rearrange("p t m -> p (t m)"), ks_g[:].rearrange("p t m -> p (t m)")))
         v_g2 = gather_v(2)
         v_bf2 = turn_v(2, v_g2)
         v_q.append(quantize_v(1, v_bf1))
         quantize_y("y_%s1", y_bf1)
-
-        parts = [slice(0, 1), slice(1, 2), pairs[1]]
-        o01 = [bank("o01_%d" % i, 4 + i, [P, part.stop - part.start, HALF]) for i, part in enumerate(parts)]
-        for o, part in zip(o01, parts):
-            for c in range(part.start, part.stop):
-                for b in range(2):
-                    product(o[:, c - part.start, blocks[b]], y_q[c], v_q[b])
-        o_sb = sbuf("o_sb", [P, 1, HALF], F32)
-        nc.scalar.copy(o_sb[:], o01[0][:])
-        res0 = sbuf("res0", [P, 1, HALF], F32)
-        nc.gpsimd.tensor_tensor(res0[:], o_sb[:], rs_sb[0][:], ALU.add)
-        nc.sync.dma_start(out_rows[:, 0:1, halves[0]], res0[:])
+        o01 = bank("o01", 5, [P, 2, P])
+        for c in range(2):
+            product(o01[:, c, :], y_q[c], v_q[1])
+        o23 = bank("o23", 6, [P, 2, HALF])
+        for c in range(2):
+            for b in range(2):
+                product(o23[:, c, blocks[b]], y_q[2 + c], v_q[b])
         v_g3 = gather_v(3)
         v_bf3 = turn_v(3, v_g3)
 
@@ -239,8 +246,8 @@ def tile_attend_mlpb_gelu_topk_kernel(tc, qT, k_words, k_scales, vT, nb, rs, us,
         o2 = bank("o2", 7, [P, 4, P])
         for c in range(4):
             product(o2[:, c, :], y_q[c], v_q2)
-        finish("res01_1", o01[2][:], rs_sb[1][:], parts[2], halves[0])
-        finish("res01_0", o01[1][:], rs_sb[2][:], parts[1], halves[0])
+        finish("res23", o23[:], rs_sb[1][:], pairs[1], halves[0])
+        finish("res01", o01[:], rs_sb[2][:], pairs[0], blocks[1])
         v_q3 = quantize_v(3, v_bf3)
         o3 = [bank("o3_%d" % h, h, [P, 2, P]) for h in range(2)]
         for c in range(4):

@@ -22,7 +22,6 @@ PACK = 4
 RUN = 4
 HALF = NQ // 2
 SCALE_ROWS = 16
-WARM_COLS = 8
 BANK = 2048
 KIB = 1024
 
@@ -31,8 +30,8 @@ PLAN = {
     "kw_pool": 2 * KIB, "q_scales1": 2 * KIB,
     "v_pool2": 10 * KIB, "v_codes1": 10 * KIB, "v_scales1": 11 * KIB, "y_codes1": 12 * KIB, "y_scales1": 13 * KIB,
     "v_pool3": 18 * KIB, "v_codes2": 18 * KIB, "v_scales2": 19 * KIB,
-    "rs_sb1": 30 * KIB, "v_codes3": 30 * KIB,
     "v_g0": 28 * KIB, "y_planes": 28 * KIB,
+    "rs_sb1": 30 * KIB, "v_codes3": 30 * KIB,
 }
 
 
@@ -63,7 +62,10 @@ def tile_attend_mlpb_gelu_topk_kernel(tc, qT, k_words, k_scales, vT, nb, rs, us,
             codes = sbuf(name % "codes", [P, width], U32)
             scales = sbuf(name % "scales", [P, width], U8)
             nc.vector.quantize_mx(out=codes[:].bitcast(FP8X4), scales=scales[:], in_=values)
-            return codes, scales
+            return codes[:], scales[:]
+
+        def columns(operand, cols):
+            return operand[0][:, cols], operand[1][:, cols]
 
         def product(o, stationary, moving):
             nc.tensor.matmul_mx(out=o, lhsT=stationary[0].bitcast(FP8X4), lhsT_scale=stationary[1],
@@ -77,55 +79,38 @@ def tile_attend_mlpb_gelu_topk_kernel(tc, qT, k_words, k_scales, vT, nb, rs, us,
         nc.sync.dma_start(offsets[:], offs)
         ks_pool = sbuf("ks_pool", [P, T], U8)
         nc.gpsimd.memset(ks_pool[:].bitcast(I32), 0)
+
+        warm_in = sbuf("warm_in", [P, 1], F32)
+        nc.vector.memset(warm_in[:], 0.0)
         nb_pool = sbuf("nb_pool", [P, T], F32)
         nc.scalar.dma_start(nb_pool[P - 1:P, :], nb[0:1, :])
         nc.vector.memset(nb_pool[:P - 1, :], 0.0)
-        q_rows = qT[0].rearrange("(p j) w -> p j w", j=PACK)
-        q_raw = []
-
-        def load_q(h):
-            q_raw.append(sbuf("q_raw%d" % h, [P, PACK, HALF], F32))
-            nc.sync.dma_start(q_raw[h][:], q_rows[:, :, halves[h]])
-
-        load_q(0)
-        for r in range(4):
-            nc.sync.dma_start(ks_pool[r:P:32, :].bitcast(I32), k_scales[0, r:SCALE_ROWS:4, :].bitcast(I32))
-        kw_pool = sbuf("kw_pool", [P, T], I32)
-        nc.sync.dma_start(kw_pool[:], k_words[0].rearrange("p n t -> p (n t)").bitcast(I32))
-
-        warm_in = sbuf("warm_in", [P, WARM_COLS], F32)
-        nc.gpsimd.memset(warm_in[:], 0.0)
-        warm = sbuf("warm", [P, WARM_COLS], F32)
+        warm = sbuf("warm", [P, 1], F32)
         nc.scalar.activation(warm[:], warm_in[:], ACT.Gelu_apprx_tanh)
         ident = sbuf("ident", [P, P], F32)
         make_identity(nc, ident[:])
 
-        v_pool = []
-
-        def load_v(b):
-            v_pool.append(sbuf("v_pool%d" % b, [P, T], F32))
-            nc.sync.dma_start(v_pool[b][:], vT[blocks[b], :])
-
-        load_q(1)
-        load_v(0)
-        us_sb = sbuf("us_sb", [P, 1, PACK, 1], F32)
-        nc.sync.dma_start(us_sb[:, 0, :, 0], us[0].rearrange("(p t) o -> p (t o)", t=PACK))
-
+        q_rows = qT[0].rearrange("(p j) w -> p j w", j=PACK)
         rs_rows = rs[0].rearrange("(c p) e -> p c e", p=P)
         out_rows = out[0].rearrange("(c p) e -> p c e", p=P)
-        rs_sb = []
 
-        def load_rs(query_blocks, features):
-            part = rs_rows[:, query_blocks, features]
-            rs_sb.append(sbuf("rs_sb%d" % len(rs_sb), list(part.shape), F32))
-            nc.sync.dma_start(rs_sb[-1][:], part)
+        def load(name, source, dtype=F32):
+            tile = sbuf(name, list(source.shape), dtype)
+            nc.sync.dma_start(tile[:], source)
+            return tile
 
-        for b in range(1, 4):
-            load_v(b)
-        load_rs(pairs[0], blocks[0])
-        load_rs(pairs[1], halves[0])
-        load_rs(pairs[0], blocks[1])
-        load_rs(slice(0, 4), halves[1])
+        q_raw = [load("q_raw0", q_rows[:, :, halves[0]])]
+        for r in range(4):
+            nc.sync.dma_start(ks_pool[r:P:32, :].bitcast(I32), k_scales[0, r:SCALE_ROWS:4, :].bitcast(I32))
+        kw_pool = load("kw_pool", k_words[0].rearrange("p n t -> p (n t)").bitcast(I32), I32)
+        q_raw.append(load("q_raw1", q_rows[:, :, halves[1]]))
+        v_pool = [load("v_pool0", vT[blocks[0], :])]
+        us_sb = sbuf("us_sb", [P, 1, PACK, 1], F32)
+        nc.sync.dma_start(us_sb[:, 0, :, 0], us[0].rearrange("(p t) o -> p (t o)", t=PACK))
+        v_pool.extend(load("v_pool%d" % b, vT[blocks[b], :]) for b in range(1, 4))
+        pieces = [(pairs[0], blocks[0]), (pairs[1], halves[0]), (pairs[0], blocks[1]), (slice(0, 4), halves[1])]
+        rs_sb = [load("rs_sb%d" % i, rs_rows[:, rows, features]) for i, (rows, features) in enumerate(pieces)]
+
         nb_list = sbuf("nb_list", [P, N], F32)
         nc.vector.tensor_copy(nb_list[:], nb_pool[:].indirect(offsets[:]))
         ks_list = sbuf("ks_list", [P, N], U8)
@@ -136,9 +121,8 @@ def tile_attend_mlpb_gelu_topk_kernel(tc, qT, k_words, k_scales, vT, nb, rs, us,
             nc.scalar.copy(packed(q_bf[:]), planes(q_raw[h][:]))
             return q_bf
 
-        def quantize_q(h, q_bf):
-            codes, scales = quantize("q_%s" + str(h), HALF, q_bf[:].rearrange("p w j -> p (w j)"))
-            return codes[:], scales[:]
+        def quantize_half(name, words):
+            return quantize(name, HALF, words[:].rearrange("p w j -> p (w j)"))
 
         q_bf0 = cast_q(0)
         nb_turn = bank("nb_turn", 7, [P, PACK, P])
@@ -147,17 +131,16 @@ def tile_attend_mlpb_gelu_topk_kernel(tc, qT, k_words, k_scales, vT, nb, rs, us,
         bias = sbuf("bias", [P, PACK], F32)
         nc.scalar.copy(bias[:], nb_turn[:, :, P - 1])
 
-        q_q0 = quantize_q(0, q_bf0)
+        q_q0 = quantize_half("q_%s0", q_bf0)
         ks_g = sbuf("ks_g", [P, PACK, P], U8)
         nc.vector.tensor_copy(ks_g[:], ks_list[:].rearrange("p (m t) -> p t m", t=PACK))
         kw_g = sbuf("kw_g", [P, PACK, P], U32)
         nc.vector.tensor_copy(kw_g[:].rearrange("p t m -> p m t"), kw_pool[:].bitcast(U32).indirect(offsets[:]))
-        keys = [(kw_g[:, t, :], ks_g[:, t, :]) for t in range(PACK)]
 
         def first_product(h, queries):
             a = [bank("a%d_%d" % (h, t), PACK * h + t, [P, HALF]) for t in range(PACK)]
             for t in range(PACK):
-                product(a[t][:], keys[t], queries)
+                product(a[t][:], (kw_g[:, t, :], ks_g[:, t, :]), queries)
             g = sbuf("g%d" % h, [P, PACK, HALF], F32)
             for t in range(PACK):
                 nc.scalar.activation(g[:, t, :], a[t][:], ACT.Gelu_apprx_tanh, bias=bias[:, t:t + 1])
@@ -166,9 +149,6 @@ def tile_attend_mlpb_gelu_topk_kernel(tc, qT, k_words, k_scales, vT, nb, rs, us,
         def gather_v(b):
             v_g = sbuf("v_g%d" % b, [P, N], BF16)
             nc.vector.tensor_copy(v_g[:].rearrange("p (u m s) -> p m u s", u=2, s=2), v_pool[b][:].indirect(offsets[:]))
-            return v_g
-
-        def turn_v(b, v_g):
             words = v_g[:].bitcast(F32)
             turn = bank("v_turn%d" % b, b, [P, 2, P])
             for u in range(2):
@@ -178,69 +158,56 @@ def tile_attend_mlpb_gelu_topk_kernel(tc, qT, k_words, k_scales, vT, nb, rs, us,
             return v_bf
 
         def quantize_v(b, v_bf):
-            codes, scales = quantize("v_%s" + str(b), P, v_bf[:])
-            return codes[:], scales[:]
+            return quantize("v_%s" + str(b), P, v_bf[:])
 
-        def scale_y(name, g_part):
-            width = g_part.shape[2]
-            y_bf = sbuf(name, [P, width, PACK], BF16)
-            nc.vector.tensor_tensor(packed(y_bf[:]), planes(g_part),
-                                    us_sb[:].to_broadcast([P, width // RUN, PACK, RUN]), ALU.mult)
-            return y_bf
-
-        y_q = []
-
-        def quantize_y(name, y_bf):
-            width = y_bf.shape[1]
-            codes, scales = quantize(name, width, y_bf[:].rearrange("p w j -> p (w j)"))
-            y_q.extend((codes[:, cols], scales[:, cols]) for cols in blocks[:width // P])
-
-        def finish(name, o, residual, query_blocks, features):
+        def finish(name, o, residual, rows, features):
             res = sbuf(name, list(o.shape), F32)
             nc.vector.tensor_tensor(res[:], o, residual, ALU.add)
-            nc.sync.dma_start(out_rows[:, query_blocks, features], res[:])
+            nc.sync.dma_start(out_rows[:, rows, features], res[:])
 
         q_bf1 = cast_q(1)
         g0 = first_product(0, q_q0)
-        q_q1 = quantize_q(1, q_bf1)
-        g1 = first_product(1, q_q1)
-        v_g0 = gather_v(0)
-        v_bf0 = turn_v(0, v_g0)
-        y_bf0 = scale_y("y_bf0", g0[:])
-        v_q = [quantize_v(0, v_bf0)]
-        quantize_y("y_%s0", y_bf0)
+        g1 = first_product(1, quantize_half("q_%s1", q_bf1))
+
+        v_bf0 = gather_v(0)
+        y_bf0 = sbuf("y_bf0", [P, HALF, PACK], BF16)
+        nc.vector.tensor_tensor(packed(y_bf0[:]), planes(g0[:]),
+                                us_sb[:].to_broadcast([P, HALF // RUN, PACK, RUN]), ALU.mult)
+        v_q0 = quantize_v(0, v_bf0)
+        y_q0 = quantize_half("y_%s0", y_bf0)
         y_planes = sbuf("y_planes", [P, PACK, HALF], BF16)
         for t in range(PACK):
             nc.scalar.activation(y_planes[:, t, :], g1[:, t, :], ACT.Copy, scale=us_sb[:, 0, t, :])
         y_bf1 = sbuf("y_bf1", [P, HALF, PACK], BF16)
         nc.scalar.copy(packed(y_bf1[:]), planes(y_planes[:]))
-        v_g1 = gather_v(1)
-        v_bf1 = turn_v(1, v_g1)
+        v_bf1 = gather_v(1)
+
         o00 = bank("o00", 4, [P, 2, P])
         for c in range(2):
-            product(o00[:, c, :], y_q[c], v_q[0])
+            product(o00[:, c, :], columns(y_q0, blocks[c]), v_q0)
         o_sb = sbuf("o_sb", [P, 2, P], F32)
         nc.scalar.copy(o_sb[:], o00[:])
         res0 = sbuf("res0", [P, 2, P], F32)
         nc.gpsimd.tensor_tensor(res0[:], o_sb[:], rs_sb[0][:], ALU.add)
         nc.sync.dma_start(out_rows[:, pairs[0], blocks[0]], res0[:])
-        idle = bank("idle", 1, [P, N])
-        for i in range(2):
-            product(idle[:], (q_q0[0][:, blocks[i]], q_q0[1][:, blocks[i]]),
+
+        idle = bank("idle", 4, [P, N])
+        for c in range(2):
+            product(idle[:], columns(q_q0, blocks[c]),
                     (kw_g[:].rearrange("p t m -> p (t m)"), ks_g[:].rearrange("p t m -> p (t m)")))
-        v_g2 = gather_v(2)
-        v_bf2 = turn_v(2, v_g2)
-        v_q.append(quantize_v(1, v_bf1))
-        quantize_y("y_%s1", y_bf1)
+
+        v_bf2 = gather_v(2)
+        y_q1 = quantize_half("y_%s1", y_bf1)
+        y_q = [columns(half, blocks[c]) for half in (y_q0, y_q1) for c in range(2)]
+        v_q1 = quantize_v(1, v_bf1)
         o01 = bank("o01", 5, [P, 2, P])
-        for c in range(2):
-            product(o01[:, c, :], y_q[c], v_q[1])
         o23 = bank("o23", 6, [P, 2, HALF])
+        for b, v_q in enumerate((v_q0, v_q1)):
+            for c in range(2):
+                product(o23[:, c, blocks[b]], y_q[2 + c], v_q)
         for c in range(2):
-            for b in range(2):
-                product(o23[:, c, blocks[b]], y_q[2 + c], v_q[b])
-        v_g3 = gather_v(3)
-        v_bf3 = turn_v(3, v_g3)
+            product(o01[:, c, :], y_q[c], v_q1)
+        v_bf3 = gather_v(3)
 
         v_q2 = quantize_v(2, v_bf2)
         o2 = bank("o2", 7, [P, 4, P])
@@ -248,6 +215,7 @@ def tile_attend_mlpb_gelu_topk_kernel(tc, qT, k_words, k_scales, vT, nb, rs, us,
             product(o2[:, c, :], y_q[c], v_q2)
         finish("res23", o23[:], rs_sb[1][:], pairs[1], halves[0])
         finish("res01", o01[:], rs_sb[2][:], pairs[0], blocks[1])
+
         v_q3 = quantize_v(3, v_bf3)
         o3 = [bank("o3_%d" % h, h, [P, 2, P]) for h in range(2)]
         for c in range(4):

@@ -29,7 +29,7 @@ PLAN = {
     "ks_pool": 0, "q_codes0": 0,
     "kw_pool": 2 * KIB, "q_scales1": 2 * KIB,
     "v_pool2": 10 * KIB, "v_codes1": 10 * KIB, "v_scales1": 11 * KIB, "y_codes1": 12 * KIB, "y_scales1": 13 * KIB,
-    "v_pool3": 18 * KIB, "v_codes2": 18 * KIB, "v_scales2": 19 * KIB,
+    "rs_sb0": 18 * KIB, "v_codes2": 18 * KIB, "v_scales2": 18 * KIB + 512,
     "v_g0": 28 * KIB, "y_planes": 28 * KIB,
     "rs_sb1": 30 * KIB, "v_codes3": 30 * KIB,
 }

@@ -22,16 +22,16 @@ PACK = 4
 RUN = 4
 HALF = NQ // 2
 SCALE_ROWS = 16
+SCALE_BASE = 48
 BANK = 2048
 KIB = 1024
+VECTOR_COLUMNS = 18
 
 PLAN = {
-    "ks_pool": 0, "q_codes0": 0,
-    "kw_pool": 2 * KIB, "q_scales1": 2 * KIB,
-    "v_pool2": 10 * KIB, "v_codes1": 10 * KIB, "v_scales1": 11 * KIB, "y_codes1": 12 * KIB, "y_scales1": 13 * KIB,
-    "rs_sb0": 18 * KIB, "v_codes2": 18 * KIB, "v_scales2": 18 * KIB + 512,
-    "v_g0": 28 * KIB, "y_planes": 28 * KIB,
-    "rs_sb1": 30 * KIB, "v_codes3": 30 * KIB,
+    "v_pool0": 0, "ks_pool": 7 * KIB, "us_sb": 8 * KIB, "v_pool1": 8 * KIB + 64,
+    "v_pool2": 17 * KIB, "q_raw": 21 * KIB, "v_pool3": 25 * KIB, "v_bf1": 17 * KIB,
+    "kw_pool": 33 * KIB, "rs_early0": 33 * KIB, "rs_early1": 36 * KIB, "rs_last": 39 * KIB,
+    "v_codes3": 33 * KIB,
 }
 
 
@@ -71,88 +71,101 @@ def tile_attend_mlpb_gelu_topk_kernel(tc, qT, k_words, k_scales, vT, nb, rs, us,
             nc.tensor.matmul_mx(out=o, lhsT=stationary[0].bitcast(FP8X4), lhsT_scale=stationary[1],
                                 rhs=moving[0].bitcast(FP8X4), rhs_scale=moving[1], start=True, stop=True)
 
-        halves = [slice(h * HALF, (h + 1) * HALF) for h in range(2)]
-        blocks = [slice(b * P, (b + 1) * P) for b in range(4)]
-        pairs = [slice(2 * h, 2 * h + 2) for h in range(2)]
-
-        offsets = keep.tile([P, N // 16], U16, name="offsets")
-        nc.sync.dma_start(offsets[:], offs)
-        ks_pool = sbuf("ks_pool", [P, T], U8)
-        nc.gpsimd.memset(ks_pool[:].bitcast(I32), 0)
-
-        warm_in = sbuf("warm_in", [P, 1], F32)
-        nc.vector.memset(warm_in[:], 0.0)
-        nb_pool = sbuf("nb_pool", [P, T], F32)
-        nc.scalar.dma_start(nb_pool[P - 1:P, :], nb[0:1, :])
-        nc.vector.memset(nb_pool[:P - 1, :], 0.0)
-        warm = sbuf("warm", [P, 1], F32)
-        nc.scalar.activation(warm[:], warm_in[:], ACT.Gelu_apprx_tanh)
-        ident = sbuf("ident", [P, P], F32)
-        make_identity(nc, ident[:])
-
-        q_rows = qT[0].rearrange("(p j) w -> p j w", j=PACK)
-        rs_rows = rs[0].rearrange("(c p) e -> p c e", p=P)
-        out_rows = out[0].rearrange("(c p) e -> p c e", p=P)
-
         def load(name, source, dtype=F32):
             tile = sbuf(name, list(source.shape), dtype)
             nc.sync.dma_start(tile[:], source)
             return tile
 
-        q_raw = [load("q_raw0", q_rows[:, :, halves[0]])]
-        for r in range(4):
-            nc.sync.dma_start(ks_pool[r:P:32, :].bitcast(I32), k_scales[0, r:SCALE_ROWS:4, :].bitcast(I32))
+        halves = [slice(h * HALF, (h + 1) * HALF) for h in range(2)]
+        blocks = [slice(b * P, (b + 1) * P) for b in range(4)]
+        early = slice(0, 3 * P)
+
+        offsets = keep.tile([P, N // 16], U16, name="offsets")
+        nc.sync.dma_start(offsets[:], offs)
+        ks_pool = sbuf("ks_pool", [P, T], U8)
+        nc.sync.dma_start(ks_pool[SCALE_BASE:SCALE_BASE + SCALE_ROWS, :].bitcast(I32), k_scales[0].bitcast(I32))
+        nc.vector.memset(ks_pool[:SCALE_BASE, :].bitcast(I32), 0)
+        nc.vector.memset(ks_pool[SCALE_BASE + SCALE_ROWS:, :].bitcast(I32), 0)
+        nb_pool = sbuf("nb_pool", [P, T], F32)
+        nc.sync.dma_start(nb_pool[P - 1:P, :], nb[0:1, :])
+        nc.gpsimd.memset(nb_pool[:P - 1, T // 2:], 0.0)
+        nc.vector.memset(nb_pool[:P - 1, :T // 2], 0.0)
+        warm_in = sbuf("warm_in", [P, 1], F32)
+        nc.gpsimd.memset(warm_in[:], 0.0)
+        warm = sbuf("warm", [P, 1], F32)
+        nc.scalar.activation(warm[:], warm_in[:], ACT.Gelu_apprx_tanh)
+        ks_plane = sbuf("ks_plane", [P, PACK, P], U8)
+        nc.vector.memset(ks_plane[:].rearrange("p t m -> p (t m)").bitcast(I32), 0)
+        ident = sbuf("ident", [P, P], F32)
+        make_identity(nc, ident[:])
+
+        q_raw = load("q_raw", qT[0].rearrange("(p j) w -> p j w", j=PACK))
         kw_pool = load("kw_pool", k_words[0].rearrange("p n t -> p (n t)").bitcast(I32), I32)
-        q_raw.append(load("q_raw1", q_rows[:, :, halves[1]]))
+
+        ks_g = sbuf("ks_g", [P, PACK, P], U8)
+        nc.vector.tensor_copy(ks_g[:].rearrange("p t m -> p m t"), ks_pool[:].indirect(offsets[:]))
+        for r in range(4):
+            nc.sync.dma_start(
+                ks_plane[r:P:32].rearrange("p t m -> p (t m)").bitcast(I32),
+                ks_g[SCALE_BASE + r:SCALE_BASE + SCALE_ROWS:4].rearrange("p t m -> p (t m)").bitcast(I32))
         v_pool = [load("v_pool0", vT[blocks[0], :])]
         us_sb = sbuf("us_sb", [P, 1, PACK, 1], F32)
         nc.sync.dma_start(us_sb[:, 0, :, 0], us[0].rearrange("(p t) o -> p (t o)", t=PACK))
-        v_pool.extend(load("v_pool%d" % b, vT[blocks[b], :]) for b in range(1, 4))
-        pieces = [(pairs[0], blocks[0]), (pairs[1], halves[0]), (pairs[0], blocks[1]), (slice(0, 4), halves[1])]
-        rs_sb = [load("rs_sb%d" % i, rs_rows[:, rows, features]) for i, (rows, features) in enumerate(pieces)]
+        v_pool.append(load("v_pool1", vT[blocks[1], :]))
 
         nb_list = sbuf("nb_list", [P, N], F32)
-        nc.vector.tensor_copy(nb_list[:], nb_pool[:].indirect(offsets[:]))
-        ks_list = sbuf("ks_list", [P, N], U8)
-        nc.vector.tensor_copy(ks_list[:], ks_pool[:].indirect(offsets[:]))
+        nc.scalar.activation(nb_list[:], nb_pool[:].indirect(offsets[:]), ACT.Copy)
+        nb_turn = bank("nb_turn", 7, [P, PACK, P])
+        for t in range(PACK):
+            nc.tensor.transpose(nb_turn[:, t, :], nb_list[:, t:N:PACK], ident[:])
 
-        def cast_q(h):
-            q_bf = sbuf("q_bf%d" % h, [P, HALF, PACK], BF16)
-            nc.scalar.copy(packed(q_bf[:]), planes(q_raw[h][:]))
-            return q_bf
+        q_bf = [sbuf("q_bf%d" % h, [P, HALF, PACK], BF16) for h in range(2)]
+        nc.vector.tensor_copy(packed(q_bf[0][:]), planes(q_raw[:, :, halves[0]]))
+        nc.scalar.copy(packed(q_bf[1][:]), planes(q_raw[:, :, halves[1]]))
+        bias = sbuf("bias", [P, PACK], F32)
+        nc.scalar.copy(bias[:], nb_turn[:, :, P - 1])
+        v_pool.extend(load("v_pool%d" % b, vT[blocks[b], :]) for b in range(2, 4))
 
         def quantize_half(name, words):
             return quantize(name, HALF, words[:].rearrange("p w j -> p (w j)"))
 
-        q_bf0 = cast_q(0)
-        nb_turn = bank("nb_turn", 7, [P, PACK, P])
-        for t in range(PACK):
-            nc.tensor.transpose(nb_turn[:, t, :], nb_list[:, t:N:PACK], ident[:])
-        bias = sbuf("bias", [P, PACK], F32)
-        nc.scalar.copy(bias[:], nb_turn[:, :, P - 1])
-
-        q_q0 = quantize_half("q_%s0", q_bf0)
-        ks_g = sbuf("ks_g", [P, PACK, P], U8)
-        nc.vector.tensor_copy(ks_g[:], ks_list[:].rearrange("p (m t) -> p t m", t=PACK))
+        q_q = [quantize_half("q_%s" + str(h), q_bf[h]) for h in range(2)]
         kw_g = sbuf("kw_g", [P, PACK, P], U32)
         nc.vector.tensor_copy(kw_g[:].rearrange("p t m -> p m t"), kw_pool[:].bitcast(U32).indirect(offsets[:]))
 
-        def first_product(h, queries):
+        rs_rows = rs[0].rearrange("(c p) e -> p c e", p=P)
+        rs_early = [load("rs_early%d" % h, rs_rows[:, 2 * h:2 * h + 2, early]) for h in range(2)]
+        rs_last = load("rs_last", rs_rows[:, :, blocks[3]])
+
+        def first_product(h):
             a = [bank("a%d_%d" % (h, t), PACK * h + t, [P, HALF]) for t in range(PACK)]
             for t in range(PACK):
-                product(a[t][:], (kw_g[:, t, :], ks_g[:, t, :]), queries)
+                product(a[t][:], (kw_g[:, t, :], ks_plane[:, t, :]), q_q[h])
             g = sbuf("g%d" % h, [P, PACK, HALF], F32)
             for t in range(PACK):
                 nc.scalar.activation(g[:, t, :], a[t][:], ACT.Gelu_apprx_tanh, bias=bias[:, t:t + 1])
             return g
 
-        def gather_v(b):
+        def scale_half(h, g):
+            y_bf = sbuf("y_bf%d" % h, [P, HALF, PACK], BF16)
+            nc.vector.tensor_tensor(packed(y_bf[:]), planes(g[:]),
+                                    us_sb[:].to_broadcast([P, HALF // RUN, PACK, RUN]), ALU.mult)
+            return y_bf
+
+        def gather_v(b, vector_columns):
             v_g = sbuf("v_g%d" % b, [P, N], BF16)
-            nc.vector.tensor_copy(v_g[:].rearrange("p (u m s) -> p m u s", u=2, s=2), v_pool[b][:].indirect(offsets[:]))
+            cut = 16 * vector_columns
+            if vector_columns:
+                nc.vector.tensor_copy(v_g[:, :cut], v_pool[b][:].indirect(offsets[:, :vector_columns]))
+            if cut < N:
+                nc.scalar.activation(v_g[:, cut:], v_pool[b][:].indirect(offsets[:, vector_columns:]), ACT.Copy)
+            return v_g
+
+        def turn_v(b, v_g):
             words = v_g[:].bitcast(F32)
             turn = bank("v_turn%d" % b, b, [P, 2, P])
             for u in range(2):
-                nc.tensor.transpose(turn[:, u, :], words[:, blocks[u]], ident[:])
+                nc.tensor.transpose(turn[:, u, :], words[:, u:2 * P:2], ident[:])
             v_bf = sbuf("v_bf%d" % b, [P, P * PACK], BF16)
             nc.scalar.copy(v_bf[:].bitcast(F32).rearrange("p (e u) -> p e u", u=2), turn[:].rearrange("p u e -> p e u"))
             return v_bf
@@ -160,66 +173,50 @@ def tile_attend_mlpb_gelu_topk_kernel(tc, qT, k_words, k_scales, vT, nb, rs, us,
         def quantize_v(b, v_bf):
             return quantize("v_%s" + str(b), P, v_bf[:])
 
-        def finish(name, o, residual, rows, features):
-            res = sbuf(name, list(o.shape), F32)
-            nc.vector.tensor_tensor(res[:], o, residual, ALU.add)
-            nc.sync.dma_start(out_rows[:, rows, features], res[:])
+        g = [first_product(h) for h in range(2)]
+        v_g0 = gather_v(0, N // 16)
+        y_bf0 = scale_half(0, g[0])
+        v_bf0 = turn_v(0, v_g0)
+        v_g1 = gather_v(1, 0)
+        y_bf1 = scale_half(1, g[1])
+        y_q = [quantize_half("y_%s0", y_bf0)]
+        v_q = [quantize_v(0, v_bf0)]
+        y_q.append(quantize_half("y_%s1", y_bf1))
+        y_q = [columns(half, blocks[c]) for half in y_q for c in range(2)]
+        o_early = [bank("o_early%d" % c, 4 + c, [P, 3 * P]) for c in range(4)]
 
-        q_bf1 = cast_q(1)
-        g0 = first_product(0, q_q0)
-        g1 = first_product(1, quantize_half("q_%s1", q_bf1))
+        def second_product(b):
+            for c in range(4):
+                product(o_early[c][:, blocks[b]], y_q[c], v_q[b])
 
-        v_bf0 = gather_v(0)
-        y_bf0 = sbuf("y_bf0", [P, HALF, PACK], BF16)
-        nc.vector.tensor_tensor(packed(y_bf0[:]), planes(g0[:]),
-                                us_sb[:].to_broadcast([P, HALF // RUN, PACK, RUN]), ALU.mult)
-        v_q0 = quantize_v(0, v_bf0)
-        y_q0 = quantize_half("y_%s0", y_bf0)
-        y_planes = sbuf("y_planes", [P, PACK, HALF], BF16)
-        for t in range(PACK):
-            nc.scalar.activation(y_planes[:, t, :], g1[:, t, :], ACT.Copy, scale=us_sb[:, 0, t, :])
-        y_bf1 = sbuf("y_bf1", [P, HALF, PACK], BF16)
-        nc.scalar.copy(packed(y_bf1[:]), planes(y_planes[:]))
-        v_bf1 = gather_v(1)
+        v_bf1 = turn_v(1, v_g1)
+        second_product(0)
+        v_q.append(quantize_v(1, v_bf1))
+        v_g2 = gather_v(2, VECTOR_COLUMNS)
+        v_bf2 = turn_v(2, v_g2)
+        second_product(1)
+        v_q.append(quantize_v(2, v_bf2))
+        second_product(2)
+        v_g3 = gather_v(3, 16)
+        v_bf3 = turn_v(3, v_g3)
 
-        o00 = bank("o00", 4, [P, 2, P])
-        for c in range(2):
-            product(o00[:, c, :], columns(y_q0, blocks[c]), v_q0)
-        o_sb = sbuf("o_sb", [P, 2, P], F32)
-        nc.scalar.copy(o_sb[:], o00[:])
-        res0 = sbuf("res0", [P, 2, P], F32)
-        nc.gpsimd.tensor_tensor(res0[:], o_sb[:], rs_sb[0][:], ALU.add)
-        nc.sync.dma_start(out_rows[:, pairs[0], blocks[0]], res0[:])
+        def finish_early(c):
+            res = sbuf("res_early%d" % c, [P, 3 * P], F32)
+            nc.vector.tensor_tensor(res[:], o_early[c][:], rs_early[c // 2][:, c % 2, :], ALU.add)
+            nc.sync.dma_start(out[0, blocks[c], early], res[:])
 
-        idle = bank("idle", 4, [P, N])
-        for c in range(2):
-            product(idle[:], columns(q_q0, blocks[c]),
-                    (kw_g[:].rearrange("p t m -> p (t m)"), ks_g[:].rearrange("p t m -> p (t m)")))
-
-        v_bf2 = gather_v(2)
-        y_q1 = quantize_half("y_%s1", y_bf1)
-        y_q = [columns(half, blocks[c]) for half in (y_q0, y_q1) for c in range(2)]
-        v_q1 = quantize_v(1, v_bf1)
-        o01 = bank("o01", 5, [P, 2, P])
-        o23 = bank("o23", 6, [P, 2, HALF])
-        for b, v_q in enumerate((v_q0, v_q1)):
-            for c in range(2):
-                product(o23[:, c, blocks[b]], y_q[2 + c], v_q)
-        for c in range(2):
-            product(o01[:, c, :], y_q[c], v_q1)
-        v_bf3 = gather_v(3)
-
-        v_q2 = quantize_v(2, v_bf2)
-        o2 = bank("o2", 7, [P, 4, P])
+        finish_early(0)
+        finish_early(1)
+        finish_early(2)
+        v_q.append(quantize_v(3, v_bf3))
+        o_last = [bank("o_last%d" % c, c, [P, P]) for c in range(4)]
         for c in range(4):
-            product(o2[:, c, :], y_q[c], v_q2)
-        finish("res23", o23[:], rs_sb[1][:], pairs[1], halves[0])
-        finish("res01", o01[:], rs_sb[2][:], pairs[0], blocks[1])
-
-        v_q3 = quantize_v(3, v_bf3)
-        o3 = [bank("o3_%d" % h, h, [P, 2, P]) for h in range(2)]
-        for c in range(4):
-            product(o3[c // 2][:, c % 2, :], y_q[c], v_q3)
-        finish("res2", o2[:], rs_sb[3][:, :, blocks[0]], slice(0, 4), blocks[2])
+            product(o_last[c][:], y_q[c], v_q[3])
+        finish_early(3)
+        out_rows = out[0].rearrange("(c p) e -> p c e", p=P)
         for h in range(2):
-            finish("res3_%d" % h, o3[h][:], rs_sb[3][:, pairs[h], blocks[1]], pairs[h], blocks[3])
+            res = sbuf("res_last%d" % h, [P, 2, P], F32)
+            for i in range(2):
+                c = 2 * h + i
+                nc.vector.tensor_tensor(res[:, i, :], o_last[c][:], rs_last[:, c, :], ALU.add)
+            nc.sync.dma_start(out_rows[:, 2 * h:2 * h + 2, blocks[3]], res[:])

@@ -28,10 +28,8 @@ KIB = 1024
 VECTOR_COLUMNS = 18
 
 PLAN = {
-    "v_pool0": 0, "ks_pool": 7 * KIB, "us_sb": 8 * KIB, "v_pool1": 8 * KIB + 64,
-    "v_pool2": 17 * KIB, "q_raw": 21 * KIB, "v_pool3": 25 * KIB, "v_bf1": 17 * KIB,
-    "kw_pool": 33 * KIB, "rs_early0": 33 * KIB, "rs_early1": 36 * KIB, "rs_last": 39 * KIB,
-    "v_codes3": 33 * KIB,
+    "v_pool2": 0, "v_bf1": 0, "o_sb": 2 * KIB,
+    "rs_sb0": 10 * KIB, "v_codes2": 10 * KIB, "rs_sb1": 8 * KIB, "v_codes3": 8 * KIB,
 }
 
 
@@ -83,35 +81,32 @@ def tile_attend_mlpb_gelu_topk_kernel(tc, qT, k_words, k_scales, vT, nb, rs, us,
         offsets = keep.tile([P, N // 16], U16, name="offsets")
         nc.sync.dma_start(offsets[:], offs)
         ks_pool = sbuf("ks_pool", [P, T], U8)
-        nc.sync.dma_start(ks_pool[SCALE_BASE:SCALE_BASE + SCALE_ROWS, :].bitcast(I32), k_scales[0].bitcast(I32))
-        nc.vector.memset(ks_pool[:SCALE_BASE, :].bitcast(I32), 0)
-        nc.vector.memset(ks_pool[SCALE_BASE + SCALE_ROWS:, :].bitcast(I32), 0)
+        nc.gpsimd.memset(ks_pool[:].bitcast(I32), 0)
         nb_pool = sbuf("nb_pool", [P, T], F32)
-        nc.sync.dma_start(nb_pool[P - 1:P, :], nb[0:1, :])
-        nc.gpsimd.memset(nb_pool[:P - 1, T // 2:], 0.0)
-        nc.vector.memset(nb_pool[:P - 1, :T // 2], 0.0)
+        nc.scalar.dma_start(nb_pool[P - 1:P, :], nb[0:1, :])
         warm_in = sbuf("warm_in", [P, 1], F32)
-        nc.gpsimd.memset(warm_in[:], 0.0)
+        nc.vector.memset(warm_in[:], 0.0)
         warm = sbuf("warm", [P, 1], F32)
         nc.scalar.activation(warm[:], warm_in[:], ACT.Gelu_apprx_tanh)
-        ks_plane = sbuf("ks_plane", [P, PACK, P], U8)
-        nc.vector.memset(ks_plane[:].rearrange("p t m -> p (t m)").bitcast(I32), 0)
+        nc.vector.memset(nb_pool[:P - 1, :], 0.0)
         ident = sbuf("ident", [P, P], F32)
         make_identity(nc, ident[:])
 
-        q_raw = load("q_raw", qT[0].rearrange("(p j) w -> p j w", j=PACK))
-        kw_pool = load("kw_pool", k_words[0].rearrange("p n t -> p (n t)").bitcast(I32), I32)
-
-        ks_g = sbuf("ks_g", [P, PACK, P], U8)
-        nc.vector.tensor_copy(ks_g[:].rearrange("p t m -> p m t"), ks_pool[:].indirect(offsets[:]))
+        q_rows = qT[0].rearrange("(p j) w -> p j w", j=PACK)
+        q_raw = [load("q_raw0", q_rows[:, :, halves[0]])]
         for r in range(4):
-            nc.sync.dma_start(
-                ks_plane[r:P:32].rearrange("p t m -> p (t m)").bitcast(I32),
-                ks_g[SCALE_BASE + r:SCALE_BASE + SCALE_ROWS:4].rearrange("p t m -> p (t m)").bitcast(I32))
+            nc.sync.dma_start(ks_pool[r:P:32, :].bitcast(I32), k_scales[0, r:SCALE_ROWS:4, :].bitcast(I32))
+        kw_pool = load("kw_pool", k_words[0].rearrange("p n t -> p (n t)").bitcast(I32), I32)
+        q_raw.append(load("q_raw1", q_rows[:, :, halves[1]]))
         v_pool = [load("v_pool0", vT[blocks[0], :])]
         us_sb = sbuf("us_sb", [P, 1, PACK, 1], F32)
         nc.sync.dma_start(us_sb[:, 0, :, 0], us[0].rearrange("(p t) o -> p (t o)", t=PACK))
-        v_pool.append(load("v_pool1", vT[blocks[1], :]))
+        v_pool.extend(load("v_pool%d" % b, vT[blocks[b], :]) for b in range(1, 4))
+        rs_rows = rs[0].rearrange("(c p) e -> p c e", p=P)
+        out_rows = out[0].rearrange("(c p) e -> p c e", p=P)
+        pairs = [slice(2 * h, 2 * h + 2) for h in range(2)]
+        pieces = [(pairs[0], blocks[0]), (pairs[1], halves[0]), (pairs[0], blocks[1]), (slice(0, 4), halves[1])]
+        rs_sb = [load("rs_sb%d" % i, rs_rows[:, rows, features]) for i, (rows, features) in enumerate(pieces)]
 
         nb_list = sbuf("nb_list", [P, N], F32)
         nc.scalar.activation(nb_list[:], nb_pool[:].indirect(offsets[:]), ACT.Copy)
@@ -119,23 +114,24 @@ def tile_attend_mlpb_gelu_topk_kernel(tc, qT, k_words, k_scales, vT, nb, rs, us,
         for t in range(PACK):
             nc.tensor.transpose(nb_turn[:, t, :], nb_list[:, t:N:PACK], ident[:])
 
-        q_bf = [sbuf("q_bf%d" % h, [P, HALF, PACK], BF16) for h in range(2)]
-        nc.vector.tensor_copy(packed(q_bf[0][:]), planes(q_raw[:, :, halves[0]]))
-        nc.scalar.copy(packed(q_bf[1][:]), planes(q_raw[:, :, halves[1]]))
         bias = sbuf("bias", [P, PACK], F32)
         nc.scalar.copy(bias[:], nb_turn[:, :, P - 1])
-        v_pool.extend(load("v_pool%d" % b, vT[blocks[b], :]) for b in range(2, 4))
+
+        def cast_q(h):
+            q_bf = sbuf("q_bf%d" % h, [P, HALF, PACK], BF16)
+            nc.vector.tensor_copy(packed(q_bf[:]), planes(q_raw[h][:]))
+            return q_bf
 
         def quantize_half(name, words):
             return quantize(name, HALF, words[:].rearrange("p w j -> p (w j)"))
 
-        q_q = [quantize_half("q_%s" + str(h), q_bf[h]) for h in range(2)]
+        q_bf0 = cast_q(0)
+        ks_plane = sbuf("ks_plane", [P, PACK, P], U8)
+        nc.vector.tensor_copy(ks_plane[:].rearrange("p t m -> p m t"), ks_pool[:].indirect(offsets[:]))
+        q_q = [quantize_half("q_%s0", q_bf0)]
         kw_g = sbuf("kw_g", [P, PACK, P], U32)
         nc.vector.tensor_copy(kw_g[:].rearrange("p t m -> p m t"), kw_pool[:].bitcast(U32).indirect(offsets[:]))
-
-        rs_rows = rs[0].rearrange("(c p) e -> p c e", p=P)
-        rs_early = [load("rs_early%d" % h, rs_rows[:, 2 * h:2 * h + 2, early]) for h in range(2)]
-        rs_last = load("rs_last", rs_rows[:, :, blocks[3]])
+        q_q.append(quantize_half("q_%s1", cast_q(1)))
 
         def first_product(h):
             a = [bank("a%d_%d" % (h, t), PACK * h + t, [P, HALF]) for t in range(PACK)]
@@ -183,40 +179,47 @@ def tile_attend_mlpb_gelu_topk_kernel(tc, qT, k_words, k_scales, vT, nb, rs, us,
         v_q = [quantize_v(0, v_bf0)]
         y_q.append(quantize_half("y_%s1", y_bf1))
         y_q = [columns(half, blocks[c]) for half in y_q for c in range(2)]
-        o_early = [bank("o_early%d" % c, 4 + c, [P, 3 * P]) for c in range(4)]
 
-        def second_product(b):
-            for c in range(4):
-                product(o_early[c][:, blocks[b]], y_q[c], v_q[b])
+        def finish(name, o, residual, rows, features):
+            res = sbuf(name, list(o.shape), F32)
+            nc.vector.tensor_tensor(res[:], o, residual, ALU.add)
+            nc.sync.dma_start(out_rows[:, rows, features], res[:])
 
-        v_bf1 = turn_v(1, v_g1)
-        second_product(0)
-        v_q.append(quantize_v(1, v_bf1))
+        o00 = bank("o00", 4, [P, 2, P])
+        o01 = bank("o01", 5, [P, 2, P])
+        o23 = bank("o23", 6, [P, 2, HALF])
+        for c in range(2):
+            product(o00[:, c, :], y_q[c], v_q[0])
+        for c in range(2):
+            product(o23[:, c, blocks[0]], y_q[2 + c], v_q[0])
         v_g2 = gather_v(2, VECTOR_COLUMNS)
+        v_bf1 = turn_v(1, v_g1)
+        o_sb = sbuf("o_sb", [P, 2, P], F32)
+        nc.scalar.copy(o_sb[:], o00[:])
+        res0 = sbuf("res0", [P, 2, P], F32)
+        nc.gpsimd.tensor_tensor(res0[:], o_sb[:], rs_sb[0][:], ALU.add)
+        nc.sync.dma_start(out_rows[:, pairs[0], blocks[0]], res0[:])
         v_bf2 = turn_v(2, v_g2)
-        second_product(1)
-        v_q.append(quantize_v(2, v_bf2))
-        second_product(2)
-        v_g3 = gather_v(3, 16)
+        v_q.append(quantize_v(1, v_bf1))
+        for c in range(2):
+            product(o23[:, c, blocks[1]], y_q[2 + c], v_q[1])
+        for c in range(2):
+            product(o01[:, c, :], y_q[c], v_q[1])
+        v_g3 = gather_v(3, VECTOR_COLUMNS)
         v_bf3 = turn_v(3, v_g3)
-
-        def finish_early(c):
-            res = sbuf("res_early%d" % c, [P, 3 * P], F32)
-            nc.vector.tensor_tensor(res[:], o_early[c][:], rs_early[c // 2][:, c % 2, :], ALU.add)
-            nc.sync.dma_start(out[0, blocks[c], early], res[:])
-
-        finish_early(0)
-        finish_early(1)
-        finish_early(2)
-        v_q.append(quantize_v(3, v_bf3))
-        o_last = [bank("o_last%d" % c, c, [P, P]) for c in range(4)]
+        finish("res23", o23[:], rs_sb[1][:], pairs[1], halves[0])
+        v_q.append(quantize_v(2, v_bf2))
+        o2 = bank("o2", 7, [P, 4, P])
         for c in range(4):
-            product(o_last[c][:], y_q[c], v_q[3])
-        finish_early(3)
-        out_rows = out[0].rearrange("(c p) e -> p c e", p=P)
+            product(o2[:, c, :], y_q[c], v_q[2])
+        finish("res01", o01[:], rs_sb[2][:], pairs[0], blocks[1])
+        v_q.append(quantize_v(3, v_bf3))
+        finish("res2", o2[:], rs_sb[3][:, :, blocks[0]], slice(0, 4), blocks[2])
+        o3 = [bank("o3_%d" % c, c, [P, P]) for c in range(4)]
+        for c in range(4):
+            product(o3[c][:], y_q[c], v_q[3])
         for h in range(2):
-            res = sbuf("res_last%d" % h, [P, 2, P], F32)
+            res = sbuf("res3_%d" % h, [P, 2, P], F32)
             for i in range(2):
-                c = 2 * h + i
-                nc.vector.tensor_tensor(res[:, i, :], o_last[c][:], rs_last[:, c, :], ALU.add)
-            nc.sync.dma_start(out_rows[:, 2 * h:2 * h + 2, blocks[3]], res[:])
+                nc.vector.tensor_tensor(res[:, i, :], o3[2 * h + i][:], rs_sb[3][:, 2 * h + i, blocks[1]], ALU.add)
+            nc.sync.dma_start(out_rows[:, pairs[h], blocks[3]], res[:])

@@ -29,7 +29,7 @@ VECTOR_COLUMNS = 18
 
 PLAN = {
     "v_pool2": 0, "v_bf1": 0, "o_sb": 2 * KIB,
-    "rs_sb0": 10 * KIB, "v_codes2": 10 * KIB, "rs_sb1": 8 * KIB, "v_codes3": 8 * KIB,
+    "rs_sb1": 8 * KIB, "v_bf3": 8 * KIB,
 }
 
 
@@ -105,7 +105,7 @@ def tile_attend_mlpb_gelu_topk_kernel(tc, qT, k_words, k_scales, vT, nb, rs, us,
         rs_rows = rs[0].rearrange("(c p) e -> p c e", p=P)
         out_rows = out[0].rearrange("(c p) e -> p c e", p=P)
         pairs = [slice(2 * h, 2 * h + 2) for h in range(2)]
-        pieces = [(pairs[0], blocks[0]), (pairs[1], halves[0]), (pairs[0], blocks[1]), (slice(0, 4), halves[1])]
+        pieces = [(pairs[0], blocks[0]), (pairs[1], halves[0]), (pairs[0], slice(P, DV)), (pairs[1], halves[1])]
         rs_sb = [load("rs_sb%d" % i, rs_rows[:, rows, features]) for i, (rows, features) in enumerate(pieces)]
 
         nb_list = sbuf("nb_list", [P, N], F32)
@@ -186,7 +186,7 @@ def tile_attend_mlpb_gelu_topk_kernel(tc, qT, k_words, k_scales, vT, nb, rs, us,
             nc.sync.dma_start(out_rows[:, rows, features], res[:])
 
         o00 = bank("o00", 4, [P, 2, P])
-        o01 = bank("o01", 5, [P, 2, P])
+        o01 = bank("o01", 5, [P, 2, HALF])
         o23 = bank("o23", 6, [P, 2, HALF])
         for c in range(2):
             product(o00[:, c, :], y_q[c], v_q[0])
@@ -204,22 +204,25 @@ def tile_attend_mlpb_gelu_topk_kernel(tc, qT, k_words, k_scales, vT, nb, rs, us,
         for c in range(2):
             product(o23[:, c, blocks[1]], y_q[2 + c], v_q[1])
         for c in range(2):
-            product(o01[:, c, :], y_q[c], v_q[1])
-        v_g3 = gather_v(3, VECTOR_COLUMNS)
+            product(o01[:, c, blocks[0]], y_q[c], v_q[1])
+        v_q.append(quantize_v(2, v_bf2))
+        for c in range(2):
+            product(o01[:, c, blocks[1]], y_q[c], v_q[2])
+        o2 = bank("o2", 7, [P, 2, P])
+        for c in range(2):
+            product(o2[:, c, :], y_q[2 + c], v_q[2])
+        v_g3 = gather_v(3, 16)
         v_bf3 = turn_v(3, v_g3)
         finish("res23", o23[:], rs_sb[1][:], pairs[1], halves[0])
-        v_q.append(quantize_v(2, v_bf2))
-        o2 = bank("o2", 7, [P, 4, P])
-        for c in range(4):
-            product(o2[:, c, :], y_q[c], v_q[2])
-        finish("res01", o01[:], rs_sb[2][:], pairs[0], blocks[1])
+        finish("res01", o01[:], rs_sb[2][:, :, :HALF], pairs[0], slice(P, 3 * P))
         v_q.append(quantize_v(3, v_bf3))
-        finish("res2", o2[:], rs_sb[3][:, :, blocks[0]], slice(0, 4), blocks[2])
-        o3 = [bank("o3_%d" % c, c, [P, P]) for c in range(4)]
+        finish("res2", o2[:], rs_sb[3][:, :, blocks[0]], pairs[1], blocks[2])
+        o3 = [bank("o3_%d" % c, number, [P, P]) for c, number in enumerate((0, 1, 2, 3))]
         for c in range(4):
             product(o3[c][:], y_q[c], v_q[3])
+        last = [rs_sb[2][:, :, blocks[2]], rs_sb[3][:, :, blocks[1]]]
         for h in range(2):
             res = sbuf("res3_%d" % h, [P, 2, P], F32)
             for i in range(2):
-                nc.vector.tensor_tensor(res[:, i, :], o3[2 * h + i][:], rs_sb[3][:, 2 * h + i, blocks[1]], ALU.add)
+                nc.vector.tensor_tensor(res[:, i, :], o3[2 * h + i][:], last[h][:, i, :], ALU.add)
             nc.sync.dma_start(out_rows[:, pairs[h], blocks[3]], res[:])

@@ -28,8 +28,10 @@ KIB = 1024
 VECTOR_COLUMNS = 18
 
 PLAN = {
-    "v_pool2": 0, "v_bf1": 0, "o_sb": 2 * KIB,
-    "rs_sb1": 8 * KIB, "v_bf3": 8 * KIB,
+    "v_pool0": 0, "ks_pool": 7 * KIB, "us_sb": 8 * KIB, "v_pool1": 8 * KIB + 64,
+    "v_pool2": 17 * KIB, "q_raw": 21 * KIB, "v_pool3": 25 * KIB, "v_bf1": 17 * KIB, "o_sb": 19 * KIB,
+    "kw_pool": 33 * KIB, "rs_sb0": 33 * KIB, "rs_sb1": 34 * KIB, "rs_sb2": 36 * KIB, "rs_sb3": 39 * KIB,
+    "v_bf3": 34 * KIB,
 }
 
 
@@ -76,37 +78,39 @@ def tile_attend_mlpb_gelu_topk_kernel(tc, qT, k_words, k_scales, vT, nb, rs, us,
 
         halves = [slice(h * HALF, (h + 1) * HALF) for h in range(2)]
         blocks = [slice(b * P, (b + 1) * P) for b in range(4)]
-        early = slice(0, 3 * P)
 
         offsets = keep.tile([P, N // 16], U16, name="offsets")
         nc.sync.dma_start(offsets[:], offs)
         ks_pool = sbuf("ks_pool", [P, T], U8)
-        nc.gpsimd.memset(ks_pool[:].bitcast(I32), 0)
+        nc.sync.dma_start(ks_pool[SCALE_BASE:SCALE_BASE + SCALE_ROWS, :].bitcast(I32), k_scales[0].bitcast(I32))
+        nc.vector.memset(ks_pool[:SCALE_BASE, :].bitcast(I32), 0)
+        nc.vector.memset(ks_pool[SCALE_BASE + SCALE_ROWS:, :].bitcast(I32), 0)
         nb_pool = sbuf("nb_pool", [P, T], F32)
-        nc.scalar.dma_start(nb_pool[P - 1:P, :], nb[0:1, :])
+        nc.sync.dma_start(nb_pool[P - 1:P, :], nb[0:1, :])
+        nc.gpsimd.memset(nb_pool[:P - 1, T // 2:], 0.0)
+        nc.vector.memset(nb_pool[:P - 1, :T // 2], 0.0)
         warm_in = sbuf("warm_in", [P, 1], F32)
-        nc.vector.memset(warm_in[:], 0.0)
+        nc.gpsimd.memset(warm_in[:], 0.0)
         warm = sbuf("warm", [P, 1], F32)
         nc.scalar.activation(warm[:], warm_in[:], ACT.Gelu_apprx_tanh)
-        nc.vector.memset(nb_pool[:P - 1, :], 0.0)
+        ks_plane = sbuf("ks_plane", [P, PACK, P], U8)
+        nc.vector.memset(ks_plane[:].rearrange("p t m -> p (t m)").bitcast(I32), 0)
         ident = sbuf("ident", [P, P], F32)
         make_identity(nc, ident[:])
 
-        q_rows = qT[0].rearrange("(p j) w -> p j w", j=PACK)
-        q_raw = [load("q_raw0", q_rows[:, :, halves[0]])]
-        for r in range(4):
-            nc.sync.dma_start(ks_pool[r:P:32, :].bitcast(I32), k_scales[0, r:SCALE_ROWS:4, :].bitcast(I32))
+        q_raw = load("q_raw", qT[0].rearrange("(p j) w -> p j w", j=PACK))
         kw_pool = load("kw_pool", k_words[0].rearrange("p n t -> p (n t)").bitcast(I32), I32)
-        q_raw.append(load("q_raw1", q_rows[:, :, halves[1]]))
+
+        ks_g = sbuf("ks_g", [P, PACK, P], U8)
+        nc.vector.tensor_copy(ks_g[:].rearrange("p t m -> p m t"), ks_pool[:].indirect(offsets[:]))
+        for r in range(4):
+            nc.sync.dma_start(
+                ks_plane[r:P:32].rearrange("p t m -> p (t m)").bitcast(I32),
+                ks_g[SCALE_BASE + r:SCALE_BASE + SCALE_ROWS:4].rearrange("p t m -> p (t m)").bitcast(I32))
         v_pool = [load("v_pool0", vT[blocks[0], :])]
         us_sb = sbuf("us_sb", [P, 1, PACK, 1], F32)
         nc.sync.dma_start(us_sb[:, 0, :, 0], us[0].rearrange("(p t) o -> p (t o)", t=PACK))
-        v_pool.extend(load("v_pool%d" % b, vT[blocks[b], :]) for b in range(1, 4))
-        rs_rows = rs[0].rearrange("(c p) e -> p c e", p=P)
-        out_rows = out[0].rearrange("(c p) e -> p c e", p=P)
-        pairs = [slice(2 * h, 2 * h + 2) for h in range(2)]
-        pieces = [(pairs[0], blocks[0]), (pairs[1], halves[0]), (pairs[0], slice(P, DV)), (pairs[1], halves[1])]
-        rs_sb = [load("rs_sb%d" % i, rs_rows[:, rows, features]) for i, (rows, features) in enumerate(pieces)]
+        v_pool.append(load("v_pool1", vT[blocks[1], :]))
 
         nb_list = sbuf("nb_list", [P, N], F32)
         nc.scalar.activation(nb_list[:], nb_pool[:].indirect(offsets[:]), ACT.Copy)
@@ -114,24 +118,25 @@ def tile_attend_mlpb_gelu_topk_kernel(tc, qT, k_words, k_scales, vT, nb, rs, us,
         for t in range(PACK):
             nc.tensor.transpose(nb_turn[:, t, :], nb_list[:, t:N:PACK], ident[:])
 
+        q_bf = [sbuf("q_bf%d" % h, [P, HALF, PACK], BF16) for h in range(2)]
+        nc.vector.tensor_copy(packed(q_bf[0][:]), planes(q_raw[:, :, halves[0]]))
+        nc.scalar.copy(packed(q_bf[1][:]), planes(q_raw[:, :, halves[1]]))
         bias = sbuf("bias", [P, PACK], F32)
         nc.scalar.copy(bias[:], nb_turn[:, :, P - 1])
-
-        def cast_q(h):
-            q_bf = sbuf("q_bf%d" % h, [P, HALF, PACK], BF16)
-            nc.vector.tensor_copy(packed(q_bf[:]), planes(q_raw[h][:]))
-            return q_bf
+        v_pool.extend(load("v_pool%d" % b, vT[blocks[b], :]) for b in range(2, 4))
 
         def quantize_half(name, words):
             return quantize(name, HALF, words[:].rearrange("p w j -> p (w j)"))
 
-        q_bf0 = cast_q(0)
-        ks_plane = sbuf("ks_plane", [P, PACK, P], U8)
-        nc.vector.tensor_copy(ks_plane[:].rearrange("p t m -> p m t"), ks_pool[:].indirect(offsets[:]))
-        q_q = [quantize_half("q_%s0", q_bf0)]
+        q_q = [quantize_half("q_%s" + str(h), q_bf[h]) for h in range(2)]
         kw_g = sbuf("kw_g", [P, PACK, P], U32)
         nc.vector.tensor_copy(kw_g[:].rearrange("p t m -> p m t"), kw_pool[:].bitcast(U32).indirect(offsets[:]))
-        q_q.append(quantize_half("q_%s1", cast_q(1)))
+
+        rs_rows = rs[0].rearrange("(c p) e -> p c e", p=P)
+        out_rows = out[0].rearrange("(c p) e -> p c e", p=P)
+        pairs = [slice(2 * h, 2 * h + 2) for h in range(2)]
+        pieces = [(pairs[0], blocks[0]), (pairs[1], halves[0]), (pairs[0], slice(P, DV)), (pairs[1], halves[1])]
+        rs_sb = [load("rs_sb%d" % i, rs_rows[:, rows, features]) for i, (rows, features) in enumerate(pieces)]
 
         def first_product(h):
             a = [bank("a%d_%d" % (h, t), PACK * h + t, [P, HALF]) for t in range(PACK)]

@@ -28,8 +28,8 @@ KIB = 1024
 VECTOR_COLUMNS = 18
 
 PLAN = {
-    "v_pool0": 0, "ks_pool": 7 * KIB, "us_sb": 8 * KIB, "v_pool1": 8 * KIB + 64,
-    "v_pool2": 17 * KIB, "q_raw": 21 * KIB, "v_pool3": 25 * KIB, "v_bf1": 17 * KIB, "o_sb": 19 * KIB,
+    "v_pool0": 0, "ks_pool": 7 * KIB, "y_bf0": 0, "y_bf1": 2 * KIB, "v_pool1": 8 * KIB,
+    "v_pool2": 17 * KIB, "q_raw": 21 * KIB, "v_pool3": 25 * KIB, "v_bf1": 17 * KIB, "o_sb": 19 * KIB, "y_codes1": 20 * KIB,
     "kw_pool": 33 * KIB, "rs_sb0": 33 * KIB, "rs_sb1": 34 * KIB, "rs_sb2": 36 * KIB, "rs_sb3": 39 * KIB,
     "v_bf3": 34 * KIB,
 }
@@ -99,6 +99,9 @@ def tile_attend_mlpb_gelu_topk_kernel(tc, qT, k_words, k_scales, vT, nb, rs, us,
         make_identity(nc, ident[:])
 
         q_raw = load("q_raw", qT[0].rearrange("(p j) w -> p j w", j=PACK))
+        us_row = sbuf("us_row", [P, N], F32)
+        nc.sync.dma_start(us_row[P - 1:P, :], us.rearrange("b n o -> b (n o)"))
+        nc.gpsimd.memset(us_row[:P - 1, :], 0.0)
         kw_pool = load("kw_pool", k_words[0].rearrange("p n t -> p (n t)").bitcast(I32), I32)
 
         ks_g = sbuf("ks_g", [P, PACK, P], U8)
@@ -108,8 +111,6 @@ def tile_attend_mlpb_gelu_topk_kernel(tc, qT, k_words, k_scales, vT, nb, rs, us,
                 ks_plane[r:P:32].rearrange("p t m -> p (t m)").bitcast(I32),
                 ks_g[SCALE_BASE + r:SCALE_BASE + SCALE_ROWS:4].rearrange("p t m -> p (t m)").bitcast(I32))
         v_pool = [load("v_pool0", vT[blocks[0], :])]
-        us_sb = sbuf("us_sb", [P, 1, PACK, 1], F32)
-        nc.sync.dma_start(us_sb[:, 0, :, 0], us[0].rearrange("(p t) o -> p (t o)", t=PACK))
         v_pool.append(load("v_pool1", vT[blocks[1], :]))
 
         nb_list = sbuf("nb_list", [P, N], F32)
@@ -123,6 +124,11 @@ def tile_attend_mlpb_gelu_topk_kernel(tc, qT, k_words, k_scales, vT, nb, rs, us,
         nc.scalar.copy(packed(q_bf[1][:]), planes(q_raw[:, :, halves[1]]))
         bias = sbuf("bias", [P, PACK], F32)
         nc.scalar.copy(bias[:], nb_turn[:, :, P - 1])
+        us_turn = bank("us_turn", 6, [P, PACK, P])
+        for t in range(PACK):
+            nc.tensor.transpose(us_turn[:, t, :], us_row[:, t:N:PACK], ident[:])
+        us_sb = sbuf("us_sb", [P, 1, PACK, 1], F32)
+        nc.scalar.copy(us_sb[:, 0, :, 0], us_turn[:, :, P - 1])
         v_pool.extend(load("v_pool%d" % b, vT[blocks[b], :]) for b in range(2, 4))
 
         def quantize_half(name, words):
@@ -182,8 +188,7 @@ def tile_attend_mlpb_gelu_topk_kernel(tc, qT, k_words, k_scales, vT, nb, rs, us,
         y_bf1 = scale_half(1, g[1])
         y_q = [quantize_half("y_%s0", y_bf0)]
         v_q = [quantize_v(0, v_bf0)]
-        y_q.append(quantize_half("y_%s1", y_bf1))
-        y_q = [columns(half, blocks[c]) for half in y_q for c in range(2)]
+        y_q = [columns(y_q[0], blocks[c]) for c in range(2)]
 
         def finish(name, o, residual, rows, features):
             res = sbuf(name, list(o.shape), F32)
@@ -195,17 +200,19 @@ def tile_attend_mlpb_gelu_topk_kernel(tc, qT, k_words, k_scales, vT, nb, rs, us,
         o23 = bank("o23", 6, [P, 2, HALF])
         for c in range(2):
             product(o00[:, c, :], y_q[c], v_q[0])
-        for c in range(2):
-            product(o23[:, c, blocks[0]], y_q[2 + c], v_q[0])
         v_g2 = gather_v(2, VECTOR_COLUMNS)
+        y_q1 = quantize_half("y_%s1", y_bf1)
+        y_q.extend(columns(y_q1, blocks[c]) for c in range(2))
         v_bf1 = turn_v(1, v_g1)
+        v_bf2 = turn_v(2, v_g2)
         o_sb = sbuf("o_sb", [P, 2, P], F32)
         nc.scalar.copy(o_sb[:], o00[:])
         res0 = sbuf("res0", [P, 2, P], F32)
         nc.gpsimd.tensor_tensor(res0[:], o_sb[:], rs_sb[0][:], ALU.add)
         nc.sync.dma_start(out_rows[:, pairs[0], blocks[0]], res0[:])
-        v_bf2 = turn_v(2, v_g2)
         v_q.append(quantize_v(1, v_bf1))
+        for c in range(2):
+            product(o23[:, c, blocks[0]], y_q[2 + c], v_q[0])
         for c in range(2):
             product(o23[:, c, blocks[1]], y_q[2 + c], v_q[1])
         for c in range(2):
@@ -216,7 +223,7 @@ def tile_attend_mlpb_gelu_topk_kernel(tc, qT, k_words, k_scales, vT, nb, rs, us,
         o2 = bank("o2", 7, [P, 2, P])
         for c in range(2):
             product(o2[:, c, :], y_q[2 + c], v_q[2])
-        v_g3 = gather_v(3, 16)
+        v_g3 = gather_v(3, 12)
         v_bf3 = turn_v(3, v_g3)
         finish("res23", o23[:], rs_sb[1][:], pairs[1], halves[0])
         finish("res01", o01[:], rs_sb[2][:, :, :HALF], pairs[0], slice(P, 3 * P))

@@ -83,18 +83,19 @@ def tile_attend_mlpb_gelu_topk_kernel(tc, qT, k_words, k_scales, vT, nb, rs, us,
         nc.sync.dma_start(offsets[:], offs)
         ks_pool = sbuf("ks_pool", [P, T], U8)
         nc.sync.dma_start(ks_pool[SCALE_BASE:SCALE_BASE + SCALE_ROWS, :].bitcast(I32), k_scales[0].bitcast(I32))
-        nc.vector.memset(ks_pool[:SCALE_BASE, :].bitcast(I32), 0)
-        nc.vector.memset(ks_pool[SCALE_BASE + SCALE_ROWS:, :].bitcast(I32), 0)
-        nb_pool = sbuf("nb_pool", [P, T], F32)
-        nc.sync.dma_start(nb_pool[P - 1:P, :], nb[0:1, :])
-        nc.gpsimd.memset(nb_pool[:P - 1, T // 2:], 0.0)
-        nc.vector.memset(nb_pool[:P - 1, :T // 2], 0.0)
+        ks_words = ks_pool[:].bitcast(I32)
+        for rows in (slice(0, SCALE_BASE), slice(SCALE_BASE + SCALE_ROWS, P)):
+            for words in (slice(0, T // 4 - 1), slice(T // 4 - 1, T // 4)):
+                nc.vector.memset(ks_words[rows, words], 0)
         warm_in = sbuf("warm_in", [P, 1], F32)
-        nc.gpsimd.memset(warm_in[:], 0.0)
+        nc.vector.memset(warm_in[:], 0.0)
         warm = sbuf("warm", [P, 1], F32)
         nc.scalar.activation(warm[:], warm_in[:], ACT.Gelu_apprx_tanh)
         ks_plane = sbuf("ks_plane", [P, PACK, P], U8)
-        nc.vector.memset(ks_plane[:].rearrange("p t m -> p (t m)").bitcast(I32), 0)
+        nc.gpsimd.memset(ks_plane[:].rearrange("p t m -> p (t m)").bitcast(I32), 0)
+        nb_pool = sbuf("nb_pool", [P, T], F32)
+        nc.sync.dma_start(nb_pool[P - 1:P, :], nb[0:1, :])
+        nc.gpsimd.memset(nb_pool[:P - 1, :], 0.0)
         ident = sbuf("ident", [P, P], F32)
         make_identity(nc, ident[:])
 

@@ -227,6 +227,9 @@ def tile_attend_mlpb_gelu_topk_kernel(tc, qT, k_words, k_scales, vT, nb, rs, us,
         v_g3 = gather_v(3, 12)
         v_bf3 = turn_v(3, v_g3)
         finish("res23", o23[:], rs_sb[1][:], pairs[1], halves[0])
+        idle = bank("idle", 6, [P, 3 * P])
+        product(idle[:, :HALF], y_q[0], y_q1)
+        product(idle[:, HALF:], y_q[0], v_q[0])
         finish("res01", o01[:], rs_sb[2][:, :, :HALF], pairs[0], slice(P, 3 * P))
         v_q.append(quantize_v(3, v_bf3))
         finish("res2", o2[:], rs_sb[3][:, :, blocks[0]], pairs[1], blocks[2])

@@ -29,8 +29,8 @@ VECTOR_COLUMNS = 18
 
 PLAN = {
     "v_pool0": 0, "ks_pool": 7 * KIB, "y_bf0": 0, "y_bf1": 2 * KIB, "v_pool1": 8 * KIB,
-    "v_pool2": 17 * KIB, "q_raw": 21 * KIB, "v_pool3": 25 * KIB, "v_bf1": 17 * KIB, "o_sb": 19 * KIB, "y_codes1": 20 * KIB,
-    "kw_pool": 33 * KIB, "rs_sb0": 33 * KIB, "rs_sb1": 34 * KIB, "rs_sb2": 36 * KIB, "rs_sb3": 39 * KIB,
+    "v_pool2": 17 * KIB, "kw_pool": 21 * KIB, "v_pool3": 25 * KIB, "v_bf1": 17 * KIB, "o_sb": 19 * KIB, "y_codes1": 20 * KIB,
+    "q_raw": 33 * KIB, "rs_sb0": 33 * KIB, "rs_sb1": 34 * KIB, "rs_sb2": 36 * KIB, "rs_sb3": 39 * KIB,
     "v_bf3": 34 * KIB,
 }
 
@@ -99,11 +99,11 @@ def tile_attend_mlpb_gelu_topk_kernel(tc, qT, k_words, k_scales, vT, nb, rs, us,
         ident = sbuf("ident", [P, P], F32)
         make_identity(nc, ident[:])
 
-        q_raw = load("q_raw", qT[0].rearrange("(p j) w -> p j w", j=PACK))
+        kw_pool = load("kw_pool", k_words[0].rearrange("p n t -> p (n t)").bitcast(I32), I32)
         us_row = sbuf("us_row", [P, N], F32)
         nc.sync.dma_start(us_row[P - 1:P, :], us.rearrange("b n o -> b (n o)"))
         nc.gpsimd.memset(us_row[:P - 1, :], 0.0)
-        kw_pool = load("kw_pool", k_words[0].rearrange("p n t -> p (n t)").bitcast(I32), I32)
+        q_raw = load("q_raw", qT[0].rearrange("(p j) w -> p j w", j=PACK))
 
         ks_g = sbuf("ks_g", [P, PACK, P], U8)
         nc.vector.tensor_copy(ks_g[:].rearrange("p t m -> p m t"), ks_pool[:].indirect(offsets[:]))
@@ -120,24 +120,26 @@ def tile_attend_mlpb_gelu_topk_kernel(tc, qT, k_words, k_scales, vT, nb, rs, us,
         for t in range(PACK):
             nc.tensor.transpose(nb_turn[:, t, :], nb_list[:, t:N:PACK], ident[:])
 
+        kw_g = sbuf("kw_g", [P, PACK, P], U32)
+        nc.vector.tensor_copy(kw_g[:].rearrange("p t m -> p m t"), kw_pool[:].bitcast(U32).indirect(offsets[:]))
+        v_pool.extend(load("v_pool%d" % b, vT[blocks[b], :]) for b in range(2, 4))
+        us_dealt = sbuf("us_dealt", [P, PACK, P], F32)
+        nc.vector.tensor_copy(us_dealt[:].rearrange("p t m -> p m t"), us_row[:].rearrange("p (m t) -> p m t", t=PACK))
+        us_turn = bank("us_turn", 6, [P, PACK, P])
+        for t in range(PACK):
+            nc.tensor.transpose(us_turn[:, t, :], us_dealt[:, t, :], ident[:])
         q_bf = [sbuf("q_bf%d" % h, [P, HALF, PACK], BF16) for h in range(2)]
         nc.vector.tensor_copy(packed(q_bf[0][:]), planes(q_raw[:, :, halves[0]]))
         nc.scalar.copy(packed(q_bf[1][:]), planes(q_raw[:, :, halves[1]]))
         bias = sbuf("bias", [P, PACK], F32)
         nc.scalar.copy(bias[:], nb_turn[:, :, P - 1])
-        us_turn = bank("us_turn", 6, [P, PACK, P])
-        for t in range(PACK):
-            nc.tensor.transpose(us_turn[:, t, :], us_row[:, t:N:PACK], ident[:])
         us_sb = sbuf("us_sb", [P, 1, PACK, 1], F32)
         nc.scalar.copy(us_sb[:, 0, :, 0], us_turn[:, :, P - 1])
-        v_pool.extend(load("v_pool%d" % b, vT[blocks[b], :]) for b in range(2, 4))
 
         def quantize_half(name, words):
             return quantize(name, HALF, words[:].rearrange("p w j -> p (w j)"))
 
         q_q = [quantize_half("q_%s" + str(h), q_bf[h]) for h in range(2)]
-        kw_g = sbuf("kw_g", [P, PACK, P], U32)
-        nc.vector.tensor_copy(kw_g[:].rearrange("p t m -> p m t"), kw_pool[:].bitcast(U32).indirect(offsets[:]))
 
         rs_rows = rs[0].rearrange("(c p) e -> p c e", p=P)
         out_rows = out[0].rearrange("(c p) e -> p c e", p=P)

from contextlib import ExitStack

import concourse.mybir as mybir
from concourse.masks import make_identity

N, T, D, NQ, DV = 512, 2048, 512, 512, 512
FLOPS = 2 * N * NQ * (D + DV)
BYTES = 4 * (D * NQ + DV * T + T + 2 * NQ * DV + N) + D * T + 16 * T + 128 * 32 * 2

F32 = mybir.dt.float32
BF16 = mybir.dt.bfloat16
I32 = mybir.dt.int32
U32 = mybir.dt.uint32
U16 = mybir.dt.uint16
U8 = mybir.dt.uint8
FP8X4 = mybir.dt.float8_e4m3fn_x4
ACT = mybir.ActivationFunctionType
ALU = mybir.AluOpType

P = 128
PACK = 4
RUN = 4
HALF = NQ // 2
SCALE_ROWS = 16
SCALE_BASE = 48
BANK = 2048
KIB = 1024
VECTOR_COLUMNS = 18

PLAN = {
    "v_pool0": 0, "ks_pool": 7 * KIB, "y_bf0": 0, "y_bf1": 2 * KIB, "v_pool1": 8 * KIB,
    "v_pool2": 17 * KIB, "kw_pool": 21 * KIB, "v_pool3": 25 * KIB, "v_bf1": 17 * KIB, "o_sb": 19 * KIB, "y_codes1": 20 * KIB,
    "q_raw": 33 * KIB, "rs_sb0": 33 * KIB, "rs_sb1": 34 * KIB, "rs_sb2": 36 * KIB, "rs_sb3": 39 * KIB,
    "v_bf3": 34 * KIB,
}


def packed(tile):
    return tile.rearrange("p (c i) t -> p c t i", i=RUN)


def planes(tile):
    return tile.rearrange("p t (c i) -> p c t i", i=RUN)


def tile_attend_mlpb_gelu_topk_kernel(tc, qT, k_words, k_scales, vT, nb, rs, us, offs, out):
    nc = tc.nc
    with ExitStack() as ctx:
        keep = ctx.enter_context(tc.tile_pool(name="keep", bufs=1))
        shared = ctx.enter_context(tc.tile_pool(name="shared", bufs=1))
        psum = ctx.enter_context(tc.psum_pool(name="psum", bufs=1))

        def sbuf(name, shape, dtype):
            if name in PLAN:
                return shared.tile(shape, dtype, name=name, offset=PLAN[name], align_bytes=64)
            return keep.tile(shape, dtype, name=name, align_bytes=64)

        def bank(name, number, shape):
            return psum.tile(shape, F32, name=name, offset=number * BANK)

        def quantize(name, width, values):
            codes = sbuf(name % "codes", [P, width], U32)
            scales = sbuf(name % "scales", [P, width], U8)
            nc.vector.quantize_mx(out=codes[:].bitcast(FP8X4), scales=scales[:], in_=values)
            return codes[:], scales[:]

        def columns(operand, cols):
            return operand[0][:, cols], operand[1][:, cols]

        def product(o, stationary, moving):
            nc.tensor.matmul_mx(out=o, lhsT=stationary[0].bitcast(FP8X4), lhsT_scale=stationary[1],
                                rhs=moving[0].bitcast(FP8X4), rhs_scale=moving[1], start=True, stop=True)

        def load(name, source, dtype=F32):
            tile = sbuf(name, list(source.shape), dtype)
            nc.sync.dma_start(tile[:], source)
            return tile

        halves = [slice(h * HALF, (h + 1) * HALF) for h in range(2)]
        blocks = [slice(b * P, (b + 1) * P) for b in range(4)]

        offsets = keep.tile([P, N // 16], U16, name="offsets")
        nc.sync.dma_start(offsets[:], offs)
        ks_pool = sbuf("ks_pool", [P, T], U8)
        nc.sync.dma_start(ks_pool[SCALE_BASE:SCALE_BASE + SCALE_ROWS, :].bitcast(I32), k_scales[0].bitcast(I32))
        ks_words = ks_pool[:].bitcast(I32)
        for rows in (slice(0, SCALE_BASE), slice(SCALE_BASE + SCALE_ROWS, P)):
            for words in (slice(0, T // 4 - 1), slice(T // 4 - 1, T // 4)):
                nc.vector.memset(ks_words[rows, words], 0)
        warm_in = sbuf("warm_in", [P, 1], F32)
        nc.vector.memset(warm_in[:], 0.0)
        warm = sbuf("warm", [P, 1], F32)
        nc.scalar.activation(warm[:], warm_in[:], ACT.Gelu_apprx_tanh)
        ks_plane = sbuf("ks_plane", [P, PACK, P], U8)
        nc.gpsimd.memset(ks_plane[:].rearrange("p t m -> p (t m)").bitcast(I32), 0)
        nb_pool = sbuf("nb_pool", [P, T], F32)
        nc.sync.dma_start(nb_pool[P - 1:P, :], nb[0:1, :])
        nc.gpsimd.memset(nb_pool[:P - 1, :], 0.0)
        ident = sbuf("ident", [P, P], F32)
        make_identity(nc, ident[:])

        kw_pool = load("kw_pool", k_words[0].rearrange("p n t -> p (n t)").bitcast(I32), I32)
        us_row = sbuf("us_row", [P, N], F32)
        nc.sync.dma_start(us_row[P - 1:P, :], us.rearrange("b n o -> b (n o)"))
        nc.gpsimd.memset(us_row[:P - 1, :], 0.0)
        q_raw = load("q_raw", qT[0].rearrange("(p j) w -> p j w", j=PACK))

        ks_g = sbuf("ks_g", [P, PACK, P], U8)
        nc.vector.tensor_copy(ks_g[:].rearrange("p t m -> p m t"), ks_pool[:].indirect(offsets[:]))
        for r in range(4):
            nc.sync.dma_start(
                ks_plane[r:P:32].rearrange("p t m -> p (t m)").bitcast(I32),
                ks_g[SCALE_BASE + r:SCALE_BASE + SCALE_ROWS:4].rearrange("p t m -> p (t m)").bitcast(I32))
        v_pool = [load("v_pool0", vT[blocks[0], :])]
        v_pool.append(load("v_pool1", vT[blocks[1], :]))

        nb_list = sbuf("nb_list", [P, N], F32)
        nc.scalar.activation(nb_list[:], nb_pool[:].indirect(offsets[:]), ACT.Copy)
        nb_turn = bank("nb_turn", 7, [P, PACK, P])
        for t in range(PACK):
            nc.tensor.transpose(nb_turn[:, t, :], nb_list[:, t:N:PACK], ident[:])

        kw_g = sbuf("kw_g", [P, PACK, P], U32)
        nc.vector.tensor_copy(kw_g[:].rearrange("p t m -> p m t"), kw_pool[:].bitcast(U32).indirect(offsets[:]))
        v_pool.extend(load("v_pool%d" % b, vT[blocks[b], :]) for b in range(2, 4))
        us_dealt = sbuf("us_dealt", [P, PACK, P], F32)
        nc.vector.tensor_copy(us_dealt[:].rearrange("p t m -> p m t"), us_row[:].rearrange("p (m t) -> p m t", t=PACK))
        us_turn = bank("us_turn", 6, [P, PACK, P])
        for t in range(PACK):
            nc.tensor.transpose(us_turn[:, t, :], us_dealt[:, t, :], ident[:])
        q_bf = [sbuf("q_bf%d" % h, [P, HALF, PACK], BF16) for h in range(2)]
        nc.vector.tensor_copy(packed(q_bf[0][:]), planes(q_raw[:, :, halves[0]]))
        nc.scalar.copy(packed(q_bf[1][:]), planes(q_raw[:, :, halves[1]]))
        bias = sbuf("bias", [P, PACK], F32)
        nc.scalar.copy(bias[:], nb_turn[:, :, P - 1])
        us_sb = sbuf("us_sb", [P, 1, PACK, 1], F32)
        nc.scalar.copy(us_sb[:, 0, :, 0], us_turn[:, :, P - 1])

        def quantize_half(name, words):
            return quantize(name, HALF, words[:].rearrange("p w j -> p (w j)"))

        q_q = [quantize_half("q_%s" + str(h), q_bf[h]) for h in range(2)]

        rs_rows = rs[0].rearrange("(c p) e -> p c e", p=P)
        out_rows = out[0].rearrange("(c p) e -> p c e", p=P)
        pairs = [slice(2 * h, 2 * h + 2) for h in range(2)]
        pieces = [(pairs[0], blocks[0]), (pairs[1], halves[0]), (pairs[0], slice(P, DV)), (pairs[1], halves[1])]
        rs_sb = [load("rs_sb%d" % i, rs_rows[:, rows, features]) for i, (rows, features) in enumerate(pieces)]

        def first_product(h):
            a = [bank("a%d_%d" % (h, t), PACK * h + t, [P, HALF]) for t in range(PACK)]
            for t in range(PACK):
                product(a[t][:], (kw_g[:, t, :], ks_plane[:, t, :]), q_q[h])
            g = sbuf("g%d" % h, [P, PACK, HALF], F32)
            for t in range(PACK):
                nc.scalar.activation(g[:, t, :], a[t][:], ACT.Gelu_apprx_tanh, bias=bias[:, t:t + 1])
            return g

        def scale_half(h, g):
            y_bf = sbuf("y_bf%d" % h, [P, HALF, PACK], BF16)
            nc.vector.tensor_tensor(packed(y_bf[:]), planes(g[:]),
                                    us_sb[:].to_broadcast([P, HALF // RUN, PACK, RUN]), ALU.mult)
            return y_bf

        def gather_v(b, vector_columns):
            v_g = sbuf("v_g%d" % b, [P, N], BF16)
            cut = 16 * vector_columns
            if vector_columns:
                nc.vector.tensor_copy(v_g[:, :cut], v_pool[b][:].indirect(offsets[:, :vector_columns]))
            if cut < N:
                nc.scalar.activation(v_g[:, cut:], v_pool[b][:].indirect(offsets[:, vector_columns:]), ACT.Copy)
            return v_g

        def turn_v(b, v_g):
            words = v_g[:].bitcast(F32)
            turn = bank("v_turn%d" % b, b, [P, 2, P])
            for u in range(2):
                nc.tensor.transpose(turn[:, u, :], words[:, u:2 * P:2], ident[:])
            v_bf = sbuf("v_bf%d" % b, [P, P * PACK], BF16)
            nc.scalar.copy(v_bf[:].bitcast(F32).rearrange("p (e u) -> p e u", u=2), turn[:].rearrange("p u e -> p e u"))
            return v_bf

        def quantize_v(b, v_bf):
            return quantize("v_%s" + str(b), P, v_bf[:])

        g = [first_product(h) for h in range(2)]
        v_g0 = gather_v(0, N // 16)
        y_bf0 = scale_half(0, g[0])
        v_bf0 = turn_v(0, v_g0)
        v_g1 = gather_v(1, 0)
        y_bf1 = scale_half(1, g[1])
        y_q = [quantize_half("y_%s0", y_bf0)]
        v_q = [quantize_v(0, v_bf0)]
        y_q = [columns(y_q[0], blocks[c]) for c in range(2)]

        def finish(name, o, residual, rows, features):
            res = sbuf(name, list(o.shape), F32)
            nc.vector.tensor_tensor(res[:], o, residual, ALU.add)
            nc.sync.dma_start(out_rows[:, rows, features], res[:])

        o00 = bank("o00", 4, [P, 2, P])
        o01 = bank("o01", 5, [P, 2, HALF])
        o23 = bank("o23", 6, [P, 2, HALF])
        for c in range(2):
            product(o00[:, c, :], y_q[c], v_q[0])
        v_g2 = gather_v(2, VECTOR_COLUMNS)
        y_q1 = quantize_half("y_%s1", y_bf1)
        y_q.extend(columns(y_q1, blocks[c]) for c in range(2))
        v_bf1 = turn_v(1, v_g1)
        v_bf2 = turn_v(2, v_g2)
        o_sb = sbuf("o_sb", [P, 2, P], F32)
        nc.scalar.copy(o_sb[:], o00[:])
        res0 = sbuf("res0", [P, 2, P], F32)
        nc.gpsimd.tensor_tensor(res0[:], o_sb[:], rs_sb[0][:], ALU.add)
        nc.sync.dma_start(out_rows[:, pairs[0], blocks[0]], res0[:])
        v_q.append(quantize_v(1, v_bf1))
        for c in range(2):
            product(o23[:, c, blocks[0]], y_q[2 + c], v_q[0])
        for c in range(2):
            product(o23[:, c, blocks[1]], y_q[2 + c], v_q[1])
        for c in range(2):
            product(o01[:, c, blocks[0]], y_q[c], v_q[1])
        v_q.append(quantize_v(2, v_bf2))
        for c in range(2):
            product(o01[:, c, blocks[1]], y_q[c], v_q[2])
        o2 = bank("o2", 7, [P, 2, P])
        for c in range(2):
            product(o2[:, c, :], y_q[2 + c], v_q[2])
        v_g3 = gather_v(3, 12)
        v_bf3 = turn_v(3, v_g3)
        finish("res23", o23[:], rs_sb[1][:], pairs[1], halves[0])
        idle = bank("idle", 6, [P, 3 * P])
        product(idle[:, :HALF], y_q[0], y_q1)
        product(idle[:, HALF:], y_q[0], v_q[0])
        finish("res01", o01[:], rs_sb[2][:, :, :HALF], pairs[0], slice(P, 3 * P))
        v_q.append(quantize_v(3, v_bf3))
        finish("res2", o2[:], rs_sb[3][:, :, blocks[0]], pairs[1], blocks[2])
        o3 = [bank("o3_%d" % c, number, [P, P]) for c, number in enumerate((0, 1, 2, 3))]
        for c in range(4):
            product(o3[c][:], y_q[c], v_q[3])
        last = [rs_sb[2][:, :, blocks[2]], rs_sb[3][:, :, blocks[1]]]
        for h in range(2):
            res = sbuf("res3_%d" % h, [P, 2, P], F32)
            for i in range(2):
                nc.vector.tensor_tensor(res[:, i, :], o3[2 * h + i][:], last[h][:, i, :], ALU.add)
            nc.sync.dma_start(out_rows[:, pairs[h], blocks[3]], res[:])
